import numpy as np
import ml_dtypes


def mxq(x, axis, fmt="e4m3"):
    dtype, down = {"e4m3": (ml_dtypes.float8_e4m3fn, 7), "e5m2": (ml_dtypes.float8_e5m2, 14)}[fmt]
    v = np.moveaxis(np.asarray(x, np.float32).astype(ml_dtypes.bfloat16).astype(np.float64), axis, -1)
    blocks = v.reshape(v.shape[:-1] + (-1, 32))
    amax = np.abs(blocks).max(-1, keepdims=True)
    byte = np.maximum(np.where(amax > 0, np.frexp(amax)[1] - 1 + 127, 0) - down, 1)
    scale = np.exp2(byte - 127.0)
    codes = (blocks / scale).astype(np.float32).astype(dtype).astype(np.float64)
    return np.moveaxis((codes * scale).reshape(v.shape), -1, axis)


WIDE = False


def mx_kscale(k):
    if not WIDE:
        return np.ones(k)
    levels = np.array([10, -10, 5, -5, 0])
    if k % 512:
        return np.exp2(np.random.permutation(np.resize(levels, k // 32))).repeat(32)
    a = np.empty((k // 512, 16))
    for p in range(k // 512):
        a[p, :8] = np.random.permutation(np.resize(levels, 8))
        for g in range(8):
            far = levels[np.abs(levels - a[p, g]) >= 10]
            a[p, g + 8] = far[np.random.randint(len(far))]
    return np.exp2(a.ravel()).repeat(32)


def f64(x):
    return np.asarray(x).astype(np.float64)


def striped(idx):
    return np.tile(idx.reshape(-1, 16).T, (8, 1)).astype(np.uint16)


def unstriped(offs):
    return offs[:16].T.reshape(-1).astype(np.int64)


E2M1 = np.array([0.0, 0.5, 1.0, 1.5, 2.0, 3.0, 4.0, 6.0, -0.0, -0.5, -1.0, -1.5, -2.0, -3.0, -4.0, -6.0])


def pack_weight(w, fmt):
    k, n = w.shape
    w = f64(np.asarray(w, np.float32).astype(ml_dtypes.bfloat16)).reshape(k // 32, 32, n)
    amax = np.abs(w).max(1)
    if fmt == "e4m3":
        byte = np.frexp(amax)[1] - 1 + 127 - 7
    else:
        mant, ex = np.frexp(amax / 6.0)
        byte = np.where(mant > 0.5, ex, ex - 1) + 127
    byte = np.clip(np.where(amax > 0, byte, 1), 1, 254)
    scaled = (w * np.exp2(127.0 - byte)[:, None, :]).reshape(k, n).astype(np.float32)
    by_word = np.ascontiguousarray(scaled.reshape(k // 512, 128, 4, n).transpose(0, 1, 3, 2))
    if fmt == "e4m3":
        words = by_word.astype(ml_dtypes.float8_e4m3fn).view(np.uint8)
    else:
        c = by_word.astype(ml_dtypes.float4_e2m1fn).view(np.uint8) & 0xF
        words = (c[..., 0::2] | (c[..., 1::2] << 4)).reshape(k // 512, 128, 2 * n)
    return np.ascontiguousarray(words), np.ascontiguousarray(byte.astype(np.uint8).reshape(k // 512, 16, n))


def unpack_weight(words, scales, fmt):
    g, _, n = scales.shape
    words = np.ascontiguousarray(words).reshape(g, 128, n, -1)
    if fmt == "e4m3":
        vals = words.view(ml_dtypes.float8_e4m3fn).astype(np.float64)
    else:
        nib = np.empty((g, 128, n, 4), np.uint8)
        nib[..., 0::2] = words & 0xF
        nib[..., 1::2] = words >> 4
        vals = E2M1[nib]
    vals = vals * np.repeat(np.exp2(scales.astype(np.float64) - 127.0), 8, axis=1)[..., None]
    return vals.transpose(0, 1, 3, 2).reshape(g * 512, n)


def gelu(v):
    return 0.5 * v * (1.0 + np.tanh(np.sqrt(2.0 / np.pi) * (v + 0.044715 * v**3)))


K, H, N, T, S, P = 512, 1024, 384, 2048, 1024, 512

def setup_inputs():
    n = np.random.standard_normal
    s = mx_kscale(K)[:, None]
    u = mx_kscale(H)[:, None]
    tab_words, tab_scales = pack_weight(n((K, T)) * s, "e4m3")
    w4_words, w4_scales = pack_weight(n((K, H)) / np.sqrt(K) / s, "e2m1")
    return {
        "tab_words": tab_words, "tab_scales": tab_scales,
        "offs": striped(np.random.permutation(T)[:S]),
        "pos1": striped(np.random.permutation(S)[:P]),
        "pos2": striped(np.random.permutation(S)[:P]),
        "w1": (n((K, H)) / np.sqrt(K) / s).astype(np.float32),
        "w4_words": w4_words, "w4_scales": w4_scales,
        "gz": (np.exp(0.3 * n(H)) * u[:, 0]).astype(np.float32),
        "w2": (n((H, N)) / np.sqrt(H) / u).astype(np.float32),
        "b2": (0.5 * n(N)).astype(np.float32),
    }

def reference(tab_words, tab_scales, offs, pos1, pos2, w1, w4_words, w4_scales, gz, w2, b2):
    v = unpack_weight(tab_words, tab_scales, "e4m3")[:, unstriped(offs)]
    w1q = mxq(f64(w1), 0, "e4m3")
    w4q = unpack_weight(w4_words, w4_scales, "e2m1")
    h = np.maximum(w1q.T @ v, w4q.T @ v)
    a = h[:, unstriped(pos1)]
    b = h[:, unstriped(pos2)]
    z = a * b * f64(gz)[:, None]
    y = mxq(f64(w2), 0, "e4m3").T @ mxq(z, 0, "e4m3")
    return np.tanh(y + f64(b2)[:, None])

@@ -1,0 +1,297 @@
+from contextlib import ExitStack
+
+import concourse.mybir as mybir
+
+K, H, N, T, S, PAIRS = 512, 1024, 384, 2048, 1024, 512
+FLOPS = 2 * (2 * K * H * S) + 2 * H * N * PAIRS
+
+F32 = mybir.dt.float32
+BF16 = mybir.dt.bfloat16
+I32 = mybir.dt.int32
+U32 = mybir.dt.uint32
+U16 = mybir.dt.uint16
+U8 = mybir.dt.uint8
+FP8X4 = mybir.dt.float8_e4m3fn_x4
+FP4X4 = mybir.dt.float4_e2m1fn_x4
+MULT = mybir.AluOpType.mult
+MAX = mybir.AluOpType.max
+TANH = mybir.ActivationFunctionType.Tanh
+
+P = 128
+PACK = 4
+PASS = P * PACK
+BANK = 512
+GROUPS = H // PASS
+TILES = H // P
+N_TILES = N // P
+W1_CHUNK = 256
+CHUNKS = [(0, 256), (256, 128), (384, 128)]
+
+
+def tile_list_code_pair_match_kernel(
+    tc, tab_words, tab_scales, offs, pos1, pos2, w1, w4_words, w4_scales, gz, w2, b2, out
+):
+    nc = tc.nc
+    with ExitStack() as ctx:
+        keep = ctx.enter_context(tc.tile_pool(name="keep", bufs=1))
+        ring = ctx.enter_context(tc.tile_pool(name="ring", bufs=3))
+        psum_a = ctx.enter_context(tc.psum_pool(name="psum_a", bufs=2))
+        psum_b = ctx.enter_context(tc.psum_pool(name="psum_b", bufs=2))
+        psum_y = ctx.enter_context(tc.psum_pool(name="psum_y", bufs=4))
+
+        offs_sb = keep.tile([P, S // 16], U16, name="offs_sb")
+        pos1_sb = keep.tile([P, PAIRS // 16], U16, name="pos1_sb")
+        pos2_sb = keep.tile([P, PAIRS // 16], U16, name="pos2_sb")
+        tab_w = keep.tile([P, T], I32, name="tab_w", align_bytes=64)
+        tab_s = keep.tile([P, T // 4], I32, name="tab_s", align_bytes=64)
+        w4_raw = keep.tile([P, H // 2], I32, name="w4_raw", align_bytes=64)
+        w4s_raw = keep.tile([P, H // 4], I32, name="w4s_raw", align_bytes=64)
+        w1_raw = [
+            keep.tile([P, PACK, W1_CHUNK], F32, name="w1_raw%d" % i, align_bytes=64)
+            for i in range(H // W1_CHUNK)
+        ]
+        w2_raw = [keep.tile([P, PACK, N], F32, name="w2_raw%d" % g, align_bytes=64) for g in range(GROUPS)]
+        gz_sb = keep.tile([P, GROUPS, PACK], F32, name="gz_sb")
+        b2_sb = keep.tile([P, N_TILES], F32, name="b2_sb")
+        warm_in = keep.tile([P, 1], F32, name="warm_in")
+        warm_out = keep.tile([P, 1], F32, name="warm_out")
+
+        nc.vector.memset(tab_s[:], 0)
+        nc.gpsimd.memset(warm_in[:], 0.0)
+        nc.gpsimd.memset(w4s_raw[:], 0)
+        nc.scalar.activation(warm_out[:], warm_in[:], TANH)
+        nc.gpsimd.dma_start(gz_sb[:], gz.rearrange("(g p t) -> p g t", g=GROUPS, t=PACK))
+
+        def load_scale_rows(plane, rows):
+            by_r = rows.rearrange("(q r) c -> r q c", r=4)
+            for r in range(4):
+                nc.sync.dma_start(plane[r:P:32, :], by_r[r].bitcast(I32))
+
+        w1_rows = w1.rearrange("(p j) c -> p j c", j=PACK)
+
+        def load_w1(i):
+            nc.sync.dma_start(w1_raw[i][:], w1_rows[:, :, i * W1_CHUNK : (i + 1) * W1_CHUNK])
+
+        nc.sync.dma_start(offs_sb[:], offs)
+        load_scale_rows(tab_s, tab_scales[0])
+        nc.sync.dma_start(tab_w[:], tab_words[0].rearrange("p t i -> p (t i)").bitcast(I32))
+        nc.sync.dma_start(w4_raw[:], w4_words[0].bitcast(I32))
+        load_w1(0)
+        load_scale_rows(w4s_raw, w4_scales[0])
+        load_w1(1)
+        nc.sync.dma_start(pos1_sb[:], pos1)
+        nc.sync.dma_start(pos2_sb[:], pos2)
+        load_w1(2)
+        load_w1(3)
+        for g in range(GROUPS):
+            nc.sync.dma_start(
+                w2_raw[g][:], w2[g * PASS : (g + 1) * PASS, :].rearrange("(p j) n -> p j n", j=PACK)
+            )
+        with nc.allow_non_contiguous_dma(reason="one bias value to a partition"):
+            nc.sync.dma_start(b2_sb[:], b2.rearrange("(c p) -> p c", p=P))
+
+        v_w = keep.tile([P, S], U32, name="v_w", align_bytes=64)
+        v_s = keep.tile([P, S], U8, name="v_s", align_bytes=64)
+        nc.vector.tensor_copy(v_s[:], tab_s[:].bitcast(U8).indirect(offs_sb[:]))
+
+        def gather_words(half):
+            cols = slice(half * BANK, (half + 1) * BANK)
+            lst = offs_sb[:, half * BANK // 16 : (half + 1) * BANK // 16]
+            nc.vector.tensor_copy(v_w[:, cols], tab_w[:].bitcast(U32).indirect(lst))
+
+        w4_w = keep.tile([P, 2 * H], U8, name="w4_w", align_bytes=64)
+        w4_s = keep.tile([P, H], U8, name="w4_s", align_bytes=64)
+
+        def permute_w4():
+            nc.vector.tensor_copy(
+                w4_w[:].bitcast(U16).rearrange("p (g t m) -> p g t m", g=GROUPS, t=PACK),
+                w4_raw[:].bitcast(U16).rearrange("p (g m t) -> p g t m", g=GROUPS, t=PACK),
+            )
+            nc.vector.tensor_copy(
+                w4_s[:].rearrange("p (g t m) -> p g t m", g=GROUPS, t=PACK),
+                w4s_raw[:].bitcast(U8).rearrange("p (g m t) -> p g t m", g=GROUPS, t=PACK),
+            )
+
+        w1_bf = [keep.tile([P, PACK, P, PACK], BF16, name="w1_bf%d" % g, align_bytes=64) for g in range(GROUPS)]
+        w1_w = keep.tile([P, H], U32, name="w1_w", align_bytes=64)
+        w1_s = keep.tile([P, H], U8, name="w1_s", align_bytes=64)
+
+        def cast_w1(i):
+            g, part = divmod(i, PASS // W1_CHUNK)
+            m_count = W1_CHUNK // PACK
+            ms = slice(part * m_count, (part + 1) * m_count)
+            nc.scalar.copy(
+                w1_bf[g][:, :, ms, :].rearrange("p t m j -> p m j t"),
+                w1_raw[i][:].rearrange("p j (m t) -> p m j t", t=PACK),
+            )
+
+        def quantize(codes, scales, src, first, count):
+            nc.vector.quantize_mx(
+                out=codes[:, first : first + count].bitcast(FP8X4),
+                scales=scales[:, first : first + count],
+                in_=src,
+            )
+
+        def quantize_w1(g, t0, t1):
+            src = w1_bf[g][:, t0:t1, :, :].rearrange("p t m j -> p (t m j)")
+            quantize(w1_w, w1_s, src, g * PASS + t0 * P, (t1 - t0) * P)
+
+        w2_bf = keep.tile([P, GROUPS * N, PACK], BF16, name="w2_bf", align_bytes=64)
+        w2_w = keep.tile([P, GROUPS * N], U32, name="w2_w", align_bytes=64)
+        w2_s = keep.tile([P, GROUPS * N], U8, name="w2_s", align_bytes=64)
+
+        def interleave(copy, dst, src):
+            copy(
+                dst.rearrange("p (c i) t -> p c t i", i=4),
+                src.rearrange("p t (c i) -> p c t i", i=4),
+            )
+
+        def quantize_w2(first, count):
+            src = w2_bf[:, first : first + count, :].rearrange("p n j -> p (n j)")
+            quantize(w2_w, w2_s, src, first, count)
+
+        h = [keep.tile([P, S], F32, name="h%d" % c, align_bytes=64) for c in range(TILES)]
+
+        def encode(c, half):
+            cols = slice(half * BANK, (half + 1) * BANK)
+            acc_b = psum_b.tile([P, BANK], F32, name="acc_b")
+            nc.tensor.matmul_mx(
+                out=acc_b[:],
+                lhsT=w4_w[:, 2 * c * P : 2 * (c + 1) * P].bitcast(FP4X4),
+                lhsT_scale=w4_s[:, c * P : (c + 1) * P],
+                rhs=v_w[:, cols].bitcast(FP8X4),
+                rhs_scale=v_s[:, cols],
+                start=True,
+                stop=True,
+            )
+            acc_a = psum_a.tile([P, BANK], F32, name="acc_a")
+            nc.tensor.matmul_mx(
+                out=acc_a[:],
+                lhsT=w1_w[:, c * P : (c + 1) * P].bitcast(FP8X4),
+                lhsT_scale=w1_s[:, c * P : (c + 1) * P],
+                rhs=v_w[:, cols].bitcast(FP8X4),
+                rhs_scale=v_s[:, cols],
+                start=True,
+                stop=True,
+            )
+            nc.scalar.copy(h[c][:, cols], acc_b[:])
+            nc.vector.tensor_tensor(h[c][:, cols], acc_a[:], h[c][:, cols], MAX)
+
+        z_f = [keep.tile([P, PACK, PAIRS], F32, name="z_f%d" % g, align_bytes=64) for g in range(GROUPS)]
+        z_bf = [keep.tile([P, PAIRS, PACK], BF16, name="z_bf%d" % g, align_bytes=64) for g in range(GROUPS)]
+        z_w = [keep.tile([P, PAIRS], U32, name="z_w%d" % g, align_bytes=64) for g in range(GROUPS)]
+        z_s = [keep.tile([P, PAIRS], U8, name="z_s%d" % g, align_bytes=64) for g in range(GROUPS)]
+        query = {}
+
+        gain = [keep.tile([P, PAIRS], F32, name="gain%d" % c, align_bytes=64) for c in range(TILES)]
+
+        def spread_gain(c, count):
+            g, t = divmod(c, PACK)
+            nc.scalar.copy(gain[c][:, 0:count], gz_sb[:, g, t : t + 1].to_broadcast([P, count]))
+
+        def pick_query(c, first, count):
+            picked = ring.tile([P, count], F32, name="picked", align_bytes=64)
+            lst = pos1_sb[:, first // 16 : (first + count) // 16]
+            nc.vector.tensor_tensor(picked[:], h[c][:].indirect(lst), gain[c][:, 0:count], MULT)
+            query[(c, first)] = picked
+
+        def pick_candidate(c, first, count):
+            g, t = divmod(c, PACK)
+            lst = pos2_sb[:, first // 16 : (first + count) // 16]
+            nc.vector.tensor_tensor(
+                z_f[g][:, t, first : first + count], h[c][:].indirect(lst), query[(c, first)][:], MULT
+            )
+
+        def round_z(copy, g, first, count):
+            interleave(copy, z_bf[g][:, first : first + count, :], z_f[g][:, :, first : first + count])
+
+        def quantize_z(g, first, count):
+            src = z_bf[g][:, first : first + count, :].rearrange("p n j -> p (n j)")
+            quantize(z_w[g], z_s[g], src, first, count)
+
+        out_rows = out.rearrange("(c p) j -> p c j", p=P)
+
+        def score(first, count, accs):
+            cols = slice(first, first + count)
+            result = ring.tile([P, N_TILES, count], F32, name="result", align_bytes=64)
+            for n in range(N_TILES):
+                acc = accs[n]
+                for g in range(GROUPS):
+                    w_cols = slice(g * N + n * P, g * N + (n + 1) * P)
+                    nc.tensor.matmul_mx(
+                        out=acc,
+                        lhsT=w2_w[:, w_cols].bitcast(FP8X4),
+                        lhsT_scale=w2_s[:, w_cols],
+                        rhs=z_w[g][:, cols].bitcast(FP8X4),
+                        rhs_scale=z_s[g][:, cols],
+                        start=(g == 0),
+                        stop=(g == GROUPS - 1),
+                    )
+            for n in range(N_TILES):
+                nc.scalar.activation(result[:, n, :], accs[n], TANH, bias=b2_sb[:, n : n + 1])
+            nc.sync.dma_start(out_rows[:, :, cols], result[:])
+
+        gather_words(0)
+        permute_w4()
+        cast_w1(0)
+        cast_w1(1)
+        quantize_w1(0, 0, 1)
+        gather_words(1)
+        quantize_w1(0, 1, 2)
+        encode(0, 0)
+        quantize_w1(0, 2, 4)
+        encode(0, 1)
+        for c in range(TILES - 2):
+            encode(c + 1, 0)
+            spread_gain(c, PAIRS)
+            pick_query(c, 0, PAIRS)
+            encode(c + 1, 1)
+            pick_candidate(c, 0, PAIRS)
+            if c == 0:
+                cast_w1(2)
+            if c == 1:
+                cast_w1(3)
+            if c == 2:
+                quantize_w1(1, 0, 4)
+                interleave(nc.scalar.copy, w2_bf[:, 0:N, :], w2_raw[0][:])
+            if c == 3:
+                round_z(nc.scalar.copy, 0, 0, PAIRS)
+            if c == 4:
+                interleave(nc.scalar.copy, w2_bf[:, N : 2 * N, :], w2_raw[1][:])
+                quantize_z(0, 0, PAIRS)
+            if c == 5:
+                quantize_w2(0, 512)
+                quantize_w2(512, 256)
+        first_c, second_c, third_c = CHUNKS
+        spread_gain(6, first_c[1])
+        spread_gain(7, first_c[1])
+        encode(7, 0)
+        pick_query(6, *first_c)
+        encode(7, 1)
+        pick_candidate(6, *first_c)
+        pick_query(7, *first_c)
+        pick_query(6, *second_c)
+        pick_candidate(7, *first_c)
+        round_z(nc.scalar.copy, 1, *first_c)
+        pick_candidate(6, *second_c)
+        pick_query(7, *second_c)
+        pick_query(6, *third_c)
+        pick_candidate(7, *second_c)
+        round_z(nc.scalar.copy, 1, *second_c)
+        pick_candidate(6, *third_c)
+        pick_query(7, *third_c)
+        quantize_z(1, *first_c)
+        y_first = [psum_y.tile([P, first_c[1]], F32, name="acc_y") for n in range(N_TILES)]
+        score(*first_c, [acc[:] for acc in y_first])
+        pick_candidate(7, *third_c)
+        quantize_z(1, *second_c)
+        y_second = psum_y.tile([P, N_TILES, second_c[1]], F32, name="acc_y")
+        score(*second_c, [y_second[:, n, :] for n in range(N_TILES)])
+        round_z(nc.vector.tensor_copy, 1, *third_c)
+        quantize_z(1, *third_c)
+        y_third = [
+            psum_a.tile([P, third_c[1]], F32, name="acc_a"),
+            psum_b.tile([P, third_c[1]], F32, name="acc_b"),
+            psum_a.tile([P, third_c[1]], F32, name="acc_a"),
+        ]
+        score(*third_c, [acc[:] for acc in y_third])

@@ -24,7 +24,10 @@ BANK = 512
 GROUPS = H // PASS
 TILES = H // P
 N_TILES = N // P
-W1_CHUNK = 256
+RUN = 2
+SPAN = PACK * RUN
+GZ_ROW = SPAN - RUN + 1
+W1_LOADS = [(0, 256), (256, 256), (512, 512)]
 CHUNKS = [(0, 256), (256, 128), (384, 128)]
 
 
@@ -47,20 +50,19 @@ def tile_list_code_pair_match_kernel(
         w4_raw = keep.tile([P, H // 2], I32, name="w4_raw", align_bytes=64)
         w4s_raw = keep.tile([P, H // 4], I32, name="w4s_raw", align_bytes=64)
         w1_raw = [
-            keep.tile([P, PACK, W1_CHUNK], F32, name="w1_raw%d" % i, align_bytes=64)
-            for i in range(H // W1_CHUNK)
+            keep.tile([P, PACK, count], F32, name="w1_raw%d" % first, align_bytes=64)
+            for first, count in W1_LOADS
         ]
         w2_raw = [keep.tile([P, PACK, N], F32, name="w2_raw%d" % g, align_bytes=64) for g in range(GROUPS)]
-        gz_sb = keep.tile([P, GROUPS, PACK], F32, name="gz_sb")
+        gz_sb = keep.tile([P, GROUPS, GZ_ROW], F32, name="gz_sb")
         b2_sb = keep.tile([P, N_TILES], F32, name="b2_sb")
         warm_in = keep.tile([P, 1], F32, name="warm_in")
         warm_out = keep.tile([P, 1], F32, name="warm_out")
 
         nc.vector.memset(tab_s[:], 0)
-        nc.gpsimd.memset(warm_in[:], 0.0)
-        nc.gpsimd.memset(w4s_raw[:], 0)
+        nc.vector.memset(w4s_raw[:], 0)
+        nc.vector.memset(warm_in[:], 0.0)
         nc.scalar.activation(warm_out[:], warm_in[:], TANH)
-        nc.gpsimd.dma_start(gz_sb[:], gz.rearrange("(g p t) -> p g t", g=GROUPS, t=PACK))
 
         def load_scale_rows(plane, rows):
             by_r = rows.rearrange("(q r) c -> r q c", r=4)
@@ -70,7 +72,8 @@ def tile_list_code_pair_match_kernel(
         w1_rows = w1.rearrange("(p j) c -> p j c", j=PACK)
 
         def load_w1(i):
-            nc.sync.dma_start(w1_raw[i][:], w1_rows[:, :, i * W1_CHUNK : (i + 1) * W1_CHUNK])
+            first, count = W1_LOADS[i]
+            nc.sync.dma_start(w1_raw[i][:], w1_rows[:, :, first : first + count])
 
         nc.sync.dma_start(offs_sb[:], offs)
         load_scale_rows(tab_s, tab_scales[0])
@@ -81,48 +84,51 @@ def tile_list_code_pair_match_kernel(
         load_w1(1)
         nc.sync.dma_start(pos1_sb[:], pos1)
         nc.sync.dma_start(pos2_sb[:], pos2)
+        gz_runs = gz.rearrange("(g u s) -> u g s", g=GROUPS, s=SPAN)
+        for e in range(RUN):
+            nc.sync.dma_start(gz_sb[e:P:RUN, :, :], gz_runs[:, :, e : e + GZ_ROW])
         load_w1(2)
-        load_w1(3)
+        w2_rows = w2.rearrange("(g u t e) n -> g e u t n", g=GROUPS, t=PACK, e=RUN)
         for g in range(GROUPS):
-            nc.sync.dma_start(
-                w2_raw[g][:], w2[g * PASS : (g + 1) * PASS, :].rearrange("(p j) n -> p j n", j=PACK)
-            )
+            for e in range(RUN):
+                nc.sync.dma_start(w2_raw[g][e:P:RUN, :, :], w2_rows[g, e])
         with nc.allow_non_contiguous_dma(reason="one bias value to a partition"):
             nc.sync.dma_start(b2_sb[:], b2.rearrange("(c p) -> p c", p=P))
 
         v_w = keep.tile([P, S], U32, name="v_w", align_bytes=64)
         v_s = keep.tile([P, S], U8, name="v_s", align_bytes=64)
-        nc.vector.tensor_copy(v_s[:], tab_s[:].bitcast(U8).indirect(offs_sb[:]))
+
+        def gather_scales():
+            nc.vector.tensor_copy(v_s[:], tab_s[:].bitcast(U8).indirect(offs_sb[:]))
 
         def gather_words(half):
             cols = slice(half * BANK, (half + 1) * BANK)
             lst = offs_sb[:, half * BANK // 16 : (half + 1) * BANK // 16]
             nc.vector.tensor_copy(v_w[:, cols], tab_w[:].bitcast(U32).indirect(lst))
 
-        w4_w = keep.tile([P, 2 * H], U8, name="w4_w", align_bytes=64)
-        w4_s = keep.tile([P, H], U8, name="w4_s", align_bytes=64)
+        w4_w = keep.tile([P, H // 2], I32, name="w4_w", align_bytes=64)
+        w4_s = keep.tile([P, H // 4], I32, name="w4_s", align_bytes=64)
 
         def permute_w4():
             nc.vector.tensor_copy(
-                w4_w[:].bitcast(U16).rearrange("p (g t m) -> p g t m", g=GROUPS, t=PACK),
-                w4_raw[:].bitcast(U16).rearrange("p (g m t) -> p g t m", g=GROUPS, t=PACK),
+                w4_w[:].rearrange("p (g t u) -> p g t u", g=GROUPS, t=PACK),
+                w4_raw[:].rearrange("p (g u t) -> p g t u", g=GROUPS, t=PACK),
             )
             nc.vector.tensor_copy(
-                w4_s[:].rearrange("p (g t m) -> p g t m", g=GROUPS, t=PACK),
-                w4s_raw[:].bitcast(U8).rearrange("p (g m t) -> p g t m", g=GROUPS, t=PACK),
+                w4_s[:].bitcast(U16).rearrange("p (g t u) -> p g t u", g=GROUPS, t=PACK),
+                w4s_raw[:].bitcast(U16).rearrange("p (g u t) -> p g t u", g=GROUPS, t=PACK),
             )
 
         w1_bf = [keep.tile([P, PACK, P, PACK], BF16, name="w1_bf%d" % g, align_bytes=64) for g in range(GROUPS)]
         w1_w = keep.tile([P, H], U32, name="w1_w", align_bytes=64)
         w1_s = keep.tile([P, H], U8, name="w1_s", align_bytes=64)
 
-        def cast_w1(i):
-            g, part = divmod(i, PASS // W1_CHUNK)
-            m_count = W1_CHUNK // PACK
-            ms = slice(part * m_count, (part + 1) * m_count)
+        def cast_w1(i, t):
+            first, count = W1_LOADS[i]
+            g, m0 = first // PASS, first % PASS // PACK
             nc.scalar.copy(
-                w1_bf[g][:, :, ms, :].rearrange("p t m j -> p m j t"),
-                w1_raw[i][:].rearrange("p j (m t) -> p m j t", t=PACK),
+                w1_bf[g][:, t, m0 : m0 + count // PACK, :].rearrange("p (u e) j -> p u j e", e=RUN),
+                w1_raw[i][:].rearrange("p j (u t e) -> p t u j e", t=PACK, e=RUN)[:, t],
             )
 
         def quantize(codes, scales, src, first, count):
@@ -146,6 +152,11 @@ def tile_list_code_pair_match_kernel(
                 src.rearrange("p t (c i) -> p c t i", i=4),
             )
 
+        def cast_w2(g):
+            for first in range(0, N, P):
+                dst = w2_bf[:, g * N + first : g * N + first + P, :]
+                interleave(nc.scalar.copy, dst, w2_raw[g][:, :, first : first + P])
+
         def quantize_w2(first, count):
             src = w2_bf[:, first : first + count, :].rearrange("p n j -> p (n j)")
             quantize(w2_w, w2_s, src, first, count)
@@ -157,8 +168,8 @@ def tile_list_code_pair_match_kernel(
             acc_b = psum_b.tile([P, BANK], F32, name="acc_b")
             nc.tensor.matmul_mx(
                 out=acc_b[:],
-                lhsT=w4_w[:, 2 * c * P : 2 * (c + 1) * P].bitcast(FP4X4),
-                lhsT_scale=w4_s[:, c * P : (c + 1) * P],
+                lhsT=w4_w[:].bitcast(U8)[:, 2 * c * P : 2 * (c + 1) * P].bitcast(FP4X4),
+                lhsT_scale=w4_s[:].bitcast(U8)[:, c * P : (c + 1) * P],
                 rhs=v_w[:, cols].bitcast(FP8X4),
                 rhs_scale=v_s[:, cols],
                 start=True,
@@ -177,64 +188,80 @@ def tile_list_code_pair_match_kernel(
             nc.scalar.copy(h[c][:, cols], acc_b[:])
             nc.vector.tensor_tensor(h[c][:, cols], acc_a[:], h[c][:, cols], MAX)
 
-        z_f = [keep.tile([P, PACK, PAIRS], F32, name="z_f%d" % g, align_bytes=64) for g in range(GROUPS)]
-        z_bf = [keep.tile([P, PAIRS, PACK], BF16, name="z_bf%d" % g, align_bytes=64) for g in range(GROUPS)]
+        z_f = {(0, 0): keep.tile([P, PACK, PAIRS], F32, name="z_f0", align_bytes=64)}
+        for first, count in CHUNKS:
+            z_f[(1, first)] = keep.tile([P, PACK, count], F32, name="z_f1_%d" % first, align_bytes=64)
+        z_bf = {}
         z_w = [keep.tile([P, PAIRS], U32, name="z_w%d" % g, align_bytes=64) for g in range(GROUPS)]
         z_s = [keep.tile([P, PAIRS], U8, name="z_s%d" % g, align_bytes=64) for g in range(GROUPS)]
-        query = {}
-
         gain = [keep.tile([P, PAIRS], F32, name="gain%d" % c, align_bytes=64) for c in range(TILES)]
+        query = {}
 
         def spread_gain(c, count):
             g, t = divmod(c, PACK)
-            nc.scalar.copy(gain[c][:, 0:count], gz_sb[:, g, t : t + 1].to_broadcast([P, count]))
+            nc.scalar.copy(gain[c][:, 0:count], gz_sb[:, g, RUN * t : RUN * t + 1].to_broadcast([P, count]))
 
         def pick_query(c, first, count):
-            picked = ring.tile([P, count], F32, name="picked", align_bytes=64)
+            if (c, first) == (TILES - 1, CHUNKS[2][0]):
+                picked = keep.tile([P, count], F32, name="picked_last", tag="z_first", align_bytes=64)
+            else:
+                picked = ring.tile([P, count], F32, name="picked", align_bytes=64)
             lst = pos1_sb[:, first // 16 : (first + count) // 16]
             nc.vector.tensor_tensor(picked[:], h[c][:].indirect(lst), gain[c][:, 0:count], MULT)
-            query[(c, first)] = picked
+            for at in range(0, count, P):
+                query[(c, first + at)] = (picked, at)
 
         def pick_candidate(c, first, count):
             g, t = divmod(c, PACK)
             lst = pos2_sb[:, first // 16 : (first + count) // 16]
-            nc.vector.tensor_tensor(
-                z_f[g][:, t, first : first + count], h[c][:].indirect(lst), query[(c, first)][:], MULT
-            )
+            picked, at = query[(c, first)]
+            nc.vector.tensor_tensor(z_f[(g, first)][:, t, :], h[c][:].indirect(lst), picked[:, at : at + count], MULT)
 
         def round_z(copy, g, first, count):
-            interleave(copy, z_bf[g][:, first : first + count, :], z_f[g][:, :, first : first + count])
+            base = first if g else 0
+            src = z_f[(g, base)][:, :, first - base : first - base + count]
+            if (g, base) not in z_bf:
+                tag = ["z_zero", "z_first" if first == 0 else "z_rest"][g]
+                width = count if g else PAIRS
+                z_bf[(g, base)] = keep.tile([P, width, PACK], BF16, name="z_bf", tag=tag, align_bytes=64)
+            interleave(copy, z_bf[(g, base)][:, first - base : first - base + count, :], src)
 
         def quantize_z(g, first, count):
-            src = z_bf[g][:, first : first + count, :].rearrange("p n j -> p (n j)")
+            src = z_bf[(g, first)][:].rearrange("p n j -> p (n j)")
             quantize(z_w[g], z_s[g], src, first, count)
 
         out_rows = out.rearrange("(c p) j -> p c j", p=P)
 
-        def score(first, count, accs):
+        def score_pass(g, n, first, count, acc):
+            cols = slice(first, first + count)
+            w_cols = slice(g * N + n * P, g * N + (n + 1) * P)
+            nc.tensor.matmul_mx(
+                out=acc,
+                lhsT=w2_w[:, w_cols].bitcast(FP8X4),
+                lhsT_scale=w2_s[:, w_cols],
+                rhs=z_w[g][:, cols].bitcast(FP8X4),
+                rhs_scale=z_s[g][:, cols],
+                start=(g == 0),
+                stop=(g == GROUPS - 1),
+            )
+
+        def score(first, count, accs, unopened):
             cols = slice(first, first + count)
             result = ring.tile([P, N_TILES, count], F32, name="result", align_bytes=64)
             for n in range(N_TILES):
-                acc = accs[n]
-                for g in range(GROUPS):
-                    w_cols = slice(g * N + n * P, g * N + (n + 1) * P)
-                    nc.tensor.matmul_mx(
-                        out=acc,
-                        lhsT=w2_w[:, w_cols].bitcast(FP8X4),
-                        lhsT_scale=w2_s[:, w_cols],
-                        rhs=z_w[g][:, cols].bitcast(FP8X4),
-                        rhs_scale=z_s[g][:, cols],
-                        start=(g == 0),
-                        stop=(g == GROUPS - 1),
-                    )
+                if n in unopened:
+                    score_pass(0, n, first, count, accs[n])
+                score_pass(1, n, first, count, accs[n])
             for n in range(N_TILES):
                 nc.scalar.activation(result[:, n, :], accs[n], TANH, bias=b2_sb[:, n : n + 1])
             nc.sync.dma_start(out_rows[:, :, cols], result[:])
 
+        gather_scales()
         gather_words(0)
         permute_w4()
-        cast_w1(0)
-        cast_w1(1)
+        for t in range(PACK):
+            cast_w1(0, t)
+            cast_w1(1, t)
         quantize_w1(0, 0, 1)
         gather_words(1)
         quantize_w1(0, 1, 2)
@@ -246,18 +273,21 @@ def tile_list_code_pair_match_kernel(
             spread_gain(c, PAIRS)
             pick_query(c, 0, PAIRS)
             encode(c + 1, 1)
-            pick_candidate(c, 0, PAIRS)
-            if c == 0:
-                cast_w1(2)
+            for first, count in CHUNKS if c >= PACK else [(0, PAIRS)]:
+                pick_candidate(c, first, count)
+            if c < 2:
+                cast_w1(2, 2 * c)
+                cast_w1(2, 2 * c + 1)
             if c == 1:
-                cast_w1(3)
+                quantize_w1(1, 0, 2)
             if c == 2:
-                quantize_w1(1, 0, 4)
-                interleave(nc.scalar.copy, w2_bf[:, 0:N, :], w2_raw[0][:])
+                quantize_w1(1, 2, 4)
+                cast_w2(0)
             if c == 3:
-                round_z(nc.scalar.copy, 0, 0, PAIRS)
+                for first in range(0, PAIRS, P):
+                    round_z(nc.scalar.copy, 0, first, P)
             if c == 4:
-                interleave(nc.scalar.copy, w2_bf[:, N : 2 * N, :], w2_raw[1][:])
+                cast_w2(1)
                 quantize_z(0, 0, PAIRS)
             if c == 5:
                 quantize_w2(0, 512)
@@ -268,6 +298,25 @@ def tile_list_code_pair_match_kernel(
         encode(7, 0)
         pick_query(6, *first_c)
         encode(7, 1)
+        y_pair = psum_y.tile([P, 2, first_c[1]], F32, name="acc_y")
+        y_lone = psum_y.tile([P, first_c[1]], F32, name="acc_y")
+        y_first = [y_pair[:, 0, :], y_lone[:], y_pair[:, 1, :]]
+        y_rest = [
+            psum_y.tile([P, P], F32, name="acc_y"),
+            psum_y.tile([P, P], F32, name="acc_y"),
+            psum_b.tile([P, P], F32, name="acc_b"),
+            psum_b.tile([P, P], F32, name="acc_b"),
+            psum_a.tile([P, P], F32, name="acc_a"),
+            psum_a.tile([P, P], F32, name="acc_a"),
+        ]
+        y_second = [acc[:] for acc in y_rest[:N_TILES]]
+        y_third = [acc[:] for acc in y_rest[N_TILES:]]
+        for n in range(2):
+            score_pass(0, n, *first_c, y_first[n])
+        for n in range(N_TILES):
+            score_pass(0, n, *second_c, y_second[n])
+        for n in range(N_TILES):
+            score_pass(0, n, *third_c, y_third[n])
         pick_candidate(6, *first_c)
         pick_query(7, *first_c)
         pick_query(6, *second_c)
@@ -279,19 +328,12 @@ def tile_list_code_pair_match_kernel(
         pick_candidate(7, *second_c)
         round_z(nc.scalar.copy, 1, *second_c)
         pick_candidate(6, *third_c)
-        pick_query(7, *third_c)
         quantize_z(1, *first_c)
-        y_first = [psum_y.tile([P, first_c[1]], F32, name="acc_y") for n in range(N_TILES)]
-        score(*first_c, [acc[:] for acc in y_first])
-        pick_candidate(7, *third_c)
+        score(*first_c, y_first, [2])
+        pick_query(7, *third_c)
         quantize_z(1, *second_c)
-        y_second = psum_y.tile([P, N_TILES, second_c[1]], F32, name="acc_y")
-        score(*second_c, [y_second[:, n, :] for n in range(N_TILES)])
+        score(*second_c, y_second, [])
+        pick_candidate(7, *third_c)
         round_z(nc.vector.tensor_copy, 1, *third_c)
         quantize_z(1, *third_c)
-        y_third = [
-            psum_a.tile([P, third_c[1]], F32, name="acc_a"),
-            psum_b.tile([P, third_c[1]], F32, name="acc_b"),
-            psum_a.tile([P, third_c[1]], F32, name="acc_a"),
-        ]
-        score(*third_c, [acc[:] for acc in y_third])
+        score(*third_c, y_third, [])

@@ -15,6 +15,7 @@ FP8X4 = mybir.dt.float8_e4m3fn_x4
 FP4X4 = mybir.dt.float4_e2m1fn_x4
 MULT = mybir.AluOpType.mult
 MAX = mybir.AluOpType.max
+COPY = mybir.ActivationFunctionType.Copy
 TANH = mybir.ActivationFunctionType.Tanh
 
 P = 128
@@ -27,6 +28,7 @@ N_TILES = N // P
 RUN = 2
 SPAN = PACK * RUN
 GZ_ROW = SPAN - RUN + 1
+W1_CALLS = [(0, 2), (2, 4), (4, 6), (6, 8)]
 W1_LOADS = [(0, 256), (256, 256), (512, 512)]
 CHUNKS = [(0, 256), (256, 128), (384, 128)]
 
@@ -38,9 +40,10 @@ def tile_list_code_pair_match_kernel(
     with ExitStack() as ctx:
         keep = ctx.enter_context(tc.tile_pool(name="keep", bufs=1))
         ring = ctx.enter_context(tc.tile_pool(name="ring", bufs=3))
-        psum_a = ctx.enter_context(tc.psum_pool(name="psum_a", bufs=2))
-        psum_b = ctx.enter_context(tc.psum_pool(name="psum_b", bufs=2))
-        psum_y = ctx.enter_context(tc.psum_pool(name="psum_y", bufs=4))
+        picks = ctx.enter_context(tc.tile_pool(name="picks", bufs=5))
+        psum_a = ctx.enter_context(tc.psum_pool(name="psum_a", bufs=3))
+        psum_b = ctx.enter_context(tc.psum_pool(name="psum_b", bufs=1))
+        psum_y = ctx.enter_context(tc.psum_pool(name="psum_y", bufs=3))
 
         offs_sb = keep.tile([P, S // 16], U16, name="offs_sb")
         pos1_sb = keep.tile([P, PAIRS // 16], U16, name="pos1_sb")
@@ -48,21 +51,16 @@ def tile_list_code_pair_match_kernel(
         tab_w = keep.tile([P, T], I32, name="tab_w", align_bytes=64)
         tab_s = keep.tile([P, T // 4], I32, name="tab_s", align_bytes=64)
         w4_raw = keep.tile([P, H // 2], I32, name="w4_raw", align_bytes=64)
-        w4s_raw = keep.tile([P, H // 4], I32, name="w4s_raw", align_bytes=64)
+        w4s_raw = keep.tile([P, H // 4], I32, name="w4s_raw", tag="w4s_raw", align_bytes=64)
         w1_raw = [
-            keep.tile([P, PACK, count], F32, name="w1_raw%d" % first, align_bytes=64)
+            keep.tile([P, PACK, count], F32, name="w1_raw", tag="raw%d" % first, align_bytes=64)
             for first, count in W1_LOADS
         ]
-        w2_raw = [keep.tile([P, PACK, N], F32, name="w2_raw%d" % g, align_bytes=64) for g in range(GROUPS)]
         gz_sb = keep.tile([P, GROUPS, GZ_ROW], F32, name="gz_sb")
         b2_sb = keep.tile([P, N_TILES], F32, name="b2_sb")
-        warm_in = keep.tile([P, 1], F32, name="warm_in")
-        warm_out = keep.tile([P, 1], F32, name="warm_out")
 
         nc.vector.memset(tab_s[:], 0)
         nc.vector.memset(w4s_raw[:], 0)
-        nc.vector.memset(warm_in[:], 0.0)
-        nc.scalar.activation(warm_out[:], warm_in[:], TANH)
 
         def load_scale_rows(plane, rows):
             by_r = rows.rearrange("(q r) c -> r q c", r=4)
@@ -76,9 +74,9 @@ def tile_list_code_pair_match_kernel(
             nc.sync.dma_start(w1_raw[i][:], w1_rows[:, :, first : first + count])
 
         nc.sync.dma_start(offs_sb[:], offs)
-        load_scale_rows(tab_s, tab_scales[0])
         nc.sync.dma_start(tab_w[:], tab_words[0].rearrange("p t i -> p (t i)").bitcast(I32))
         nc.sync.dma_start(w4_raw[:], w4_words[0].bitcast(I32))
+        load_scale_rows(tab_s, tab_scales[0])
         load_w1(0)
         load_scale_rows(w4s_raw, w4_scales[0])
         load_w1(1)
@@ -89,22 +87,26 @@ def tile_list_code_pair_match_kernel(
             nc.sync.dma_start(gz_sb[e:P:RUN, :, :], gz_runs[:, :, e : e + GZ_ROW])
         load_w1(2)
         w2_rows = w2.rearrange("(g u t e) n -> g e u t n", g=GROUPS, t=PACK, e=RUN)
-        for g in range(GROUPS):
+        w2_raw = []
+
+        def load_w2(g):
+            w2_raw.append(keep.tile([P, PACK, N], F32, name="w2_raw", tag="raw%d" % W1_LOADS[g][0], align_bytes=64))
             for e in range(RUN):
-                nc.sync.dma_start(w2_raw[g][e:P:RUN, :, :], w2_rows[g, e])
+                nc.scalar.dma_start(w2_raw[g][e:P:RUN, :, :], w2_rows[g, e])
+
         with nc.allow_non_contiguous_dma(reason="one bias value to a partition"):
             nc.sync.dma_start(b2_sb[:], b2.rearrange("(c p) -> p c", p=P))
 
-        v_w = keep.tile([P, S], U32, name="v_w", align_bytes=64)
+        v_w = {}
         v_s = keep.tile([P, S], U8, name="v_s", align_bytes=64)
 
         def gather_scales():
             nc.vector.tensor_copy(v_s[:], tab_s[:].bitcast(U8).indirect(offs_sb[:]))
 
-        def gather_words(half):
-            cols = slice(half * BANK, (half + 1) * BANK)
+        def gather_words(half, tag):
+            v_w[half] = keep.tile([P, BANK], U32, name="v_w", tag=tag, align_bytes=64)
             lst = offs_sb[:, half * BANK // 16 : (half + 1) * BANK // 16]
-            nc.vector.tensor_copy(v_w[:, cols], tab_w[:].bitcast(U32).indirect(lst))
+            nc.vector.tensor_copy(v_w[half][:], tab_w[:].bitcast(U32).indirect(lst))
 
         w4_w = keep.tile([P, H // 2], I32, name="w4_w", align_bytes=64)
         w4_s = keep.tile([P, H // 4], I32, name="w4_s", align_bytes=64)
@@ -119,16 +121,22 @@ def tile_list_code_pair_match_kernel(
                 w4s_raw[:].bitcast(U16).rearrange("p (g u t) -> p g t u", g=GROUPS, t=PACK),
             )
 
-        w1_bf = [keep.tile([P, PACK, P, PACK], BF16, name="w1_bf%d" % g, align_bytes=64) for g in range(GROUPS)]
+        w1_bf = {}
+        for c0, c1 in W1_CALLS:
+            staged = keep.tile([P, c1 - c0, P, PACK], BF16, name="w1_bf", tag="w1_bf%d" % c0, align_bytes=64)
+            for c in range(c0, c1):
+                w1_bf[c] = (staged, c - c0)
         w1_w = keep.tile([P, H], U32, name="w1_w", align_bytes=64)
         w1_s = keep.tile([P, H], U8, name="w1_s", align_bytes=64)
 
         def cast_w1(i, t):
             first, count = W1_LOADS[i]
             g, m0 = first // PASS, first % PASS // PACK
-            nc.scalar.copy(
-                w1_bf[g][:, t, m0 : m0 + count // PACK, :].rearrange("p (u e) j -> p u j e", e=RUN),
+            staged, slot = w1_bf[g * PACK + t]
+            nc.scalar.activation(
+                staged[:, slot, m0 : m0 + count // PACK, :].rearrange("p (u e) j -> p u j e", e=RUN),
                 w1_raw[i][:].rearrange("p j (u t e) -> p t u j e", t=PACK, e=RUN)[:, t],
+                COPY,
             )
 
         def quantize(codes, scales, src, first, count):
@@ -138,9 +146,10 @@ def tile_list_code_pair_match_kernel(
                 in_=src,
             )
 
-        def quantize_w1(g, t0, t1):
-            src = w1_bf[g][:, t0:t1, :, :].rearrange("p t m j -> p (t m j)")
-            quantize(w1_w, w1_s, src, g * PASS + t0 * P, (t1 - t0) * P)
+        def quantize_w1(i):
+            c0, c1 = W1_CALLS[i]
+            src = w1_bf[c0][0][:].rearrange("p t m j -> p (t m j)")
+            quantize(w1_w, w1_s, src, c0 * P, (c1 - c0) * P)
 
         w2_bf = keep.tile([P, GROUPS * N, PACK], BF16, name="w2_bf", align_bytes=64)
         w2_w = keep.tile([P, GROUPS * N], U32, name="w2_w", align_bytes=64)
@@ -165,12 +174,12 @@ def tile_list_code_pair_match_kernel(
 
         def encode(c, half):
             cols = slice(half * BANK, (half + 1) * BANK)
-            acc_b = psum_b.tile([P, BANK], F32, name="acc_b")
+            acc_b = psum_b.tile([P, BANK], F32, name="acc_b", tag="acc_b%d" % half)
             nc.tensor.matmul_mx(
                 out=acc_b[:],
                 lhsT=w4_w[:].bitcast(U8)[:, 2 * c * P : 2 * (c + 1) * P].bitcast(FP4X4),
                 lhsT_scale=w4_s[:].bitcast(U8)[:, c * P : (c + 1) * P],
-                rhs=v_w[:, cols].bitcast(FP8X4),
+                rhs=v_w[half][:].bitcast(FP8X4),
                 rhs_scale=v_s[:, cols],
                 start=True,
                 stop=True,
@@ -180,7 +189,7 @@ def tile_list_code_pair_match_kernel(
                 out=acc_a[:],
                 lhsT=w1_w[:, c * P : (c + 1) * P].bitcast(FP8X4),
                 lhsT_scale=w1_s[:, c * P : (c + 1) * P],
-                rhs=v_w[:, cols].bitcast(FP8X4),
+                rhs=v_w[half][:].bitcast(FP8X4),
                 rhs_scale=v_s[:, cols],
                 start=True,
                 stop=True,
@@ -189,7 +198,7 @@ def tile_list_code_pair_match_kernel(
             nc.vector.tensor_tensor(h[c][:, cols], acc_a[:], h[c][:, cols], MAX)
 
         z_f = {(0, 0): keep.tile([P, PACK, PAIRS], F32, name="z_f0", align_bytes=64)}
-        for first, count in CHUNKS:
+        for first, count in CHUNKS[:2]:
             z_f[(1, first)] = keep.tile([P, PACK, count], F32, name="z_f1_%d" % first, align_bytes=64)
         z_bf = {}
         z_w = [keep.tile([P, PAIRS], U32, name="z_w%d" % g, align_bytes=64) for g in range(GROUPS)]
@@ -202,10 +211,7 @@ def tile_list_code_pair_match_kernel(
             nc.scalar.copy(gain[c][:, 0:count], gz_sb[:, g, RUN * t : RUN * t + 1].to_broadcast([P, count]))
 
         def pick_query(c, first, count):
-            if (c, first) == (TILES - 1, CHUNKS[2][0]):
-                picked = keep.tile([P, count], F32, name="picked_last", tag="z_first", align_bytes=64)
-            else:
-                picked = ring.tile([P, count], F32, name="picked", align_bytes=64)
+            picked = picks.tile([P, count], F32, name="picked", align_bytes=64)
             lst = pos1_sb[:, first // 16 : (first + count) // 16]
             nc.vector.tensor_tensor(picked[:], h[c][:].indirect(lst), gain[c][:, 0:count], MULT)
             for at in range(0, count, P):
@@ -248,64 +254,65 @@ def tile_list_code_pair_match_kernel(
         def score(first, count, accs, unopened):
             cols = slice(first, first + count)
             result = ring.tile([P, N_TILES, count], F32, name="result", align_bytes=64)
-            for n in range(N_TILES):
+            order = [1, 0, 2]
+            for n in order:
                 if n in unopened:
                     score_pass(0, n, first, count, accs[n])
                 score_pass(1, n, first, count, accs[n])
-            for n in range(N_TILES):
+            for n in order:
                 nc.scalar.activation(result[:, n, :], accs[n], TANH, bias=b2_sb[:, n : n + 1])
-            nc.sync.dma_start(out_rows[:, :, cols], result[:])
+                if first == CHUNKS[-1][0]:
+                    queue = nc.scalar if n == order[-1] else nc.sync
+                    queue.dma_start(out_rows[:, n, cols], result[:, n, :])
+            if first != CHUNKS[-1][0]:
+                nc.sync.dma_start(out_rows[:, :, cols], result[:])
 
+        gather_words(0, "v_w0")
         gather_scales()
-        gather_words(0)
         permute_w4()
         for t in range(PACK):
             cast_w1(0, t)
             cast_w1(1, t)
-        quantize_w1(0, 0, 1)
-        gather_words(1)
-        quantize_w1(0, 1, 2)
+        load_w2(0)
+        load_w2(1)
+        quantize_w1(0)
+        gather_words(1, "w1_bf0")
         encode(0, 0)
-        quantize_w1(0, 2, 4)
+        quantize_w1(1)
+        encode(1, 0)
         encode(0, 1)
+        encode(1, 1)
+        first_c, second_c, third_c = CHUNKS
         for c in range(TILES - 2):
-            encode(c + 1, 0)
+            chunk = (0, PAIRS) if c < PACK else first_c
             spread_gain(c, PAIRS)
             pick_query(c, 0, PAIRS)
-            encode(c + 1, 1)
-            for first, count in CHUNKS if c >= PACK else [(0, PAIRS)]:
-                pick_candidate(c, first, count)
+            encode(c + 2, 0)
+            pick_candidate(c, *chunk)
+            encode(c + 2, 1)
             if c < 2:
                 cast_w1(2, 2 * c)
                 cast_w1(2, 2 * c + 1)
-            if c == 1:
-                quantize_w1(1, 0, 2)
-            if c == 2:
-                quantize_w1(1, 2, 4)
-                cast_w2(0)
+                quantize_w1(2 + c)
+            if c in (1, 2):
+                cast_w2(c - 1)
             if c == 3:
-                for first in range(0, PAIRS, P):
-                    round_z(nc.scalar.copy, 0, first, P)
-            if c == 4:
-                cast_w2(1)
-                quantize_z(0, 0, PAIRS)
-            if c == 5:
                 quantize_w2(0, 512)
                 quantize_w2(512, 256)
-        first_c, second_c, third_c = CHUNKS
-        spread_gain(6, first_c[1])
-        spread_gain(7, first_c[1])
-        encode(7, 0)
-        pick_query(6, *first_c)
-        encode(7, 1)
+                for first in range(0, PAIRS, P):
+                    round_z(nc.scalar.copy, 0, first, P)
+            if c == 5:
+                quantize_z(0, 0, PAIRS)
+        spread_gain(6, PAIRS)
+        spread_gain(7, PAIRS)
         y_pair = psum_y.tile([P, 2, first_c[1]], F32, name="acc_y")
         y_lone = psum_y.tile([P, first_c[1]], F32, name="acc_y")
         y_first = [y_pair[:, 0, :], y_lone[:], y_pair[:, 1, :]]
         y_rest = [
             psum_y.tile([P, P], F32, name="acc_y"),
-            psum_y.tile([P, P], F32, name="acc_y"),
-            psum_b.tile([P, P], F32, name="acc_b"),
-            psum_b.tile([P, P], F32, name="acc_b"),
+            psum_b.tile([P, P], F32, name="acc_y", tag="acc_b0"),
+            psum_b.tile([P, P], F32, name="acc_y", tag="acc_b1"),
+            psum_a.tile([P, P], F32, name="acc_a"),
             psum_a.tile([P, P], F32, name="acc_a"),
             psum_a.tile([P, P], F32, name="acc_a"),
         ]
@@ -317,20 +324,19 @@ def tile_list_code_pair_match_kernel(
             score_pass(0, n, *second_c, y_second[n])
         for n in range(N_TILES):
             score_pass(0, n, *third_c, y_third[n])
+        pick_query(6, 0, PAIRS)
+        pick_query(7, 0, PAIRS)
         pick_candidate(6, *first_c)
-        pick_query(7, *first_c)
-        pick_query(6, *second_c)
         pick_candidate(7, *first_c)
         round_z(nc.scalar.copy, 1, *first_c)
-        pick_candidate(6, *second_c)
-        pick_query(7, *second_c)
-        pick_query(6, *third_c)
-        pick_candidate(7, *second_c)
+        for c in range(PACK, TILES):
+            pick_candidate(c, *second_c)
         round_z(nc.scalar.copy, 1, *second_c)
-        pick_candidate(6, *third_c)
         quantize_z(1, *first_c)
         score(*first_c, y_first, [2])
-        pick_query(7, *third_c)
+        z_f[(1, third_c[0])] = keep.tile([P, PACK, third_c[1]], F32, name="z_f1_last", tag="z_first", align_bytes=64)
+        for c in range(PACK, TILES - 1):
+            pick_candidate(c, *third_c)
         quantize_z(1, *second_c)
         score(*second_c, y_second, [])
         pick_candidate(7, *third_c)

@@ -28,7 +28,7 @@ N_TILES = N // P
 RUN = 2
 SPAN = PACK * RUN
 GZ_ROW = SPAN - RUN + 1
-W1_CALLS = [(0, 2), (2, 4), (4, 6), (6, 8)]
+W1_CALLS = [(0, 1), (1, 2), (2, 4), (4, 6), (6, 8)]
 W1_LOADS = [(0, 256), (256, 256), (512, 512)]
 CHUNKS = [(0, 256), (256, 128), (384, 128)]
 
@@ -74,9 +74,9 @@ def tile_list_code_pair_match_kernel(
             nc.sync.dma_start(w1_raw[i][:], w1_rows[:, :, first : first + count])
 
         nc.sync.dma_start(offs_sb[:], offs)
-        nc.sync.dma_start(tab_w[:], tab_words[0].rearrange("p t i -> p (t i)").bitcast(I32))
         nc.sync.dma_start(w4_raw[:], w4_words[0].bitcast(I32))
         load_scale_rows(tab_s, tab_scales[0])
+        nc.sync.dma_start(tab_w[:], tab_words[0].rearrange("p t i -> p (t i)").bitcast(I32))
         load_w1(0)
         load_scale_rows(w4s_raw, w4_scales[0])
         load_w1(1)
@@ -267,20 +267,21 @@ def tile_list_code_pair_match_kernel(
             if first != CHUNKS[-1][0]:
                 nc.sync.dma_start(out_rows[:, :, cols], result[:])
 
-        gather_words(0, "v_w0")
         gather_scales()
+        gather_words(0, "v_w0")
         permute_w4()
+        gather_words(1, "v_w1")
         for t in range(PACK):
             cast_w1(0, t)
             cast_w1(1, t)
         load_w2(0)
         load_w2(1)
         quantize_w1(0)
-        gather_words(1, "w1_bf0")
-        encode(0, 0)
         quantize_w1(1)
-        encode(1, 0)
+        quantize_w1(2)
+        encode(0, 0)
         encode(0, 1)
+        encode(1, 0)
         encode(1, 1)
         first_c, second_c, third_c = CHUNKS
         for c in range(TILES - 2):
@@ -293,7 +294,7 @@ def tile_list_code_pair_match_kernel(
             if c < 2:
                 cast_w1(2, 2 * c)
                 cast_w1(2, 2 * c + 1)
-                quantize_w1(2 + c)
+                quantize_w1(3 + c)
             if c in (1, 2):
                 cast_w2(c - 1)
             if c == 3:

@@ -1,6 +1,7 @@
 from contextlib import ExitStack
 
 import concourse.mybir as mybir
+from concourse.masks import make_identity
 
 K, H, N, T, S, PAIRS = 512, 1024, 384, 2048, 1024, 512
 FLOPS = 2 * (2 * K * H * S) + 2 * H * N * PAIRS
@@ -16,6 +17,7 @@ FP4X4 = mybir.dt.float4_e2m1fn_x4
 MULT = mybir.AluOpType.mult
 MAX = mybir.AluOpType.max
 COPY = mybir.ActivationFunctionType.Copy
+RELU = mybir.ActivationFunctionType.Relu
 TANH = mybir.ActivationFunctionType.Tanh
 
 P = 128
@@ -30,6 +32,9 @@ SPAN = PACK * RUN
 GZ_ROW = SPAN - RUN + 1
 W1_CALLS = [(0, 1), (1, 2), (2, 4), (4, 6), (6, 8)]
 W1_LOADS = [(0, 256), (256, 256), (512, 512)]
+NEGATED = (6, 7)
+ADDED = [(6, 1), (7, 0), (7, 1)]
+GAIN = 256
 CHUNKS = [(0, 256), (256, 128), (384, 128)]
 
 
@@ -41,6 +46,7 @@ def tile_list_code_pair_match_kernel(
         keep = ctx.enter_context(tc.tile_pool(name="keep", bufs=1))
         ring = ctx.enter_context(tc.tile_pool(name="ring", bufs=3))
         picks = ctx.enter_context(tc.tile_pool(name="picks", bufs=5))
+        gains = ctx.enter_context(tc.tile_pool(name="gains", bufs=2))
         psum_a = ctx.enter_context(tc.psum_pool(name="psum_a", bufs=3))
         psum_b = ctx.enter_context(tc.psum_pool(name="psum_b", bufs=1))
         psum_y = ctx.enter_context(tc.psum_pool(name="psum_y", bufs=3))
@@ -80,11 +86,11 @@ def tile_list_code_pair_match_kernel(
         load_w1(0)
         load_scale_rows(w4s_raw, w4_scales[0])
         load_w1(1)
-        nc.sync.dma_start(pos1_sb[:], pos1)
-        nc.sync.dma_start(pos2_sb[:], pos2)
         gz_runs = gz.rearrange("(g u s) -> u g s", g=GROUPS, s=SPAN)
         for e in range(RUN):
             nc.sync.dma_start(gz_sb[e:P:RUN, :, :], gz_runs[:, :, e : e + GZ_ROW])
+        nc.sync.dma_start(pos1_sb[:], pos1)
+        nc.sync.dma_start(pos2_sb[:], pos2)
         load_w1(2)
         w2_rows = w2.rearrange("(g u t e) n -> g e u t n", g=GROUPS, t=PACK, e=RUN)
         w2_raw = []
@@ -137,6 +143,7 @@ def tile_list_code_pair_match_kernel(
                 staged[:, slot, m0 : m0 + count // PACK, :].rearrange("p (u e) j -> p u j e", e=RUN),
                 w1_raw[i][:].rearrange("p j (u t e) -> p t u j e", t=PACK, e=RUN)[:, t],
                 COPY,
+                scale=-1.0 if g * PACK + t in NEGATED else 1.0,
             )
 
         def quantize(codes, scales, src, first, count):
@@ -161,10 +168,10 @@ def tile_list_code_pair_match_kernel(
                 src.rearrange("p t (c i) -> p c t i", i=4),
             )
 
-        def cast_w2(g):
-            for first in range(0, N, P):
-                dst = w2_bf[:, g * N + first : g * N + first + P, :]
-                interleave(nc.scalar.copy, dst, w2_raw[g][:, :, first : first + P])
+        def cast_w2(i):
+            g, n = divmod(i, N_TILES)
+            dst = w2_bf[:, i * P : (i + 1) * P, :]
+            interleave(nc.scalar.copy, dst, w2_raw[g][:, :, n * P : (n + 1) * P])
 
         def quantize_w2(first, count):
             src = w2_bf[:, first : first + count, :].rearrange("p n j -> p (n j)")
@@ -195,25 +202,72 @@ def tile_list_code_pair_match_kernel(
                 stop=True,
             )
             nc.scalar.copy(h[c][:, cols], acc_b[:])
-            nc.vector.tensor_tensor(h[c][:, cols], acc_a[:], h[c][:, cols], MAX)
+            if c in NEGATED:
+                nc.vector.scalar_tensor_tensor(h[c][:, cols], acc_a[:], -1.0, h[c][:, cols], MULT, MAX)
+            else:
+                nc.vector.tensor_tensor(h[c][:, cols], acc_a[:], h[c][:, cols], MAX)
+
+        ident = keep.tile([P, P], F32, name="ident", align_bytes=64)
+        make_identity(nc, ident[:])
+
+        turned_parts = {}
+
+        def project_turned(c, half):
+            minus_a = psum_y.tile([P, PACK, P], F32, name="acc_y")
+            b_less_a = psum_y.tile([P, PACK, P], F32, name="acc_y")
+            w1_codes, w1_scales = w1_w[:, c * P : (c + 1) * P].bitcast(FP8X4), w1_s[:, c * P : (c + 1) * P]
+            w4_codes = w4_w[:].bitcast(U8)[:, 2 * c * P : 2 * (c + 1) * P].bitcast(FP4X4)
+            w4_scale = w4_s[:].bitcast(U8)[:, c * P : (c + 1) * P]
+
+            def turned(acc, j, codes, scales, start, stop):
+                nc.tensor.matmul_mx(
+                    out=acc[:, j, :],
+                    lhsT=v_w[half][:, j * P : (j + 1) * P].bitcast(FP8X4),
+                    lhsT_scale=v_s[:, half * BANK + j * P : half * BANK + (j + 1) * P],
+                    rhs=codes,
+                    rhs_scale=scales,
+                    start=start,
+                    stop=stop,
+                )
+
+            for j in range(PACK):
+                turned(minus_a, j, w1_codes, w1_scales, True, True)
+            for j in range(PACK):
+                turned(b_less_a, j, w1_codes, w1_scales, True, False)
+                turned(b_less_a, j, w4_codes, w4_scale, False, True)
+            tag = "z_zero" if (c, half) == ADDED[-1] else "parts%d" % ADDED.index((c, half))
+            parts = keep.tile([P, 2, PACK, P], F32, name="parts", tag=tag, align_bytes=64)
+            a_t, r_t = parts[:, 0], parts[:, 1]
+            nc.scalar.activation(a_t, minus_a[:], COPY, scale=-1.0)
+            nc.scalar.activation(r_t, b_less_a[:], RELU)
+            turned_parts[(c, half)] = (a_t, r_t)
+
+        def add_turned(c, half):
+            a_t, r_t = turned_parts[(c, half)]
+            total = psum_y.tile([P, PACK, P], F32, name="acc_y")
+            for j in range(PACK):
+                nc.tensor.matmul(total[:, j, :], a_t[:, j, :], ident[:], start=True, stop=False, is_transpose=True)
+                nc.tensor.matmul(total[:, j, :], r_t[:, j, :], ident[:], start=False, stop=True, is_transpose=True)
+            nc.scalar.copy(h[c][:, half * BANK : (half + 1) * BANK], total[:].rearrange("p j s -> p (j s)"))
 
         z_f = {(0, 0): keep.tile([P, PACK, PAIRS], F32, name="z_f0", align_bytes=64)}
-        for first, count in CHUNKS[:2]:
-            z_f[(1, first)] = keep.tile([P, PACK, count], F32, name="z_f1_%d" % first, align_bytes=64)
+        z_f[(1, 0)] = keep.tile([P, PACK, CHUNKS[0][1]], F32, name="z_f1", align_bytes=64)
         z_bf = {}
         z_w = [keep.tile([P, PAIRS], U32, name="z_w%d" % g, align_bytes=64) for g in range(GROUPS)]
         z_s = [keep.tile([P, PAIRS], U8, name="z_s%d" % g, align_bytes=64) for g in range(GROUPS)]
-        gain = [keep.tile([P, PAIRS], F32, name="gain%d" % c, align_bytes=64) for c in range(TILES)]
+        gain = {}
         query = {}
 
         def spread_gain(c, count):
             g, t = divmod(c, PACK)
-            nc.scalar.copy(gain[c][:, 0:count], gz_sb[:, g, RUN * t : RUN * t + 1].to_broadcast([P, count]))
+            gain[c] = gains.tile([P, count], F32, name="gain", align_bytes=64)
+            nc.scalar.copy(gain[c][:], gz_sb[:, g, RUN * t : RUN * t + 1].to_broadcast([P, count]))
 
         def pick_query(c, first, count):
             picked = picks.tile([P, count], F32, name="picked", align_bytes=64)
-            lst = pos1_sb[:, first // 16 : (first + count) // 16]
-            nc.vector.tensor_tensor(picked[:], h[c][:].indirect(lst), gain[c][:, 0:count], MULT)
+            for at in range(0, count, GAIN):
+                lst = pos1_sb[:, (first + at) // 16 : (first + at + GAIN) // 16]
+                nc.vector.tensor_tensor(picked[:, at : at + GAIN], h[c][:].indirect(lst), gain[c][:], MULT)
             for at in range(0, count, P):
                 query[(c, first + at)] = (picked, at)
 
@@ -286,26 +340,35 @@ def tile_list_code_pair_match_kernel(
         first_c, second_c, third_c = CHUNKS
         for c in range(TILES - 2):
             chunk = (0, PAIRS) if c < PACK else first_c
-            spread_gain(c, PAIRS)
+            spread_gain(c, GAIN)
             pick_query(c, 0, PAIRS)
-            encode(c + 2, 0)
+            if (c + 2, 0) not in ADDED:
+                encode(c + 2, 0)
             pick_candidate(c, *chunk)
-            encode(c + 2, 1)
+            if (c + 2, 1) not in ADDED:
+                encode(c + 2, 1)
             if c < 2:
-                cast_w1(2, 2 * c)
-                cast_w1(2, 2 * c + 1)
-                quantize_w1(3 + c)
-            if c in (1, 2):
-                cast_w2(c - 1)
-            if c == 3:
-                quantize_w2(0, 512)
-                quantize_w2(512, 256)
-                for first in range(0, PAIRS, P):
-                    round_z(nc.scalar.copy, 0, first, P)
+                cast_w1(2, 2 - 2 * c)
+                cast_w1(2, 3 - 2 * c)
+                quantize_w1(4 - c)
+            if 2 <= c <= len(ADDED) + 1:
+                add_turned(*ADDED[c - 2])
+            if 1 <= c <= len(ADDED):
+                project_turned(*ADDED[c - 1])
             if c == 5:
-                quantize_z(0, 0, PAIRS)
-        spread_gain(6, PAIRS)
-        spread_gain(7, PAIRS)
+                spread_gain(6, GAIN)
+            for i in {3: [0], 4: [1, 2], 5: [3, 4, 5]}.get(c, []):
+                cast_w2(i)
+        spread_gain(7, GAIN)
+        for first in range(0, PAIRS, P):
+            round_z(nc.scalar.copy, 0, first, P)
+        pick_query(6, 0, PAIRS)
+        pick_query(7, 0, PAIRS)
+        quantize_w2(0, 512)
+        quantize_w2(512, 256)
+        pick_candidate(6, *first_c)
+        pick_candidate(7, *first_c)
+        quantize_z(0, 0, PAIRS)
         y_pair = psum_y.tile([P, 2, first_c[1]], F32, name="acc_y")
         y_lone = psum_y.tile([P, first_c[1]], F32, name="acc_y")
         y_first = [y_pair[:, 0, :], y_lone[:], y_pair[:, 1, :]]
@@ -325,11 +388,8 @@ def tile_list_code_pair_match_kernel(
             score_pass(0, n, *second_c, y_second[n])
         for n in range(N_TILES):
             score_pass(0, n, *third_c, y_third[n])
-        pick_query(6, 0, PAIRS)
-        pick_query(7, 0, PAIRS)
-        pick_candidate(6, *first_c)
-        pick_candidate(7, *first_c)
         round_z(nc.scalar.copy, 1, *first_c)
+        z_f[(1, second_c[0])] = keep.tile([P, PACK, second_c[1]], F32, name="z_f1_next", tag="z_zero", align_bytes=64)
         for c in range(PACK, TILES):
             pick_candidate(c, *second_c)
         round_z(nc.scalar.copy, 1, *second_c)

@@ -34,7 +34,7 @@ W1_CALLS = [(0, 1), (1, 2), (2, 4), (4, 6), (6, 8)]
 W1_LOADS = [(0, 256), (256, 256), (512, 512)]
 NEGATED = (6, 7)
 ADDED = [(6, 1), (7, 0), (7, 1)]
-GAIN = 256
+EARLY_GAINS = 6
 CHUNKS = [(0, 256), (256, 128), (384, 128)]
 
 
@@ -46,7 +46,6 @@ def tile_list_code_pair_match_kernel(
         keep = ctx.enter_context(tc.tile_pool(name="keep", bufs=1))
         ring = ctx.enter_context(tc.tile_pool(name="ring", bufs=3))
         picks = ctx.enter_context(tc.tile_pool(name="picks", bufs=5))
-        gains = ctx.enter_context(tc.tile_pool(name="gains", bufs=2))
         psum_a = ctx.enter_context(tc.psum_pool(name="psum_a", bufs=3))
         psum_b = ctx.enter_context(tc.psum_pool(name="psum_b", bufs=1))
         psum_y = ctx.enter_context(tc.psum_pool(name="psum_y", bufs=3))
@@ -56,7 +55,7 @@ def tile_list_code_pair_match_kernel(
         pos2_sb = keep.tile([P, PAIRS // 16], U16, name="pos2_sb")
         tab_w = keep.tile([P, T], I32, name="tab_w", align_bytes=64)
         tab_s = keep.tile([P, T // 4], I32, name="tab_s", align_bytes=64)
-        w4_raw = keep.tile([P, H // 2], I32, name="w4_raw", align_bytes=64)
+        w4_raw = [keep.tile([P, PASS // 2], I32, name="w4_raw%d" % g, align_bytes=64) for g in range(GROUPS)]
         w4s_raw = keep.tile([P, H // 4], I32, name="w4s_raw", tag="w4s_raw", align_bytes=64)
         w1_raw = [
             keep.tile([P, PACK, count], F32, name="w1_raw", tag="raw%d" % first, align_bytes=64)
@@ -67,6 +66,11 @@ def tile_list_code_pair_match_kernel(
 
         nc.vector.memset(tab_s[:], 0)
         nc.vector.memset(w4s_raw[:], 0)
+        ident = keep.tile([P, P], F32, name="ident", align_bytes=64)
+        nc.vector.memset(ident[:], 0.0)
+        warm = keep.tile([P, 1], F32, name="warm")
+        nc.scalar.activation(warm[:], ident[:, 0:1], TANH)
+        make_identity(nc, ident[:], nomemset=True)
 
         def load_scale_rows(plane, rows):
             by_r = rows.rearrange("(q r) c -> r q c", r=4)
@@ -79,24 +83,28 @@ def tile_list_code_pair_match_kernel(
             first, count = W1_LOADS[i]
             nc.sync.dma_start(w1_raw[i][:], w1_rows[:, :, first : first + count])
 
+        def load_w4(g):
+            nc.sync.dma_start(w4_raw[g][:], w4_words[0].bitcast(I32)[:, g * PASS // 2 : (g + 1) * PASS // 2])
+
         nc.sync.dma_start(offs_sb[:], offs)
-        nc.sync.dma_start(w4_raw[:], w4_words[0].bitcast(I32))
-        load_scale_rows(tab_s, tab_scales[0])
-        nc.sync.dma_start(tab_w[:], tab_words[0].rearrange("p t i -> p (t i)").bitcast(I32))
-        load_w1(0)
-        load_scale_rows(w4s_raw, w4_scales[0])
-        load_w1(1)
         gz_runs = gz.rearrange("(g u s) -> u g s", g=GROUPS, s=SPAN)
         for e in range(RUN):
             nc.sync.dma_start(gz_sb[e:P:RUN, :, :], gz_runs[:, :, e : e + GZ_ROW])
+        load_scale_rows(tab_s, tab_scales[0])
+        nc.sync.dma_start(tab_w[:], tab_words[0].rearrange("p t i -> p (t i)").bitcast(I32))
+        load_w4(0)
+        load_scale_rows(w4s_raw, w4_scales[0])
+        load_w1(0)
+        load_w1(1)
         nc.sync.dma_start(pos1_sb[:], pos1)
         nc.sync.dma_start(pos2_sb[:], pos2)
+        load_w4(1)
         load_w1(2)
         w2_rows = w2.rearrange("(g u t e) n -> g e u t n", g=GROUPS, t=PACK, e=RUN)
         w2_raw = []
 
         def load_w2(g):
-            w2_raw.append(keep.tile([P, PACK, N], F32, name="w2_raw", tag="raw%d" % W1_LOADS[g][0], align_bytes=64))
+            w2_raw.append(keep.tile([P, PACK, N], F32, name="w2_raw", tag=["raw0", "w1_bf0"][g], align_bytes=64))
             for e in range(RUN):
                 nc.scalar.dma_start(w2_raw[g][e:P:RUN, :, :], w2_rows[g, e])
 
@@ -117,11 +125,13 @@ def tile_list_code_pair_match_kernel(
         w4_w = keep.tile([P, H // 2], I32, name="w4_w", align_bytes=64)
         w4_s = keep.tile([P, H // 4], I32, name="w4_s", align_bytes=64)
 
-        def permute_w4():
+        def permute_w4_words(g):
             nc.vector.tensor_copy(
-                w4_w[:].rearrange("p (g t u) -> p g t u", g=GROUPS, t=PACK),
-                w4_raw[:].rearrange("p (g u t) -> p g t u", g=GROUPS, t=PACK),
+                w4_w[:, g * PASS // 2 : (g + 1) * PASS // 2].rearrange("p (t u) -> p t u", t=PACK),
+                w4_raw[g][:].rearrange("p (u t) -> p t u", t=PACK),
             )
+
+        def permute_w4_scales():
             nc.vector.tensor_copy(
                 w4_s[:].bitcast(U16).rearrange("p (g t u) -> p g t u", g=GROUPS, t=PACK),
                 w4s_raw[:].bitcast(U16).rearrange("p (g u t) -> p g t u", g=GROUPS, t=PACK),
@@ -177,9 +187,20 @@ def tile_list_code_pair_match_kernel(
             src = w2_bf[:, first : first + count, :].rearrange("p n j -> p (n j)")
             quantize(w2_w, w2_s, src, first, count)
 
-        h = [keep.tile([P, S], F32, name="h%d" % c, align_bytes=64) for c in range(TILES)]
+        maxed = [[half for half in range(2) if (c, half) not in ADDED] for c in range(TILES)] + [[]]
+        h = [
+            keep.tile([P, S + BANK * len(maxed[c + 1])], F32, name="h%d" % c, align_bytes=64) for c in range(TILES)
+        ]
+        b_first = []
 
-        def encode(c, half):
+        def b_staged(c, half):
+            if c == 0:
+                if not b_first:
+                    b_first.append(keep.tile([P, S], F32, name="b_first", tag="raw%d" % W1_LOADS[1][0], align_bytes=64))
+                return b_first[0][:, half * BANK : (half + 1) * BANK]
+            return h[c - 1][:, S + half * BANK : S + (half + 1) * BANK]
+
+        def project_w4(c, half):
             cols = slice(half * BANK, (half + 1) * BANK)
             acc_b = psum_b.tile([P, BANK], F32, name="acc_b", tag="acc_b%d" % half)
             nc.tensor.matmul_mx(
@@ -191,6 +212,10 @@ def tile_list_code_pair_match_kernel(
                 start=True,
                 stop=True,
             )
+            nc.scalar.copy(b_staged(c, half), acc_b[:])
+
+        def encode(c, half):
+            cols = slice(half * BANK, (half + 1) * BANK)
             acc_a = psum_a.tile([P, BANK], F32, name="acc_a")
             nc.tensor.matmul_mx(
                 out=acc_a[:],
@@ -201,14 +226,10 @@ def tile_list_code_pair_match_kernel(
                 start=True,
                 stop=True,
             )
-            nc.scalar.copy(h[c][:, cols], acc_b[:])
             if c in NEGATED:
-                nc.vector.scalar_tensor_tensor(h[c][:, cols], acc_a[:], -1.0, h[c][:, cols], MULT, MAX)
+                nc.vector.scalar_tensor_tensor(h[c][:, cols], acc_a[:], -1.0, b_staged(c, half), MULT, MAX)
             else:
-                nc.vector.tensor_tensor(h[c][:, cols], acc_a[:], h[c][:, cols], MAX)
-
-        ident = keep.tile([P, P], F32, name="ident", align_bytes=64)
-        make_identity(nc, ident[:])
+                nc.vector.tensor_tensor(h[c][:, cols], acc_a[:], b_staged(c, half), MAX)
 
         turned_parts = {}
 
@@ -260,14 +281,13 @@ def tile_list_code_pair_match_kernel(
 
         def spread_gain(c, count):
             g, t = divmod(c, PACK)
-            gain[c] = gains.tile([P, count], F32, name="gain", align_bytes=64)
+            gain[c] = keep.tile([P, PAIRS], F32, name="gain", tag="gain%d" % (c % EARLY_GAINS), align_bytes=64)
             nc.scalar.copy(gain[c][:], gz_sb[:, g, RUN * t : RUN * t + 1].to_broadcast([P, count]))
 
         def pick_query(c, first, count):
             picked = picks.tile([P, count], F32, name="picked", align_bytes=64)
-            for at in range(0, count, GAIN):
-                lst = pos1_sb[:, (first + at) // 16 : (first + at + GAIN) // 16]
-                nc.vector.tensor_tensor(picked[:, at : at + GAIN], h[c][:].indirect(lst), gain[c][:], MULT)
+            lst = pos1_sb[:, first // 16 : (first + count) // 16]
+            nc.vector.tensor_tensor(picked[:], h[c][:].indirect(lst), gain[c][:], MULT)
             for at in range(0, count, P):
                 query[(c, first + at)] = (picked, at)
 
@@ -323,30 +343,35 @@ def tile_list_code_pair_match_kernel(
 
         gather_scales()
         gather_words(0, "v_w0")
-        permute_w4()
-        gather_words(1, "v_w1")
+        permute_w4_words(0)
+        permute_w4_scales()
+        gather_words(1, "w4s_raw")
         for t in range(PACK):
             cast_w1(0, t)
             cast_w1(1, t)
+        quantize_w1(0)
         load_w2(0)
         load_w2(1)
-        quantize_w1(0)
         quantize_w1(1)
         quantize_w1(2)
-        encode(0, 0)
-        encode(0, 1)
-        encode(1, 0)
-        encode(1, 1)
+        for c, half in [(0, 0), (0, 1), (1, 0)]:
+            project_w4(c, half)
+            encode(c, half)
+        permute_w4_words(1)
+        for c in range(EARLY_GAINS):
+            spread_gain(c, PAIRS)
         first_c, second_c, third_c = CHUNKS
         for c in range(TILES - 2):
             chunk = (0, PAIRS) if c < PACK else first_c
-            spread_gain(c, GAIN)
+            if (c + 1, 1) not in ADDED:
+                project_w4(c + 1, 1)
             pick_query(c, 0, PAIRS)
-            if (c + 2, 0) not in ADDED:
-                encode(c + 2, 0)
+            if (c + 1, 1) not in ADDED:
+                encode(c + 1, 1)
             pick_candidate(c, *chunk)
-            if (c + 2, 1) not in ADDED:
-                encode(c + 2, 1)
+            if (c + 2, 0) not in ADDED:
+                project_w4(c + 2, 0)
+                encode(c + 2, 0)
             if c < 2:
                 cast_w1(2, 2 - 2 * c)
                 cast_w1(2, 3 - 2 * c)
@@ -355,11 +380,10 @@ def tile_list_code_pair_match_kernel(
                 add_turned(*ADDED[c - 2])
             if 1 <= c <= len(ADDED):
                 project_turned(*ADDED[c - 1])
-            if c == 5:
-                spread_gain(6, GAIN)
-            for i in {3: [0], 4: [1, 2], 5: [3, 4, 5]}.get(c, []):
+            if c in (2, 3):
+                spread_gain(EARLY_GAINS + c - 2, PAIRS)
+            for i in {2: [0], 3: [1], 4: [2, 3], 5: [4, 5]}.get(c, []):
                 cast_w2(i)
-        spread_gain(7, GAIN)
         for first in range(0, PAIRS, P):
             round_z(nc.scalar.copy, 0, first, P)
         pick_query(6, 0, PAIRS)

@@ -33,8 +33,9 @@ GZ_ROW = SPAN - RUN + 1
 W1_CALLS = [(0, 1), (1, 2), (2, 4), (4, 6), (6, 8)]
 W1_LOADS = [(0, 256), (256, 256), (512, 512)]
 NEGATED = (6, 7)
-ADDED = [(6, 1), (7, 0), (7, 1)]
-EARLY_GAINS = 6
+ADDED = [(6, 0), (6, 1), (7, 0), (7, 1)]
+MAXED = {(6, 0): P, (6, 1): 0, (7, 0): 0, (7, 1): 0}
+SCALAR_GAINS = 6
 CHUNKS = [(0, 256), (256, 128), (384, 128)]
 
 
@@ -104,10 +105,12 @@ def tile_list_code_pair_match_kernel(
         w2_raw = []
 
         def load_w2(g):
-            w2_raw.append(keep.tile([P, PACK, N], F32, name="w2_raw", tag=["raw0", "w1_bf0"][g], align_bytes=64))
+            w2_raw.append(keep.tile([P, PACK, N], F32, name="w2_raw", tag="w2_raw%d" % g, align_bytes=64))
             for e in range(RUN):
-                nc.scalar.dma_start(w2_raw[g][e:P:RUN, :, :], w2_rows[g, e])
+                nc.sync.dma_start(w2_raw[g][e:P:RUN, :, :], w2_rows[g, e])
 
+        load_w2(0)
+        load_w2(1)
         with nc.allow_non_contiguous_dma(reason="one bias value to a partition"):
             nc.sync.dma_start(b2_sb[:], b2.rearrange("(c p) -> p c", p=P))
 
@@ -187,9 +190,12 @@ def tile_list_code_pair_match_kernel(
             src = w2_bf[:, first : first + count, :].rearrange("p n j -> p (n j)")
             quantize(w2_w, w2_s, src, first, count)
 
-        maxed = [[half for half in range(2) if (c, half) not in ADDED] for c in range(TILES)] + [[]]
+        def maxed(c, half):
+            return MAXED.get((c, half), BANK) if c < TILES else 0
+
         h = [
-            keep.tile([P, S + BANK * len(maxed[c + 1])], F32, name="h%d" % c, align_bytes=64) for c in range(TILES)
+            keep.tile([P, S + maxed(c + 1, 0) + maxed(c + 1, 1)], F32, name="h%d" % c, align_bytes=64)
+            for c in range(TILES)
         ]
         b_first = []
 
@@ -198,16 +204,17 @@ def tile_list_code_pair_match_kernel(
                 if not b_first:
                     b_first.append(keep.tile([P, S], F32, name="b_first", tag="raw%d" % W1_LOADS[1][0], align_bytes=64))
                 return b_first[0][:, half * BANK : (half + 1) * BANK]
-            return h[c - 1][:, S + half * BANK : S + (half + 1) * BANK]
+            return h[c - 1][:, S + half * BANK : S + half * BANK + maxed(c, half)]
 
         def project_w4(c, half):
-            cols = slice(half * BANK, (half + 1) * BANK)
-            acc_b = psum_b.tile([P, BANK], F32, name="acc_b", tag="acc_b%d" % half)
+            width = maxed(c, half)
+            cols = slice(half * BANK, half * BANK + width)
+            acc_b = psum_b.tile([P, width], F32, name="acc_b", tag="acc_b%d" % half)
             nc.tensor.matmul_mx(
                 out=acc_b[:],
                 lhsT=w4_w[:].bitcast(U8)[:, 2 * c * P : 2 * (c + 1) * P].bitcast(FP4X4),
                 lhsT_scale=w4_s[:].bitcast(U8)[:, c * P : (c + 1) * P],
-                rhs=v_w[half][:].bitcast(FP8X4),
+                rhs=v_w[half][:, 0:width].bitcast(FP8X4),
                 rhs_scale=v_s[:, cols],
                 start=True,
                 stop=True,
@@ -215,13 +222,14 @@ def tile_list_code_pair_match_kernel(
             nc.scalar.copy(b_staged(c, half), acc_b[:])
 
         def encode(c, half):
-            cols = slice(half * BANK, (half + 1) * BANK)
-            acc_a = psum_a.tile([P, BANK], F32, name="acc_a")
+            width = maxed(c, half)
+            cols = slice(half * BANK, half * BANK + width)
+            acc_a = psum_a.tile([P, width], F32, name="acc_a")
             nc.tensor.matmul_mx(
                 out=acc_a[:],
                 lhsT=w1_w[:, c * P : (c + 1) * P].bitcast(FP8X4),
                 lhsT_scale=w1_s[:, c * P : (c + 1) * P],
-                rhs=v_w[half][:].bitcast(FP8X4),
+                rhs=v_w[half][:, 0:width].bitcast(FP8X4),
                 rhs_scale=v_s[:, cols],
                 start=True,
                 stop=True,
@@ -234,6 +242,7 @@ def tile_list_code_pair_match_kernel(
         turned_parts = {}
 
         def project_turned(c, half):
+            skip = maxed(c, half) // P
             minus_a = psum_y.tile([P, PACK, P], F32, name="acc_y")
             b_less_a = psum_y.tile([P, PACK, P], F32, name="acc_y")
             w1_codes, w1_scales = w1_w[:, c * P : (c + 1) * P].bitcast(FP8X4), w1_s[:, c * P : (c + 1) * P]
@@ -251,25 +260,26 @@ def tile_list_code_pair_match_kernel(
                     stop=stop,
                 )
 
-            for j in range(PACK):
+            for j in range(skip, PACK):
                 turned(minus_a, j, w1_codes, w1_scales, True, True)
-            for j in range(PACK):
+            for j in range(skip, PACK):
                 turned(b_less_a, j, w1_codes, w1_scales, True, False)
                 turned(b_less_a, j, w4_codes, w4_scale, False, True)
             tag = "z_zero" if (c, half) == ADDED[-1] else "parts%d" % ADDED.index((c, half))
             parts = keep.tile([P, 2, PACK, P], F32, name="parts", tag=tag, align_bytes=64)
             a_t, r_t = parts[:, 0], parts[:, 1]
-            nc.scalar.activation(a_t, minus_a[:], COPY, scale=-1.0)
-            nc.scalar.activation(r_t, b_less_a[:], RELU)
+            nc.scalar.activation(a_t[:, skip:], minus_a[:, skip:], COPY, scale=-1.0)
+            nc.scalar.activation(r_t[:, skip:], b_less_a[:, skip:], RELU)
             turned_parts[(c, half)] = (a_t, r_t)
 
         def add_turned(c, half):
             a_t, r_t = turned_parts[(c, half)]
+            skip = maxed(c, half) // P
             total = psum_y.tile([P, PACK, P], F32, name="acc_y")
-            for j in range(PACK):
+            for j in range(skip, PACK):
                 nc.tensor.matmul(total[:, j, :], a_t[:, j, :], ident[:], start=True, stop=False, is_transpose=True)
                 nc.tensor.matmul(total[:, j, :], r_t[:, j, :], ident[:], start=False, stop=True, is_transpose=True)
-            nc.scalar.copy(h[c][:, half * BANK : (half + 1) * BANK], total[:].rearrange("p j s -> p (j s)"))
+            nc.scalar.copy(h[c][:, half * BANK + skip * P : (half + 1) * BANK], total[:, skip:].rearrange("p j s -> p (j s)"))
 
         z_f = {(0, 0): keep.tile([P, PACK, PAIRS], F32, name="z_f0", align_bytes=64)}
         z_f[(1, 0)] = keep.tile([P, PACK, CHUNKS[0][1]], F32, name="z_f1", align_bytes=64)
@@ -281,8 +291,9 @@ def tile_list_code_pair_match_kernel(
 
         def spread_gain(c, count):
             g, t = divmod(c, PACK)
-            gain[c] = keep.tile([P, PAIRS], F32, name="gain", tag="gain%d" % (c % EARLY_GAINS), align_bytes=64)
-            nc.scalar.copy(gain[c][:], gz_sb[:, g, RUN * t : RUN * t + 1].to_broadcast([P, count]))
+            gain[c] = keep.tile([P, PAIRS], F32, name="gain", tag="gain%d" % c, align_bytes=64)
+            copy = nc.scalar.copy if c < SCALAR_GAINS else nc.vector.tensor_copy
+            copy(gain[c][:], gz_sb[:, g, RUN * t : RUN * t + 1].to_broadcast([P, count]))
 
         def pick_query(c, first, count):
             picked = picks.tile([P, count], F32, name="picked", align_bytes=64)
@@ -350,40 +361,37 @@ def tile_list_code_pair_match_kernel(
             cast_w1(0, t)
             cast_w1(1, t)
         quantize_w1(0)
-        load_w2(0)
-        load_w2(1)
         quantize_w1(1)
         quantize_w1(2)
         for c, half in [(0, 0), (0, 1), (1, 0)]:
             project_w4(c, half)
             encode(c, half)
         permute_w4_words(1)
-        for c in range(EARLY_GAINS):
+        for c in range(TILES):
             spread_gain(c, PAIRS)
         first_c, second_c, third_c = CHUNKS
         for c in range(TILES - 2):
             chunk = (0, PAIRS) if c < PACK else first_c
-            if (c + 1, 1) not in ADDED:
+            if maxed(c + 1, 1):
                 project_w4(c + 1, 1)
             pick_query(c, 0, PAIRS)
-            if (c + 1, 1) not in ADDED:
+            if maxed(c + 1, 1):
                 encode(c + 1, 1)
             pick_candidate(c, *chunk)
-            if (c + 2, 0) not in ADDED:
+            if maxed(c + 2, 0):
                 project_w4(c + 2, 0)
                 encode(c + 2, 0)
             if c < 2:
                 cast_w1(2, 2 - 2 * c)
                 cast_w1(2, 3 - 2 * c)
                 quantize_w1(4 - c)
-            if 2 <= c <= len(ADDED) + 1:
-                add_turned(*ADDED[c - 2])
             if 1 <= c <= len(ADDED):
-                project_turned(*ADDED[c - 1])
-            if c in (2, 3):
-                spread_gain(EARLY_GAINS + c - 2, PAIRS)
-            for i in {2: [0], 3: [1], 4: [2, 3], 5: [4, 5]}.get(c, []):
-                cast_w2(i)
+                add_turned(*ADDED[c - 1])
+            if c < len(ADDED):
+                project_turned(*ADDED[c])
+            if c >= PACK:
+                for n in range(N_TILES):
+                    cast_w2((c - PACK) * N_TILES + n)
         for first in range(0, PAIRS, P):
             round_z(nc.scalar.copy, 0, first, P)
         pick_query(6, 0, PAIRS)

@@ -68,9 +68,9 @@ def tile_list_code_pair_match_kernel(
         nc.vector.memset(tab_s[:], 0)
         nc.vector.memset(w4s_raw[:], 0)
         ident = keep.tile([P, P], F32, name="ident", align_bytes=64)
-        nc.vector.memset(ident[:], 0.0)
-        warm = keep.tile([P, 1], F32, name="warm")
-        nc.scalar.activation(warm[:], ident[:, 0:1], TANH)
+        zero = keep.tile([P, 1], F32, name="zero")
+        nc.vector.memset(zero[:], 0.0)
+        nc.scalar.activation(ident[:], zero[:].to_broadcast([P, P]), COPY)
         make_identity(nc, ident[:], nomemset=True)
 
         def load_scale_rows(plane, rows):
@@ -428,11 +428,10 @@ def tile_list_code_pair_match_kernel(
         quantize_z(1, *first_c)
         score(*first_c, y_first, [2])
         z_f[(1, third_c[0])] = keep.tile([P, PACK, third_c[1]], F32, name="z_f1_last", tag="z_first", align_bytes=64)
-        for c in range(PACK, TILES - 1):
+        for c in range(PACK, TILES):
             pick_candidate(c, *third_c)
         quantize_z(1, *second_c)
         score(*second_c, y_second, [])
-        pick_candidate(7, *third_c)
         round_z(nc.vector.tensor_copy, 1, *third_c)
         quantize_z(1, *third_c)
         score(*third_c, y_third, [])

@@ -193,23 +193,23 @@ def tile_list_code_pair_match_kernel(
         def maxed(c, half):
             return MAXED.get((c, half), BANK) if c < TILES else 0
 
-        h = [
-            keep.tile([P, S + maxed(c + 1, 0) + maxed(c + 1, 1)], F32, name="h%d" % c, align_bytes=64)
-            for c in range(TILES)
-        ]
-        b_first = []
+        h = {
+            c: keep.tile([P, S + maxed(c + 1, 0) + maxed(c + 1, 1)], F32, name="h%d" % c, align_bytes=64)
+            for c in range(1, TILES)
+        }
 
         def b_staged(c, half):
             if c == 0:
-                if not b_first:
-                    b_first.append(keep.tile([P, S], F32, name="b_first", tag="raw%d" % W1_LOADS[1][0], align_bytes=64))
-                return b_first[0][:, half * BANK : (half + 1) * BANK]
+                return h[0][:, 2 * S + half * BANK : 2 * S + (half + 1) * BANK]
             return h[c - 1][:, S + half * BANK : S + half * BANK + maxed(c, half)]
 
         def project_w4(c, half):
             width = maxed(c, half)
             cols = slice(half * BANK, half * BANK + width)
-            acc_b = psum_b.tile([P, width], F32, name="acc_b", tag="acc_b%d" % half)
+            if c == 1:
+                acc_b = psum_y.tile([P, width], F32, name="acc_y")
+            else:
+                acc_b = psum_b.tile([P, width], F32, name="acc_b", tag="acc_b%d" % half)
             nc.tensor.matmul_mx(
                 out=acc_b[:],
                 lhsT=w4_w[:].bitcast(U8)[:, 2 * c * P : 2 * (c + 1) * P].bitcast(FP4X4),
@@ -281,8 +281,8 @@ def tile_list_code_pair_match_kernel(
                 nc.tensor.matmul(total[:, j, :], r_t[:, j, :], ident[:], start=False, stop=True, is_transpose=True)
             nc.scalar.copy(h[c][:, half * BANK + skip * P : (half + 1) * BANK], total[:, skip:].rearrange("p j s -> p (j s)"))
 
-        z_f = {(0, 0): keep.tile([P, PACK, PAIRS], F32, name="z_f0", align_bytes=64)}
-        z_f[(1, 0)] = keep.tile([P, PACK, CHUNKS[0][1]], F32, name="z_f1", align_bytes=64)
+        z_f = {(0, 0): keep.tile([P, PACK, PAIRS], F32, name="z_f0", tag="z_f0", align_bytes=64)}
+        z_f[(1, 0)] = keep.tile([P, PACK, CHUNKS[0][1]], F32, name="z_f1", tag="z_f1", align_bytes=64)
         z_bf = {}
         z_w = [keep.tile([P, PAIRS], U32, name="z_w%d" % g, align_bytes=64) for g in range(GROUPS)]
         z_s = [keep.tile([P, PAIRS], U8, name="z_s%d" % g, align_bytes=64) for g in range(GROUPS)]
@@ -296,7 +296,10 @@ def tile_list_code_pair_match_kernel(
             copy(gain[c][:], gz_sb[:, g, RUN * t : RUN * t + 1].to_broadcast([P, count]))
 
         def pick_query(c, first, count):
-            picked = picks.tile([P, count], F32, name="picked", align_bytes=64)
+            if c in (1, 2):
+                picked = keep.tile([P, count], F32, name="picked", tag="w1_bf%d" % (TILES - 2 * c), align_bytes=64)
+            else:
+                picked = picks.tile([P, count], F32, name="picked", align_bytes=64)
             lst = pos1_sb[:, first // 16 : (first + count) // 16]
             nc.vector.tensor_tensor(picked[:], h[c][:].indirect(lst), gain[c][:], MULT)
             for at in range(0, count, P):
@@ -363,6 +366,7 @@ def tile_list_code_pair_match_kernel(
         quantize_w1(0)
         quantize_w1(1)
         quantize_w1(2)
+        h[0] = keep.tile([P, 3 * S], F32, name="h0", tag="raw%d" % W1_LOADS[1][0], align_bytes=64)
         for c, half in [(0, 0), (0, 1), (1, 0)]:
             project_w4(c, half)
             encode(c, half)
@@ -421,13 +425,13 @@ def tile_list_code_pair_match_kernel(
         for n in range(N_TILES):
             score_pass(0, n, *third_c, y_third[n])
         round_z(nc.scalar.copy, 1, *first_c)
-        z_f[(1, second_c[0])] = keep.tile([P, PACK, second_c[1]], F32, name="z_f1_next", tag="z_zero", align_bytes=64)
+        z_f[(1, second_c[0])] = keep.tile([P, PACK, second_c[1]], F32, name="z_f1_next", tag="z_f0", align_bytes=64)
         for c in range(PACK, TILES):
             pick_candidate(c, *second_c)
         round_z(nc.scalar.copy, 1, *second_c)
         quantize_z(1, *first_c)
         score(*first_c, y_first, [2])
-        z_f[(1, third_c[0])] = keep.tile([P, PACK, third_c[1]], F32, name="z_f1_last", tag="z_first", align_bytes=64)
+        z_f[(1, third_c[0])] = keep.tile([P, PACK, third_c[1]], F32, name="z_f1_last", tag="z_f1", align_bytes=64)
         for c in range(PACK, TILES):
             pick_candidate(c, *third_c)
         quantize_z(1, *second_c)

@@ -73,10 +73,10 @@ def tile_list_code_pair_match_kernel(
         nc.scalar.activation(ident[:], zero[:].to_broadcast([P, P]), COPY)
         make_identity(nc, ident[:], nomemset=True)
 
-        def load_scale_rows(plane, rows):
+        def load_scale_rows(plane, rows, queues):
             by_r = rows.rearrange("(q r) c -> r q c", r=4)
             for r in range(4):
-                nc.sync.dma_start(plane[r:P:32, :], by_r[r].bitcast(I32))
+                queues[r].dma_start(plane[r:P:32, :], by_r[r].bitcast(I32))
 
         w1_rows = w1.rearrange("(p j) c -> p j c", j=PACK)
 
@@ -91,10 +91,10 @@ def tile_list_code_pair_match_kernel(
         gz_runs = gz.rearrange("(g u s) -> u g s", g=GROUPS, s=SPAN)
         for e in range(RUN):
             nc.sync.dma_start(gz_sb[e:P:RUN, :, :], gz_runs[:, :, e : e + GZ_ROW])
-        load_scale_rows(tab_s, tab_scales[0])
+        load_scale_rows(tab_s, tab_scales[0], [nc.sync] * 4)
         nc.sync.dma_start(tab_w[:], tab_words[0].rearrange("p t i -> p (t i)").bitcast(I32))
         load_w4(0)
-        load_scale_rows(w4s_raw, w4_scales[0])
+        load_scale_rows(w4s_raw, w4_scales[0], [nc.sync] * 4)
         load_w1(0)
         load_w1(1)
         nc.sync.dma_start(pos1_sb[:], pos1)
@@ -130,21 +130,27 @@ def tile_list_code_pair_match_kernel(
 
         def permute_w4_words(g):
             nc.vector.tensor_copy(
-                w4_w[:, g * PASS // 2 : (g + 1) * PASS // 2].rearrange("p (t u) -> p t u", t=PACK),
-                w4_raw[g][:].rearrange("p (u t) -> p t u", t=PACK),
+                w4_w[:, g * PASS // 2 : (g + 1) * PASS // 2].rearrange("p (t b u) -> p b t u", t=PACK, u=4),
+                w4_raw[g][:].rearrange("p (b u t) -> p b t u", t=PACK, u=4),
             )
 
         def permute_w4_scales():
             nc.vector.tensor_copy(
-                w4_s[:].bitcast(U16).rearrange("p (g t u) -> p g t u", g=GROUPS, t=PACK),
-                w4s_raw[:].bitcast(U16).rearrange("p (g u t) -> p g t u", g=GROUPS, t=PACK),
+                w4_s[:].bitcast(U16).rearrange("p (g t b u) -> p g b t u", g=GROUPS, t=PACK, u=8),
+                w4s_raw[:].bitcast(U16).rearrange("p (g b u t) -> p g b t u", g=GROUPS, t=PACK, u=8),
             )
 
         w1_bf = {}
-        for c0, c1 in W1_CALLS:
-            staged = keep.tile([P, c1 - c0, P, PACK], BF16, name="w1_bf", tag="w1_bf%d" % c0, align_bytes=64)
+
+        def stage_w1(i, tag):
+            c0, c1 = W1_CALLS[i]
+            staged = keep.tile([P, c1 - c0, P, PACK], BF16, name="w1_bf", tag=tag, align_bytes=64)
             for c in range(c0, c1):
                 w1_bf[c] = (staged, c - c0)
+
+        for i in (0, 1, 3, 4):
+            stage_w1(i, "w1_bf%d" % W1_CALLS[i][0])
+        third_front = keep.tile([P, P // 2, PACK], BF16, name="third_front", align_bytes=64)
         w1_w = keep.tile([P, H], U32, name="w1_w", align_bytes=64)
         w1_s = keep.tile([P, H], U8, name="w1_s", align_bytes=64)
 
@@ -158,6 +164,12 @@ def tile_list_code_pair_match_kernel(
                 COPY,
                 scale=-1.0 if g * PACK + t in NEGATED else 1.0,
             )
+
+        def planes(i, t):
+            return w1_raw[i][:].rearrange("p j (u t e) -> p t u j e", t=PACK, e=RUN)[:, t]
+
+        def by_pairs(staged):
+            return staged.rearrange("p (u e) j -> p u j e", e=RUN)
 
         def quantize(codes, scales, src, first, count):
             nc.vector.quantize_mx(
@@ -198,18 +210,22 @@ def tile_list_code_pair_match_kernel(
             for c in range(1, TILES)
         }
 
+        b_fourth = keep.tile([P, BANK], F32, name="b_fourth", align_bytes=64)
+
         def b_staged(c, half):
             if c == 0:
-                return h[0][:, 2 * S + half * BANK : 2 * S + (half + 1) * BANK]
+                return h[0][:, S + (half + 1) * BANK : S + (half + 2) * BANK]
+            if (c, half) == (1, 1):
+                return b_fourth[:]
             return h[c - 1][:, S + half * BANK : S + half * BANK + maxed(c, half)]
 
         def project_w4(c, half):
             width = maxed(c, half)
             cols = slice(half * BANK, half * BANK + width)
-            if c == 1:
+            if (c, half) == (1, 0):
                 acc_b = psum_y.tile([P, width], F32, name="acc_y")
             else:
-                acc_b = psum_b.tile([P, width], F32, name="acc_b", tag="acc_b%d" % half)
+                acc_b = psum_b.tile([P, width], F32, name="acc_b", tag="acc_b%d" % ((half + min(c, 1)) % 2))
             nc.tensor.matmul_mx(
                 out=acc_b[:],
                 lhsT=w4_w[:].bitcast(U8)[:, 2 * c * P : 2 * (c + 1) * P].bitcast(FP4X4),
@@ -360,13 +376,20 @@ def tile_list_code_pair_match_kernel(
         permute_w4_words(0)
         permute_w4_scales()
         gather_words(1, "w4s_raw")
-        for t in range(PACK):
+        for t in range(2):
             cast_w1(0, t)
             cast_w1(1, t)
+        nc.scalar.copy(by_pairs(third_front[:]), planes(0, 2))
         quantize_w1(0)
         quantize_w1(1)
-        quantize_w1(2)
-        h[0] = keep.tile([P, 3 * S], F32, name="h0", tag="raw%d" % W1_LOADS[1][0], align_bytes=64)
+        late = keep.tile([P, 3, P // 2, PACK], BF16, name="late", tag="w1_bf0", align_bytes=64)
+        nc.vector.tensor_copy(by_pairs(late[:, 0]), planes(1, 2))
+        nc.vector.tensor_copy(by_pairs(late[:, 1]), planes(0, 3))
+        nc.vector.tensor_copy(by_pairs(late[:, 2]), planes(1, 3))
+        quantize(w1_w, w1_s, third_front[:].rearrange("p m j -> p (m j)"), 2 * P, P // 2)
+        quantize(w1_w, w1_s, late[:, 0].rearrange("p m j -> p (m j)"), 2 * P + P // 2, P // 2)
+        quantize(w1_w, w1_s, late[:, 1:3].rearrange("p a m j -> p (a m j)"), 3 * P, P)
+        h[0] = keep.tile([P, 2 * S + BANK], F32, name="h0", tag="w1_bf1", align_bytes=64)
         for c, half in [(0, 0), (0, 1), (1, 0)]:
             project_w4(c, half)
             encode(c, half)

@@ -365,11 +365,8 @@ def tile_list_code_pair_match_kernel(
                 score_pass(1, n, first, count, accs[n])
             for n in order:
                 nc.scalar.activation(result[:, n, :], accs[n], TANH, bias=b2_sb[:, n : n + 1])
-                if first == CHUNKS[-1][0]:
-                    queue = nc.scalar if n == order[-1] else nc.sync
-                    queue.dma_start(out_rows[:, n, cols], result[:, n, :])
-            if first != CHUNKS[-1][0]:
-                nc.sync.dma_start(out_rows[:, :, cols], result[:])
+                queue = nc.scalar if first == CHUNKS[-1][0] and n == order[-1] else nc.sync
+                queue.dma_start(out_rows[:, n, cols], result[:, n, :])
 
         gather_scales()
         gather_words(0, "v_w0")
@@ -459,6 +456,11 @@ def tile_list_code_pair_match_kernel(
             pick_candidate(c, *third_c)
         quantize_z(1, *second_c)
         score(*second_c, y_second, [])
-        round_z(nc.vector.tensor_copy, 1, *third_c)
-        quantize_z(1, *third_c)
+        z_last = keep.tile([P, third_c[1], PACK], BF16, name="z_last", align_bytes=64)
+        halves = [slice(0, third_c[1] // 2), slice(third_c[1] // 2, third_c[1])]
+        for part in halves:
+            interleave(nc.vector.tensor_copy, z_last[:, part, :], z_f[(1, third_c[0])][:, :, part])
+        for part in halves:
+            src = z_last[:, part, :].rearrange("p n j -> p (n j)")
+            quantize(z_w[1], z_s[1], src, third_c[0] + part.start, part.stop - part.start)
         score(*third_c, y_third, [])

@@ -65,13 +65,9 @@ def tile_list_code_pair_match_kernel(
         gz_sb = keep.tile([P, GROUPS, GZ_ROW], F32, name="gz_sb")
         b2_sb = keep.tile([P, N_TILES], F32, name="b2_sb")
 
-        nc.vector.memset(tab_s[:], 0)
+        nc.vector.memset(tab_s[:, 0 : T // 8], 0)
+        nc.gpsimd.memset(tab_s[:, T // 8 :], 0)
         nc.vector.memset(w4s_raw[:], 0)
-        ident = keep.tile([P, P], F32, name="ident", align_bytes=64)
-        zero = keep.tile([P, 1], F32, name="zero")
-        nc.vector.memset(zero[:], 0.0)
-        nc.scalar.activation(ident[:], zero[:].to_broadcast([P, P]), COPY)
-        make_identity(nc, ident[:], nomemset=True)
 
         def load_scale_rows(plane, rows, queues):
             by_r = rows.rearrange("(q r) c -> r q c", r=4)
@@ -90,7 +86,7 @@ def tile_list_code_pair_match_kernel(
         nc.sync.dma_start(offs_sb[:], offs)
         gz_runs = gz.rearrange("(g u s) -> u g s", g=GROUPS, s=SPAN)
         for e in range(RUN):
-            nc.sync.dma_start(gz_sb[e:P:RUN, :, :], gz_runs[:, :, e : e + GZ_ROW])
+            nc.scalar.dma_start(gz_sb[e:P:RUN, :, :], gz_runs[:, :, e : e + GZ_ROW])
         load_scale_rows(tab_s, tab_scales[0], [nc.sync] * 4)
         nc.sync.dma_start(tab_w[:], tab_words[0].rearrange("p t i -> p (t i)").bitcast(I32))
         load_w4(0)
@@ -113,6 +109,12 @@ def tile_list_code_pair_match_kernel(
         load_w2(1)
         with nc.allow_non_contiguous_dma(reason="one bias value to a partition"):
             nc.sync.dma_start(b2_sb[:], b2.rearrange("(c p) -> p c", p=P))
+
+        ident = keep.tile([P, P], F32, name="ident", align_bytes=64)
+        zero = keep.tile([P, 1], F32, name="zero")
+        nc.vector.memset(zero[:], 0.0)
+        nc.scalar.activation(ident[:], zero[:].to_broadcast([P, P]), COPY)
+        make_identity(nc, ident[:], nomemset=True)
 
         v_w = {}
         v_s = keep.tile([P, S], U8, name="v_s", align_bytes=64)

@@ -36,6 +36,7 @@ NEGATED = (6, 7)
 ADDED = [(6, 0), (6, 1), (7, 0), (7, 1)]
 MAXED = {(6, 0): P, (6, 1): 0, (7, 0): 0, (7, 1): 0}
 SCALAR_GAINS = 6
+LATE_GAIN = 5
 CHUNKS = [(0, 256), (256, 128), (384, 128)]
 
 
@@ -130,16 +131,17 @@ def tile_list_code_pair_match_kernel(
         w4_w = keep.tile([P, H // 2], I32, name="w4_w", align_bytes=64)
         w4_s = keep.tile([P, H // 4], I32, name="w4_s", align_bytes=64)
 
-        def permute_w4_words(g):
-            nc.vector.tensor_copy(
-                w4_w[:, g * PASS // 2 : (g + 1) * PASS // 2].rearrange("p (t b u) -> p b t u", t=PACK, u=4),
-                w4_raw[g][:].rearrange("p (b u t) -> p b t u", t=PACK, u=4),
+        def permute_w4_words(copy, g):
+            copy(
+                w4_w[:, g * PASS // 2 : (g + 1) * PASS // 2].bitcast(U32).rearrange("p (t b u) -> p b t u", t=PACK, u=4),
+                w4_raw[g][:].bitcast(U32).rearrange("p (b u t) -> p b t u", t=PACK, u=4),
             )
 
-        def permute_w4_scales():
-            nc.vector.tensor_copy(
-                w4_s[:].bitcast(U16).rearrange("p (g t b u) -> p g b t u", g=GROUPS, t=PACK, u=8),
-                w4s_raw[:].bitcast(U16).rearrange("p (g b u t) -> p g b t u", g=GROUPS, t=PACK, u=8),
+        def permute_w4_scales(copy, g):
+            cols = slice(g * PASS // 4, (g + 1) * PASS // 4)
+            copy(
+                w4_s[:, cols].bitcast(U16).rearrange("p (t b u) -> p b t u", t=PACK, u=8),
+                w4s_raw[:, cols].bitcast(U16).rearrange("p (b u t) -> p b t u", t=PACK, u=8),
             )
 
         w1_bf = {}
@@ -152,7 +154,6 @@ def tile_list_code_pair_match_kernel(
 
         for i in (0, 1, 3, 4):
             stage_w1(i, "w1_bf%d" % W1_CALLS[i][0])
-        third_front = keep.tile([P, P // 2, PACK], BF16, name="third_front", align_bytes=64)
         w1_w = keep.tile([P, H], U32, name="w1_w", align_bytes=64)
         w1_s = keep.tile([P, H], U8, name="w1_s", align_bytes=64)
 
@@ -221,7 +222,7 @@ def tile_list_code_pair_match_kernel(
                 return b_fourth[:]
             return h[c - 1][:, S + half * BANK : S + half * BANK + maxed(c, half)]
 
-        def project_w4(c, half):
+        def multiply_w4(c, half):
             width = maxed(c, half)
             cols = slice(half * BANK, half * BANK + width)
             if (c, half) == (1, 0):
@@ -237,6 +238,11 @@ def tile_list_code_pair_match_kernel(
                 start=True,
                 stop=True,
             )
+            return acc_b
+
+        def project_w4(c, half, acc_b=None):
+            if acc_b is None:
+                acc_b = multiply_w4(c, half)
             nc.scalar.copy(b_staged(c, half), acc_b[:])
 
         def encode(c, half):
@@ -309,7 +315,7 @@ def tile_list_code_pair_match_kernel(
 
         def spread_gain(c, count):
             g, t = divmod(c, PACK)
-            gain[c] = keep.tile([P, PAIRS], F32, name="gain", tag="gain%d" % c, align_bytes=64)
+            gain[c] = keep.tile([P, PAIRS], F32, name="gain", tag="gain%d" % (0 if c == LATE_GAIN else c), align_bytes=64)
             copy = nc.scalar.copy if c < SCALAR_GAINS else nc.vector.tensor_copy
             copy(gain[c][:], gz_sb[:, g, RUN * t : RUN * t + 1].to_broadcast([P, count]))
 
@@ -370,31 +376,37 @@ def tile_list_code_pair_match_kernel(
                 queue = nc.scalar if first == CHUNKS[-1][0] and n == order[-1] else nc.sync
                 queue.dma_start(out_rows[:, n, cols], result[:, n, :])
 
+        for c in range(TILES):
+            if c != LATE_GAIN:
+                spread_gain(c, PAIRS)
         gather_scales()
         gather_words(0, "v_w0")
-        permute_w4_words(0)
-        permute_w4_scales()
-        gather_words(1, "w4s_raw")
-        for t in range(2):
-            cast_w1(0, t)
-            cast_w1(1, t)
-        nc.scalar.copy(by_pairs(third_front[:]), planes(0, 2))
+        gather_words(1, "v_w1")
+        permute_w4_words(nc.scalar.copy, 0)
+        permute_w4_scales(nc.scalar.copy, 0)
+        permute_w4_scales(nc.vector.tensor_copy, 1)
+        for i in range(2):
+            for t in range(2):
+                cast_w1(i, t)
+
+        def round_halves(i, tag):
+            staged = keep.tile([P, 2, P // 2, PACK], BF16, name="halves", tag=tag, align_bytes=64)
+            for t in (2, 3):
+                nc.vector.tensor_copy(by_pairs(staged[:, t - 2]), planes(i, t))
+            for t in (2, 3):
+                src = staged[:, t - 2].rearrange("p m j -> p (m j)")
+                quantize(w1_w, w1_s, src, t * P + i * P // 2, P // 2)
+
+        round_halves(0, "w1_front")
         quantize_w1(0)
         quantize_w1(1)
-        late = keep.tile([P, 3, P // 2, PACK], BF16, name="late", tag="w1_bf0", align_bytes=64)
-        nc.vector.tensor_copy(by_pairs(late[:, 0]), planes(1, 2))
-        nc.vector.tensor_copy(by_pairs(late[:, 1]), planes(0, 3))
-        nc.vector.tensor_copy(by_pairs(late[:, 2]), planes(1, 3))
-        quantize(w1_w, w1_s, third_front[:].rearrange("p m j -> p (m j)"), 2 * P, P // 2)
-        quantize(w1_w, w1_s, late[:, 0].rearrange("p m j -> p (m j)"), 2 * P + P // 2, P // 2)
-        quantize(w1_w, w1_s, late[:, 1:3].rearrange("p a m j -> p (a m j)"), 3 * P, P)
+        round_halves(1, "w1_bf0")
         h[0] = keep.tile([P, 2 * S + BANK], F32, name="h0", tag="w1_bf1", align_bytes=64)
+        early = {unit: multiply_w4(*unit) for unit in [(0, 0), (1, 0), (0, 1)]}
         for c, half in [(0, 0), (0, 1), (1, 0)]:
-            project_w4(c, half)
+            project_w4(c, half, early[(c, half)])
             encode(c, half)
-        permute_w4_words(1)
-        for c in range(TILES):
-            spread_gain(c, PAIRS)
+        permute_w4_words(nc.vector.tensor_copy, 1)
         first_c, second_c, third_c = CHUNKS
         for c in range(TILES - 2):
             chunk = (0, PAIRS) if c < PACK else first_c
@@ -407,6 +419,8 @@ def tile_list_code_pair_match_kernel(
             if maxed(c + 2, 0):
                 project_w4(c + 2, 0)
                 encode(c + 2, 0)
+            if c == LATE_GAIN - 1:
+                spread_gain(LATE_GAIN, PAIRS)
             if c < 2:
                 cast_w1(2, 2 - 2 * c)
                 cast_w1(2, 3 - 2 * c)

@@ -36,7 +36,6 @@ NEGATED = (6, 7)
 ADDED = [(6, 0), (6, 1), (7, 0), (7, 1)]
 MAXED = {(6, 0): P, (6, 1): 0, (7, 0): 0, (7, 1): 0}
 SCALAR_GAINS = 6
-LATE_GAIN = 5
 CHUNKS = [(0, 256), (256, 128), (384, 128)]
 
 
@@ -66,8 +65,7 @@ def tile_list_code_pair_match_kernel(
         gz_sb = keep.tile([P, GROUPS, GZ_ROW], F32, name="gz_sb")
         b2_sb = keep.tile([P, N_TILES], F32, name="b2_sb")
 
-        nc.vector.memset(tab_s[:, 0 : T // 8], 0)
-        nc.gpsimd.memset(tab_s[:, T // 8 :], 0)
+        nc.vector.memset(tab_s[:], 0)
         nc.vector.memset(w4s_raw[:], 0)
 
         def load_scale_rows(plane, rows, queues):
@@ -87,7 +85,7 @@ def tile_list_code_pair_match_kernel(
         nc.sync.dma_start(offs_sb[:], offs)
         gz_runs = gz.rearrange("(g u s) -> u g s", g=GROUPS, s=SPAN)
         for e in range(RUN):
-            nc.scalar.dma_start(gz_sb[e:P:RUN, :, :], gz_runs[:, :, e : e + GZ_ROW])
+            nc.sync.dma_start(gz_sb[e:P:RUN, :, :], gz_runs[:, :, e : e + GZ_ROW])
         load_scale_rows(tab_s, tab_scales[0], [nc.sync] * 4)
         nc.sync.dma_start(tab_w[:], tab_words[0].rearrange("p t i -> p (t i)").bitcast(I32))
         load_w4(0)
@@ -315,7 +313,7 @@ def tile_list_code_pair_match_kernel(
 
         def spread_gain(c, count):
             g, t = divmod(c, PACK)
-            gain[c] = keep.tile([P, PAIRS], F32, name="gain", tag="gain%d" % (0 if c == LATE_GAIN else c), align_bytes=64)
+            gain[c] = keep.tile([P, PAIRS], F32, name="gain", tag="gain%d" % c, align_bytes=64)
             copy = nc.scalar.copy if c < SCALAR_GAINS else nc.vector.tensor_copy
             copy(gain[c][:], gz_sb[:, g, RUN * t : RUN * t + 1].to_broadcast([P, count]))
 
@@ -377,8 +375,7 @@ def tile_list_code_pair_match_kernel(
                 queue.dma_start(out_rows[:, n, cols], result[:, n, :])
 
         for c in range(TILES):
-            if c != LATE_GAIN:
-                spread_gain(c, PAIRS)
+            spread_gain(c, PAIRS)
         gather_scales()
         gather_words(0, "v_w0")
         gather_words(1, "v_w1")
@@ -419,8 +416,6 @@ def tile_list_code_pair_match_kernel(
             if maxed(c + 2, 0):
                 project_w4(c + 2, 0)
                 encode(c + 2, 0)
-            if c == LATE_GAIN - 1:
-                spread_gain(LATE_GAIN, PAIRS)
             if c < 2:
                 cast_w1(2, 2 - 2 * c)
                 cast_w1(2, 3 - 2 * c)

@@ -34,7 +34,15 @@ W1_CALLS = [(0, 1), (1, 2), (2, 4), (4, 6), (6, 8)]
 W1_LOADS = [(0, 256), (256, 256), (512, 512)]
 NEGATED = (6, 7)
 ADDED = [(6, 0), (6, 1), (7, 0), (7, 1)]
-MAXED = {(6, 0): P, (6, 1): 0, (7, 0): 0, (7, 1): 0}
+TWICE = (5, 1)
+MAXED = {(5, 1): 0, (6, 0): P, (6, 1): 0, (7, 0): 0, (7, 1): 0}
+PAIRED = (1, 2, 3)
+LATE_ORDER = (4, 6, 7, 5)
+B_BANK = {(0, 0): 0, (0, 1): 1, (1, 0): 5, (1, 1): 0, (2, 0): 1, (6, 0): 5}
+A_BANK = {(0, 0): 2, (0, 1): 3, (1, 0): 4, (1, 1): 1, (2, 0): 0, (6, 0): 0}
+SUM_BANK = {(6, 0): 5, (6, 1): 0, (7, 0): 5, (7, 1): 1, (5, 1): 3}
+TURNED_BANKS = (6, 7, 4)
+FIRST_BANK = {step: 2 * (step % 2) for step in PAIRED}
 SCALAR_GAINS = 6
 CHUNKS = [(0, 256), (256, 128), (384, 128)]
 
@@ -47,9 +55,15 @@ def tile_list_code_pair_match_kernel(
         keep = ctx.enter_context(tc.tile_pool(name="keep", bufs=1))
         ring = ctx.enter_context(tc.tile_pool(name="ring", bufs=3))
         picks = ctx.enter_context(tc.tile_pool(name="picks", bufs=5))
-        psum_a = ctx.enter_context(tc.psum_pool(name="psum_a", bufs=3))
-        psum_b = ctx.enter_context(tc.psum_pool(name="psum_b", bufs=1))
-        psum_y = ctx.enter_context(tc.psum_pool(name="psum_y", bufs=3))
+        psum = ctx.enter_context(tc.psum_pool(name="psum", bufs=1))
+
+        b_bank, a_bank = dict(B_BANK), dict(A_BANK)
+        for step in PAIRED:
+            b_bank[(step + 1, 1)] = a_bank[(step + 2, 0)] = FIRST_BANK[step]
+            b_bank[(step + 2, 0)] = a_bank[(step + 1, 1)] = FIRST_BANK[step] + 1
+
+        def bank(number, shape):
+            return psum.tile([P] + shape, F32, name="bank", tag="bank%d" % number)
 
         offs_sb = keep.tile([P, S // 16], U16, name="offs_sb")
         pos1_sb = keep.tile([P, PAIRS // 16], U16, name="pos1_sb")
@@ -94,8 +108,8 @@ def tile_list_code_pair_match_kernel(
         load_w1(1)
         nc.sync.dma_start(pos1_sb[:], pos1)
         nc.sync.dma_start(pos2_sb[:], pos2)
-        load_w4(1)
         load_w1(2)
+        load_w4(1)
         w2_rows = w2.rearrange("(g u t e) n -> g e u t n", g=GROUPS, t=PACK, e=RUN)
         w2_raw = []
 
@@ -126,12 +140,17 @@ def tile_list_code_pair_match_kernel(
             lst = offs_sb[:, half * BANK // 16 : (half + 1) * BANK // 16]
             nc.vector.tensor_copy(v_w[half][:], tab_w[:].bitcast(U32).indirect(lst))
 
-        w4_w = keep.tile([P, H // 2], I32, name="w4_w", align_bytes=64)
+        w4_w = {}
         w4_s = keep.tile([P, H // 4], I32, name="w4_s", align_bytes=64)
 
-        def permute_w4_words(copy, g):
+        def w4_codes(c):
+            g, t = divmod(c, PACK)
+            return w4_w[g][:].bitcast(U8)[:, 2 * t * P : 2 * (t + 1) * P].bitcast(FP4X4)
+
+        def permute_w4_words(copy, g, tag):
+            w4_w[g] = keep.tile([P, PASS // 2], I32, name="w4_w", tag=tag, align_bytes=64)
             copy(
-                w4_w[:, g * PASS // 2 : (g + 1) * PASS // 2].bitcast(U32).rearrange("p (t b u) -> p b t u", t=PACK, u=4),
+                w4_w[g][:].bitcast(U32).rearrange("p (t b u) -> p b t u", t=PACK, u=4),
                 w4_raw[g][:].bitcast(U32).rearrange("p (b u t) -> p b t u", t=PACK, u=4),
             )
 
@@ -184,7 +203,6 @@ def tile_list_code_pair_match_kernel(
             src = w1_bf[c0][0][:].rearrange("p t m j -> p (t m j)")
             quantize(w1_w, w1_s, src, c0 * P, (c1 - c0) * P)
 
-        w2_bf = keep.tile([P, GROUPS * N, PACK], BF16, name="w2_bf", align_bytes=64)
         w2_w = keep.tile([P, GROUPS * N], U32, name="w2_w", align_bytes=64)
         w2_s = keep.tile([P, GROUPS * N], U8, name="w2_s", align_bytes=64)
 
@@ -194,42 +212,49 @@ def tile_list_code_pair_match_kernel(
                 src.rearrange("p t (c i) -> p c t i", i=4),
             )
 
-        def cast_w2(i):
-            g, n = divmod(i, N_TILES)
-            dst = w2_bf[:, i * P : (i + 1) * P, :]
-            interleave(nc.scalar.copy, dst, w2_raw[g][:, :, n * P : (n + 1) * P])
+        def round_w2_late(tag):
+            w2_bf = keep.tile([P, N - P, PACK], BF16, name="w2_bf", tag=tag, align_bytes=64)
+            interleave(nc.scalar.copy, w2_bf[:], w2_raw[1][:, :, P:N])
+            quantize(w2_w, w2_s, w2_bf[:].rearrange("p n j -> p (n j)"), N + P, N - P)
 
-        def quantize_w2(first, count):
-            src = w2_bf[:, first : first + count, :].rearrange("p n j -> p (n j)")
-            quantize(w2_w, w2_s, src, first, count)
+        w2_early = {}
+
+        def cast_w2_early(n, tag):
+            w2_early[n] = keep.tile([P, P, PACK], BF16, name="w2_early", tag=tag, align_bytes=64)
+            g, cols = n // N_TILES, slice(n % N_TILES * P, (n % N_TILES + 1) * P)
+            nc.gpsimd.tensor_copy(w2_early[n][:], w2_raw[g][:, :, cols].rearrange("p t n -> p n t"))
+
+        def quantize_w2_early(n):
+            quantize(w2_w, w2_s, w2_early[n][:].rearrange("p n j -> p (n j)"), n * P, P)
 
         def maxed(c, half):
             return MAXED.get((c, half), BANK) if c < TILES else 0
 
         h = {
-            c: keep.tile([P, S + maxed(c + 1, 0) + maxed(c + 1, 1)], F32, name="h%d" % c, align_bytes=64)
+            c: keep.tile([P, S + (2 * BANK if c in PAIRED else 0)], F32, name="h%d" % c, align_bytes=64)
             for c in range(1, TILES)
         }
 
-        b_fourth = keep.tile([P, BANK], F32, name="b_fourth", align_bytes=64)
+        b_apart = {
+            unit: keep.tile([P, maxed(*unit)], F32, name="b_apart", tag="b_apart%d" % unit[0], align_bytes=64)
+            for unit in [(1, 1), (2, 0), (6, 0)]
+        }
 
         def b_staged(c, half):
             if c == 0:
                 return h[0][:, S + (half + 1) * BANK : S + (half + 2) * BANK]
-            if (c, half) == (1, 1):
-                return b_fourth[:]
-            return h[c - 1][:, S + half * BANK : S + half * BANK + maxed(c, half)]
-
-        def multiply_w4(c, half):
-            width = maxed(c, half)
-            cols = slice(half * BANK, half * BANK + width)
             if (c, half) == (1, 0):
-                acc_b = psum_y.tile([P, width], F32, name="acc_y")
-            else:
-                acc_b = psum_b.tile([P, width], F32, name="acc_b", tag="acc_b%d" % ((half + min(c, 1)) % 2))
+                return h[0][:, S : S + BANK]
+            if (c, half) in b_apart:
+                return b_apart[(c, half)][:]
+            return h[c - 2 + half][:, S + half * BANK : S + (half + 1) * BANK]
+
+        def multiply_w4(c, half, number, width):
+            cols = slice(half * BANK, half * BANK + width)
+            acc_b = bank(number, [width])
             nc.tensor.matmul_mx(
                 out=acc_b[:],
-                lhsT=w4_w[:].bitcast(U8)[:, 2 * c * P : 2 * (c + 1) * P].bitcast(FP4X4),
+                lhsT=w4_codes(c),
                 lhsT_scale=w4_s[:].bitcast(U8)[:, c * P : (c + 1) * P],
                 rhs=v_w[half][:, 0:width].bitcast(FP8X4),
                 rhs_scale=v_s[:, cols],
@@ -240,13 +265,12 @@ def tile_list_code_pair_match_kernel(
 
         def project_w4(c, half, acc_b=None):
             if acc_b is None:
-                acc_b = multiply_w4(c, half)
+                acc_b = multiply_w4(c, half, b_bank[(c, half)], maxed(c, half))
             nc.scalar.copy(b_staged(c, half), acc_b[:])
 
-        def encode(c, half):
-            width = maxed(c, half)
+        def multiply_w1(c, half, number, width):
             cols = slice(half * BANK, half * BANK + width)
-            acc_a = psum_a.tile([P, width], F32, name="acc_a")
+            acc_a = bank(number, [width])
             nc.tensor.matmul_mx(
                 out=acc_a[:],
                 lhsT=w1_w[:, c * P : (c + 1) * P].bitcast(FP8X4),
@@ -256,19 +280,29 @@ def tile_list_code_pair_match_kernel(
                 start=True,
                 stop=True,
             )
+            return acc_a
+
+        def encode(c, half):
+            width = maxed(c, half)
+            cols = slice(half * BANK, half * BANK + width)
+            acc_a = multiply_w1(c, half, a_bank[(c, half)], width)
             if c in NEGATED:
                 nc.vector.scalar_tensor_tensor(h[c][:, cols], acc_a[:], -1.0, b_staged(c, half), MULT, MAX)
             else:
                 nc.vector.tensor_tensor(h[c][:, cols], acc_a[:], b_staged(c, half), MAX)
 
         turned_parts = {}
+        dealt = []
+
+        def next_bank():
+            dealt.append(TURNED_BANKS[len(dealt) % len(TURNED_BANKS)])
+            return dealt[-1]
 
         def project_turned(c, half):
             skip = maxed(c, half) // P
-            minus_a = psum_y.tile([P, PACK, P], F32, name="acc_y")
-            b_less_a = psum_y.tile([P, PACK, P], F32, name="acc_y")
+            minus_a = bank(next_bank(), [PACK, P])
+            b_less_a = bank(next_bank(), [PACK, P])
             w1_codes, w1_scales = w1_w[:, c * P : (c + 1) * P].bitcast(FP8X4), w1_s[:, c * P : (c + 1) * P]
-            w4_codes = w4_w[:].bitcast(U8)[:, 2 * c * P : 2 * (c + 1) * P].bitcast(FP4X4)
             w4_scale = w4_s[:].bitcast(U8)[:, c * P : (c + 1) * P]
 
             def turned(acc, j, codes, scales, start, stop):
@@ -286,24 +320,45 @@ def tile_list_code_pair_match_kernel(
                 turned(minus_a, j, w1_codes, w1_scales, True, True)
             for j in range(skip, PACK):
                 turned(b_less_a, j, w1_codes, w1_scales, True, False)
-                turned(b_less_a, j, w4_codes, w4_scale, False, True)
-            tag = "z_zero" if (c, half) == ADDED[-1] else "parts%d" % ADDED.index((c, half))
+                turned(b_less_a, j, w4_codes(c), w4_scale, False, True)
+            split_turned(c, half, minus_a, b_less_a, "parts%d" % ADDED.index((c, half)))
+
+        def split_turned(c, half, minus_a, b_less_a, tag):
+            skip = maxed(c, half) // P
             parts = keep.tile([P, 2, PACK, P], F32, name="parts", tag=tag, align_bytes=64)
             a_t, r_t = parts[:, 0], parts[:, 1]
             nc.scalar.activation(a_t[:, skip:], minus_a[:, skip:], COPY, scale=-1.0)
             nc.scalar.activation(r_t[:, skip:], b_less_a[:, skip:], RELU)
             turned_parts[(c, half)] = (a_t, r_t)
 
+        def project_both(c, half):
+            both = keep.tile([P, 2, PACK, P], F32, name="both", align_bytes=64)
+            acc_a = multiply_w1(c, half, next_bank(), BANK)
+            acc_b = multiply_w4(c, half, next_bank(), BANK)
+            nc.scalar.activation(both[:, 0].rearrange("p j s -> p (j s)"), acc_a[:], COPY, scale=-1.0)
+            nc.scalar.copy(both[:, 1].rearrange("p j s -> p (j s)"), acc_b[:])
+            return both
+
+        def turn_both(c, half, both):
+            minus_a = bank(next_bank(), [PACK, P])
+            b_less_a = bank(next_bank(), [PACK, P])
+            for j in range(PACK):
+                nc.tensor.matmul(minus_a[:, j, :], both[:, 0, j, :], ident[:], start=True, stop=True, is_transpose=True)
+            for j in range(PACK):
+                nc.tensor.matmul(b_less_a[:, j, :], both[:, 0, j, :], ident[:], start=True, stop=False, is_transpose=True)
+                nc.tensor.matmul(b_less_a[:, j, :], both[:, 1, j, :], ident[:], start=False, stop=True, is_transpose=True)
+            split_turned(c, half, minus_a, b_less_a, "parts_last")
+
         def add_turned(c, half):
             a_t, r_t = turned_parts[(c, half)]
             skip = maxed(c, half) // P
-            total = psum_y.tile([P, PACK, P], F32, name="acc_y")
+            total = bank(SUM_BANK[(c, half)], [PACK, P])
             for j in range(skip, PACK):
                 nc.tensor.matmul(total[:, j, :], a_t[:, j, :], ident[:], start=True, stop=False, is_transpose=True)
                 nc.tensor.matmul(total[:, j, :], r_t[:, j, :], ident[:], start=False, stop=True, is_transpose=True)
             nc.scalar.copy(h[c][:, half * BANK + skip * P : (half + 1) * BANK], total[:, skip:].rearrange("p j s -> p (j s)"))
 
-        z_f = {(0, 0): keep.tile([P, PACK, PAIRS], F32, name="z_f0", tag="z_f0", align_bytes=64)}
+        z_f = {}
         z_f[(1, 0)] = keep.tile([P, PACK, CHUNKS[0][1]], F32, name="z_f1", tag="z_f1", align_bytes=64)
         z_bf = {}
         z_w = [keep.tile([P, PAIRS], U32, name="z_w%d" % g, align_bytes=64) for g in range(GROUPS)]
@@ -319,11 +374,17 @@ def tile_list_code_pair_match_kernel(
 
         def pick_query(c, first, count):
             if c in (1, 2):
-                picked = keep.tile([P, count], F32, name="picked", tag="w1_bf%d" % (TILES - 2 * c), align_bytes=64)
+                picked = keep.tile([P, count], F32, name="picked", tag="w1_bf%d" % (TILES - 2 * c), align_bytes=64)[:]
+            elif c in (4, 6):
+                if c == 4:
+                    query["pair"] = keep.tile([P, 2, count], F32, name="picked_pair", tag="parts2", align_bytes=64)
+                picked = query["pair"][:, (c - 4) // 2, :]
+            elif c == 7:
+                picked = keep.tile([P, count], F32, name="picked", tag="parts_last", align_bytes=64)[:]
             else:
-                picked = picks.tile([P, count], F32, name="picked", align_bytes=64)
+                picked = picks.tile([P, count], F32, name="picked", align_bytes=64)[:]
             lst = pos1_sb[:, first // 16 : (first + count) // 16]
-            nc.vector.tensor_tensor(picked[:], h[c][:].indirect(lst), gain[c][:], MULT)
+            nc.vector.tensor_tensor(picked, h[c][:].indirect(lst), gain[c][:], MULT)
             for at in range(0, count, P):
                 query[(c, first + at)] = (picked, at)
 
@@ -333,14 +394,12 @@ def tile_list_code_pair_match_kernel(
             picked, at = query[(c, first)]
             nc.vector.tensor_tensor(z_f[(g, first)][:, t, :], h[c][:].indirect(lst), picked[:, at : at + count], MULT)
 
-        def round_z(copy, g, first, count):
-            base = first if g else 0
-            src = z_f[(g, base)][:, :, first - base : first - base + count]
-            if (g, base) not in z_bf:
-                tag = ["z_zero", "z_first" if first == 0 else "z_rest"][g]
-                width = count if g else PAIRS
-                z_bf[(g, base)] = keep.tile([P, width, PACK], BF16, name="z_bf", tag=tag, align_bytes=64)
-            interleave(copy, z_bf[(g, base)][:, first - base : first - base + count, :], src)
+        def stage_z(g, first, count, tag):
+            z_bf[(g, first)] = keep.tile([P, count, PACK], BF16, name="z_bf", tag=tag, align_bytes=64)
+
+        def round_z(g, first, count, products, staged):
+            src = z_f[(g, products)][:, :, first - products : first - products + count]
+            interleave(nc.scalar.copy, z_bf[(g, staged)][:, first - staged : first - staged + count, :], src)
 
         def quantize_z(g, first, count):
             src = z_bf[(g, first)][:].rearrange("p n j -> p (n j)")
@@ -379,7 +438,7 @@ def tile_list_code_pair_match_kernel(
         gather_scales()
         gather_words(0, "v_w0")
         gather_words(1, "v_w1")
-        permute_w4_words(nc.scalar.copy, 0)
+        permute_w4_words(nc.scalar.copy, 0, "w4_w0")
         permute_w4_scales(nc.scalar.copy, 0)
         permute_w4_scales(nc.vector.tensor_copy, 1)
         for i in range(2):
@@ -399,71 +458,87 @@ def tile_list_code_pair_match_kernel(
         quantize_w1(1)
         round_halves(1, "w1_bf0")
         h[0] = keep.tile([P, 2 * S + BANK], F32, name="h0", tag="w1_bf1", align_bytes=64)
-        early = {unit: multiply_w4(*unit) for unit in [(0, 0), (1, 0), (0, 1)]}
+        early = {unit: multiply_w4(*unit, b_bank[unit], BANK) for unit in [(0, 0), (1, 0), (0, 1)]}
         for c, half in [(0, 0), (0, 1), (1, 0)]:
             project_w4(c, half, early[(c, half)])
             encode(c, half)
-        permute_w4_words(nc.vector.tensor_copy, 1)
         first_c, second_c, third_c = CHUNKS
-        for c in range(TILES - 2):
-            chunk = (0, PAIRS) if c < PACK else first_c
-            if maxed(c + 1, 1):
-                project_w4(c + 1, 1)
+        staged, slot = w1_bf[5]
+        nc.gpsimd.tensor_copy(
+            staged[:, slot].rearrange("p (u e) j -> p u e j", e=RUN),
+            w1_raw[2][:].rearrange("p j (u t e) -> p t u e j", t=PACK, e=RUN)[:, 1],
+        )
+        permute_w4_words(nc.gpsimd.tensor_copy, 1, "w4_w1")
+        project_w4(1, 1)
+        project_w4(2, 0)
+        pick_query(0, 0, PAIRS)
+        cast_w2_early(0, "gain0")
+        encode(2, 0)
+        encode(1, 1)
+        z_f[(0, 0)] = keep.tile([P, PACK, PAIRS], F32, name="z_f0", tag="b_apart2", align_bytes=64)
+        pick_candidate(0, 0, PAIRS)
+        quantize_w2_early(0)
+        for c in PAIRED:
+            project_w4(c + 1, 1)
+            project_w4(c + 2, 0)
+            if c < 3:
+                for t in [(2, 3), (0,)][c - 1]:
+                    cast_w1(2, t)
+                quantize_w1(5 - c)
             pick_query(c, 0, PAIRS)
-            if maxed(c + 1, 1):
-                encode(c + 1, 1)
-            pick_candidate(c, *chunk)
-            if maxed(c + 2, 0):
-                project_w4(c + 2, 0)
-                encode(c + 2, 0)
-            if c < 2:
-                cast_w1(2, 2 - 2 * c)
-                cast_w1(2, 3 - 2 * c)
-                quantize_w1(4 - c)
-            if 1 <= c <= len(ADDED):
-                add_turned(*ADDED[c - 1])
-            if c < len(ADDED):
-                project_turned(*ADDED[c])
-            if c >= PACK:
-                for n in range(N_TILES):
-                    cast_w2((c - PACK) * N_TILES + n)
-        for first in range(0, PAIRS, P):
-            round_z(nc.scalar.copy, 0, first, P)
+            cast_w2_early(c, "gain%d" % c)
+            encode(c + 2, 0)
+            encode(c + 1, 1)
+            pick_candidate(c, 0, PAIRS)
+            quantize_w2_early(c)
+            if c > 1:
+                add_turned(*ADDED[c - 2])
+            if c == 2:
+                project_w4(6, 0)
+            project_turned(*ADDED[c - 1])
+        encode(6, 0)
+        both = project_both(*TWICE)
+        add_turned(*ADDED[2])
+        pick_query(4, 0, PAIRS)
         pick_query(6, 0, PAIRS)
-        pick_query(7, 0, PAIRS)
-        quantize_w2(0, 512)
-        quantize_w2(512, 256)
+        pick_candidate(4, *first_c)
         pick_candidate(6, *first_c)
+        project_turned(*ADDED[3])
+        turn_both(*TWICE, both)
+        add_turned(*ADDED[3])
+        add_turned(*TWICE)
+        pick_query(7, 0, PAIRS)
+        pick_query(5, 0, PAIRS)
         pick_candidate(7, *first_c)
+        pick_candidate(5, *first_c)
+        round_w2_late("parts3")
+        stage_z(0, 0, PAIRS, "gain7")
+        for first in range(0, PAIRS, 2 * P):
+            round_z(0, first, 2 * P, 0, 0)
         quantize_z(0, 0, PAIRS)
-        y_pair = psum_y.tile([P, 2, first_c[1]], F32, name="acc_y")
-        y_lone = psum_y.tile([P, first_c[1]], F32, name="acc_y")
+        z_f[(1, second_c[0])] = keep.tile([P, PACK, second_c[1]], F32, name="z_f1_next", tag="b_apart2", align_bytes=64)
+        for c in LATE_ORDER:
+            pick_candidate(c, *second_c)
+        stage_z(1, *first_c, "z_first")
+        round_z(1, *first_c, first_c[0], first_c[0])
+        quantize_z(1, *first_c)
+        y_pair = bank(5, [2, first_c[1]])
+        y_lone = bank(6, [first_c[1]])
         y_first = [y_pair[:, 0, :], y_lone[:], y_pair[:, 1, :]]
-        y_rest = [
-            psum_y.tile([P, P], F32, name="acc_y"),
-            psum_b.tile([P, P], F32, name="acc_y", tag="acc_b0"),
-            psum_b.tile([P, P], F32, name="acc_y", tag="acc_b1"),
-            psum_a.tile([P, P], F32, name="acc_a"),
-            psum_a.tile([P, P], F32, name="acc_a"),
-            psum_a.tile([P, P], F32, name="acc_a"),
-        ]
+        y_rest = [bank(number, [P]) for number in (2, 0, 1, 7, 4, 3)]
         y_second = [acc[:] for acc in y_rest[:N_TILES]]
         y_third = [acc[:] for acc in y_rest[N_TILES:]]
         for n in range(2):
             score_pass(0, n, *first_c, y_first[n])
+        score(*first_c, y_first, [2])
         for n in range(N_TILES):
             score_pass(0, n, *second_c, y_second[n])
         for n in range(N_TILES):
             score_pass(0, n, *third_c, y_third[n])
-        round_z(nc.scalar.copy, 1, *first_c)
-        z_f[(1, second_c[0])] = keep.tile([P, PACK, second_c[1]], F32, name="z_f1_next", tag="z_f0", align_bytes=64)
-        for c in range(PACK, TILES):
-            pick_candidate(c, *second_c)
-        round_z(nc.scalar.copy, 1, *second_c)
-        quantize_z(1, *first_c)
-        score(*first_c, y_first, [2])
+        stage_z(1, *second_c, "z_rest")
+        round_z(1, *second_c, second_c[0], second_c[0])
         z_f[(1, third_c[0])] = keep.tile([P, PACK, third_c[1]], F32, name="z_f1_last", tag="z_f1", align_bytes=64)
-        for c in range(PACK, TILES):
+        for c in LATE_ORDER:
             pick_candidate(c, *third_c)
         quantize_z(1, *second_c)
         score(*second_c, y_second, [])

@@ -39,10 +39,17 @@ MAXED = {(5, 1): 0, (6, 0): P, (6, 1): 0, (7, 0): 0, (7, 1): 0}
 PAIRED = (1, 2, 3)
 LATE_ORDER = (4, 6, 7, 5)
 B_BANK = {(0, 0): 0, (0, 1): 1, (1, 0): 5, (1, 1): 0, (2, 0): 1, (6, 0): 5}
-A_BANK = {(0, 0): 2, (0, 1): 3, (1, 0): 4, (1, 1): 1, (2, 0): 0, (6, 0): 0}
-SUM_BANK = {(6, 0): 5, (6, 1): 0, (7, 0): 5, (7, 1): 1, (5, 1): 3}
+A_BANK = {(0, 0): 2, (0, 1): 3, (1, 0): 4, (1, 1): 1, (2, 0): 0, (6, 0): 5}
+SUM_BANK = {(6, 0): 5, (6, 1): 5, (7, 0): 0, (7, 1): 1, (5, 1): 3}
 TURNED_BANKS = (6, 7, 4)
 FIRST_BANK = {step: 2 * (step % 2) for step in PAIRED}
+STAGED_AT = {6: 0, 4: 4096}
+PICKED_AT = {2: 2048}
+GAIN_AT = {0: 6144, 1: 8192}
+CODES_AT = {6: 6144, 4: 8192}
+W2_AT = {0: 7168, 1: 0, 2: 4096, 3: 2048}
+W2_PIECES = [(0, 128), (128, 192), (320, 64), (384, 192), (576, 192)]
+W2_BESIDE = {0: 0, 1: 1, 2: 3, 3: 4}
 SCALAR_GAINS = 6
 CHUNKS = [(0, 256), (256, 128), (384, 128)]
 
@@ -54,7 +61,8 @@ def tile_list_code_pair_match_kernel(
     with ExitStack() as ctx:
         keep = ctx.enter_context(tc.tile_pool(name="keep", bufs=1))
         ring = ctx.enter_context(tc.tile_pool(name="ring", bufs=3))
-        picks = ctx.enter_context(tc.tile_pool(name="picks", bufs=5))
+        picks = ctx.enter_context(tc.tile_pool(name="picks", bufs=6))
+        laid = ctx.enter_context(tc.tile_pool(name="laid", bufs=1))
         psum = ctx.enter_context(tc.psum_pool(name="psum", bufs=1))
 
         b_bank, a_bank = dict(B_BANK), dict(A_BANK)
@@ -107,8 +115,8 @@ def tile_list_code_pair_match_kernel(
         load_w1(0)
         load_w1(1)
         nc.sync.dma_start(pos1_sb[:], pos1)
-        nc.sync.dma_start(pos2_sb[:], pos2)
         load_w1(2)
+        nc.sync.dma_start(pos2_sb[:], pos2)
         load_w4(1)
         w2_rows = w2.rearrange("(g u t e) n -> g e u t n", g=GROUPS, t=PACK, e=RUN)
         w2_raw = []
@@ -165,13 +173,23 @@ def tile_list_code_pair_match_kernel(
 
         def stage_w1(i, tag):
             c0, c1 = W1_CALLS[i]
-            staged = keep.tile([P, c1 - c0, P, PACK], BF16, name="w1_bf", tag=tag, align_bytes=64)
+            if c0 in STAGED_AT:
+                staged = laid.tile([P, 2, P, PACK], BF16, name=tag, offset=STAGED_AT[c0], align_bytes=64)
+            else:
+                staged = keep.tile([P, c1 - c0, P, PACK], BF16, name="w1_bf", tag=tag, align_bytes=64)
             for c in range(c0, c1):
                 w1_bf[c] = (staged, c - c0)
 
         for i in (0, 1, 3, 4):
             stage_w1(i, "w1_bf%d" % W1_CALLS[i][0])
-        w1_w = keep.tile([P, H], U32, name="w1_w", align_bytes=64)
+        w1_w = keep.tile([P, PASS], U32, name="w1_w", align_bytes=64)
+        w1_late = {}
+
+        def w1_codes(c):
+            if c < PACK:
+                return w1_w[:, c * P : (c + 1) * P].bitcast(FP8X4)
+            return w1_late[c - c % 2][:, c % 2 * P : (c % 2 + 1) * P].bitcast(FP8X4)
+
         w1_s = keep.tile([P, H], U8, name="w1_s", align_bytes=64)
 
         def cast_w1(i, t):
@@ -201,9 +219,13 @@ def tile_list_code_pair_match_kernel(
         def quantize_w1(i):
             c0, c1 = W1_CALLS[i]
             src = w1_bf[c0][0][:].rearrange("p t m j -> p (t m j)")
-            quantize(w1_w, w1_s, src, c0 * P, (c1 - c0) * P)
+            if c0 in CODES_AT:
+                w1_late[c0] = laid.tile([P, 2 * P], U32, name="w1_late%d" % c0, offset=CODES_AT[c0], align_bytes=64)
+                nc.vector.quantize_mx(out=w1_late[c0][:].bitcast(FP8X4), scales=w1_s[:, c0 * P : c1 * P], in_=src)
+            else:
+                quantize(w1_w, w1_s, src, c0 * P, (c1 - c0) * P)
 
-        w2_w = keep.tile([P, GROUPS * N], U32, name="w2_w", align_bytes=64)
+        w2_w = []
         w2_s = keep.tile([P, GROUPS * N], U8, name="w2_s", align_bytes=64)
 
         def interleave(copy, dst, src):
@@ -212,20 +234,28 @@ def tile_list_code_pair_match_kernel(
                 src.rearrange("p t (c i) -> p c t i", i=4),
             )
 
-        def round_w2_late(tag):
-            w2_bf = keep.tile([P, N - P, PACK], BF16, name="w2_bf", tag=tag, align_bytes=64)
-            interleave(nc.scalar.copy, w2_bf[:], w2_raw[1][:, :, P:N])
-            quantize(w2_w, w2_s, w2_bf[:].rearrange("p n j -> p (n j)"), N + P, N - P)
+        w2_bf = {}
 
-        w2_early = {}
+        def w2_source(i):
+            first, count = W2_PIECES[i]
+            return w2_raw[first // N][:, :, first % N : first % N + count]
 
-        def cast_w2_early(n, tag):
-            w2_early[n] = keep.tile([P, P, PACK], BF16, name="w2_early", tag=tag, align_bytes=64)
-            g, cols = n // N_TILES, slice(n % N_TILES * P, (n % N_TILES + 1) * P)
-            nc.gpsimd.tensor_copy(w2_early[n][:], w2_raw[g][:, :, cols].rearrange("p t n -> p n t"))
+        def round_w2_beside(c):
+            i = W2_BESIDE[c]
+            shape = [P, W2_PIECES[i][1], PACK]
+            w2_bf[i] = laid.tile(shape, BF16, name="w2_bf%d" % i, offset=W2_AT[c], align_bytes=64)
+            nc.gpsimd.tensor_copy(w2_bf[i][:], w2_source(i).rearrange("p t n -> p n t"))
 
-        def quantize_w2_early(n):
-            quantize(w2_w, w2_s, w2_early[n][:].rearrange("p n j -> p (n j)"), n * P, P)
+        def round_w2_late(i, tag):
+            w2_bf[i] = keep.tile([P, W2_PIECES[i][1], PACK], BF16, name="w2_bf", tag=tag, align_bytes=64)
+            interleave(nc.scalar.copy, w2_bf[i][:], w2_source(i))
+
+        def quantize_w2(i):
+            first, count = W2_PIECES[i]
+            for at in range(0, count, P):
+                width = min(P, count - at)
+                src = w2_bf[i][:, at : at + width, :].rearrange("p n j -> p (n j)")
+                quantize(w2_w[0], w2_s, src, first + at, width)
 
         def maxed(c, half):
             return MAXED.get((c, half), BANK) if c < TILES else 0
@@ -273,7 +303,7 @@ def tile_list_code_pair_match_kernel(
             acc_a = bank(number, [width])
             nc.tensor.matmul_mx(
                 out=acc_a[:],
-                lhsT=w1_w[:, c * P : (c + 1) * P].bitcast(FP8X4),
+                lhsT=w1_codes(c),
                 lhsT_scale=w1_s[:, c * P : (c + 1) * P],
                 rhs=v_w[half][:, 0:width].bitcast(FP8X4),
                 rhs_scale=v_s[:, cols],
@@ -302,7 +332,7 @@ def tile_list_code_pair_match_kernel(
             skip = maxed(c, half) // P
             minus_a = bank(next_bank(), [PACK, P])
             b_less_a = bank(next_bank(), [PACK, P])
-            w1_codes, w1_scales = w1_w[:, c * P : (c + 1) * P].bitcast(FP8X4), w1_s[:, c * P : (c + 1) * P]
+            w1_scales = w1_s[:, c * P : (c + 1) * P]
             w4_scale = w4_s[:].bitcast(U8)[:, c * P : (c + 1) * P]
 
             def turned(acc, j, codes, scales, start, stop):
@@ -317,9 +347,9 @@ def tile_list_code_pair_match_kernel(
                 )
 
             for j in range(skip, PACK):
-                turned(minus_a, j, w1_codes, w1_scales, True, True)
+                turned(minus_a, j, w1_codes(c), w1_scales, True, True)
             for j in range(skip, PACK):
-                turned(b_less_a, j, w1_codes, w1_scales, True, False)
+                turned(b_less_a, j, w1_codes(c), w1_scales, True, False)
                 turned(b_less_a, j, w4_codes(c), w4_scale, False, True)
             split_turned(c, half, minus_a, b_less_a, "parts%d" % ADDED.index((c, half)))
 
@@ -368,13 +398,16 @@ def tile_list_code_pair_match_kernel(
 
         def spread_gain(c, count):
             g, t = divmod(c, PACK)
-            gain[c] = keep.tile([P, PAIRS], F32, name="gain", tag="gain%d" % c, align_bytes=64)
+            if c in GAIN_AT:
+                gain[c] = laid.tile([P, PAIRS], F32, name="gain%d" % c, offset=GAIN_AT[c], align_bytes=64)
+            else:
+                gain[c] = keep.tile([P, PAIRS], F32, name="gain", tag="gain%d" % c, align_bytes=64)
             copy = nc.scalar.copy if c < SCALAR_GAINS else nc.vector.tensor_copy
             copy(gain[c][:], gz_sb[:, g, RUN * t : RUN * t + 1].to_broadcast([P, count]))
 
         def pick_query(c, first, count):
-            if c in (1, 2):
-                picked = keep.tile([P, count], F32, name="picked", tag="w1_bf%d" % (TILES - 2 * c), align_bytes=64)[:]
+            if c in PICKED_AT:
+                picked = laid.tile([P, count], F32, name="picked%d" % c, offset=PICKED_AT[c], align_bytes=64)[:]
             elif c in (4, 6):
                 if c == 4:
                     query["pair"] = keep.tile([P, 2, count], F32, name="picked_pair", tag="parts2", align_bytes=64)
@@ -412,7 +445,7 @@ def tile_list_code_pair_match_kernel(
             w_cols = slice(g * N + n * P, g * N + (n + 1) * P)
             nc.tensor.matmul_mx(
                 out=acc,
-                lhsT=w2_w[:, w_cols].bitcast(FP8X4),
+                lhsT=w2_w[0][:, w_cols].bitcast(FP8X4),
                 lhsT_scale=w2_s[:, w_cols],
                 rhs=z_w[g][:, cols].bitcast(FP8X4),
                 rhs_scale=z_s[g][:, cols],
@@ -472,25 +505,23 @@ def tile_list_code_pair_match_kernel(
         project_w4(1, 1)
         project_w4(2, 0)
         pick_query(0, 0, PAIRS)
-        cast_w2_early(0, "gain0")
+        round_w2_beside(0)
         encode(2, 0)
         encode(1, 1)
         z_f[(0, 0)] = keep.tile([P, PACK, PAIRS], F32, name="z_f0", tag="b_apart2", align_bytes=64)
         pick_candidate(0, 0, PAIRS)
-        quantize_w2_early(0)
         for c in PAIRED:
             project_w4(c + 1, 1)
-            project_w4(c + 2, 0)
             if c < 3:
                 for t in [(2, 3), (0,)][c - 1]:
                     cast_w1(2, t)
                 quantize_w1(5 - c)
+            project_w4(c + 2, 0)
             pick_query(c, 0, PAIRS)
-            cast_w2_early(c, "gain%d" % c)
+            round_w2_beside(c)
             encode(c + 2, 0)
             encode(c + 1, 1)
             pick_candidate(c, 0, PAIRS)
-            quantize_w2_early(c)
             if c > 1:
                 add_turned(*ADDED[c - 2])
             if c == 2:
@@ -503,6 +534,9 @@ def tile_list_code_pair_match_kernel(
         pick_query(6, 0, PAIRS)
         pick_candidate(4, *first_c)
         pick_candidate(6, *first_c)
+        w2_w.append(keep.tile([P, GROUPS * N], U32, name="w2_w", tag="gain4", align_bytes=64))
+        for i in W2_BESIDE.values():
+            quantize_w2(i)
         project_turned(*ADDED[3])
         turn_both(*TWICE, both)
         add_turned(*ADDED[3])
@@ -511,7 +545,8 @@ def tile_list_code_pair_match_kernel(
         pick_query(5, 0, PAIRS)
         pick_candidate(7, *first_c)
         pick_candidate(5, *first_c)
-        round_w2_late("parts3")
+        round_w2_late(2, "parts3")
+        quantize_w2(2)
         stage_z(0, 0, PAIRS, "gain7")
         for first in range(0, PAIRS, 2 * P):
             round_z(0, first, 2 * P, 0, 0)

@@ -35,21 +35,20 @@ W1_LOADS = [(0, 256), (256, 256), (512, 512)]
 NEGATED = (6, 7)
 ADDED = [(6, 0), (6, 1), (7, 0), (7, 1)]
 TWICE = (5, 1)
-MAXED = {(5, 1): 0, (6, 0): P, (6, 1): 0, (7, 0): 0, (7, 1): 0}
+SHORT = (7, 0)
 PAIRED = (1, 2, 3)
 LATE_ORDER = (4, 6, 7, 5)
-B_BANK = {(0, 0): 0, (0, 1): 1, (1, 0): 5, (1, 1): 0, (2, 0): 1, (6, 0): 5}
-A_BANK = {(0, 0): 2, (0, 1): 3, (1, 0): 4, (1, 1): 1, (2, 0): 0, (6, 0): 5}
+B_BANK = {(0, 0): 0, (0, 1): 1, (1, 0): 5, (1, 1): 0, (2, 0): 1}
+A_BANK = {(0, 0): 2, (0, 1): 3, (1, 0): 4, (1, 1): 1, (2, 0): 0}
 SUM_BANK = {(6, 0): 5, (6, 1): 5, (7, 0): 0, (7, 1): 1, (5, 1): 3}
 TURNED_BANKS = (6, 7, 4)
 FIRST_BANK = {step: 2 * (step % 2) for step in PAIRED}
-STAGED_AT = {6: 0, 4: 4096}
-PICKED_AT = {2: 2048}
+PICKED_AT = {0: 0, 1: 2048, 2: 4096}
 GAIN_AT = {0: 6144, 1: 8192}
 CODES_AT = {6: 6144, 4: 8192}
-W2_AT = {0: 7168, 1: 0, 2: 4096, 3: 2048}
-W2_PIECES = [(0, 128), (128, 192), (320, 64), (384, 192), (576, 192)]
-W2_BESIDE = {0: 0, 1: 1, 2: 3, 3: 4}
+W2_AT = {0: 7168, 1: 0, 2: 2048, 3: 4096}
+W2_PIECES = [(0, 128), (128, 192), (384, 192), (576, 128), (320, 64), (704, 64)]
+NARROW = (5, 0)
 SCALAR_GAINS = 6
 CHUNKS = [(0, 256), (256, 128), (384, 128)]
 
@@ -61,7 +60,7 @@ def tile_list_code_pair_match_kernel(
     with ExitStack() as ctx:
         keep = ctx.enter_context(tc.tile_pool(name="keep", bufs=1))
         ring = ctx.enter_context(tc.tile_pool(name="ring", bufs=3))
-        picks = ctx.enter_context(tc.tile_pool(name="picks", bufs=6))
+        picks = ctx.enter_context(tc.tile_pool(name="picks", bufs=5))
         laid = ctx.enter_context(tc.tile_pool(name="laid", bufs=1))
         psum = ctx.enter_context(tc.psum_pool(name="psum", bufs=1))
 
@@ -69,6 +68,8 @@ def tile_list_code_pair_match_kernel(
         for step in PAIRED:
             b_bank[(step + 1, 1)] = a_bank[(step + 2, 0)] = FIRST_BANK[step]
             b_bank[(step + 2, 0)] = a_bank[(step + 1, 1)] = FIRST_BANK[step] + 1
+
+        b_bank[(4, 1)] = 5
 
         def bank(number, shape):
             return psum.tile([P] + shape, F32, name="bank", tag="bank%d" % number)
@@ -116,15 +117,15 @@ def tile_list_code_pair_match_kernel(
         load_w1(1)
         nc.sync.dma_start(pos1_sb[:], pos1)
         load_w1(2)
-        nc.sync.dma_start(pos2_sb[:], pos2)
         load_w4(1)
         w2_rows = w2.rearrange("(g u t e) n -> g e u t n", g=GROUPS, t=PACK, e=RUN)
-        w2_raw = []
+        w2_raw = [keep.tile([P, PACK, N], F32, name="w2_raw%d" % g, align_bytes=64) for g in range(GROUPS)]
 
         def load_w2(g):
-            w2_raw.append(keep.tile([P, PACK, N], F32, name="w2_raw", tag="w2_raw%d" % g, align_bytes=64))
             for e in range(RUN):
                 nc.sync.dma_start(w2_raw[g][e:P:RUN, :, :], w2_rows[g, e])
+                if (g, e) == (0, 0):
+                    nc.sync.dma_start(pos2_sb[:], pos2)
 
         load_w2(0)
         load_w2(1)
@@ -173,10 +174,7 @@ def tile_list_code_pair_match_kernel(
 
         def stage_w1(i, tag):
             c0, c1 = W1_CALLS[i]
-            if c0 in STAGED_AT:
-                staged = laid.tile([P, 2, P, PACK], BF16, name=tag, offset=STAGED_AT[c0], align_bytes=64)
-            else:
-                staged = keep.tile([P, c1 - c0, P, PACK], BF16, name="w1_bf", tag=tag, align_bytes=64)
+            staged = keep.tile([P, c1 - c0, P, PACK], BF16, name="w1_bf", tag=tag, align_bytes=64)
             for c in range(c0, c1):
                 w1_bf[c] = (staged, c - c0)
 
@@ -241,14 +239,16 @@ def tile_list_code_pair_match_kernel(
             return w2_raw[first // N][:, :, first % N : first % N + count]
 
         def round_w2_beside(c):
-            i = W2_BESIDE[c]
+            i = c
             shape = [P, W2_PIECES[i][1], PACK]
             w2_bf[i] = laid.tile(shape, BF16, name="w2_bf%d" % i, offset=W2_AT[c], align_bytes=64)
             nc.gpsimd.tensor_copy(w2_bf[i][:], w2_source(i).rearrange("p t n -> p n t"))
 
-        def round_w2_late(i, tag):
-            w2_bf[i] = keep.tile([P, W2_PIECES[i][1], PACK], BF16, name="w2_bf", tag=tag, align_bytes=64)
-            interleave(nc.scalar.copy, w2_bf[i][:], w2_source(i))
+        def round_w2_late(tag):
+            rest = keep.tile([P, GROUPS, W2_PIECES[-1][1], PACK], BF16, name="w2_rest", tag=tag, align_bytes=64)
+            for g in range(GROUPS):
+                w2_bf[4 + g] = rest[:, g]
+                interleave(nc.scalar.copy, rest[:, g], w2_source(4 + g))
 
         def quantize_w2(i):
             first, count = W2_PIECES[i]
@@ -258,16 +258,16 @@ def tile_list_code_pair_match_kernel(
                 quantize(w2_w[0], w2_s, src, first + at, width)
 
         def maxed(c, half):
-            return MAXED.get((c, half), BANK) if c < TILES else 0
+            return BANK // 2 if (c, half) == NARROW else BANK
 
         h = {
-            c: keep.tile([P, S + (2 * BANK if c in PAIRED else 0)], F32, name="h%d" % c, align_bytes=64)
+            c: keep.tile([P, S + (BANK + maxed(c + 2, 0) if c in PAIRED else 0)], F32, name="h%d" % c, align_bytes=64)
             for c in range(1, TILES)
         }
 
         b_apart = {
-            unit: keep.tile([P, maxed(*unit)], F32, name="b_apart", tag="b_apart%d" % unit[0], align_bytes=64)
-            for unit in [(1, 1), (2, 0), (6, 0)]
+            unit: keep.tile([P, BANK], F32, name="b_apart", tag="b_apart%d" % unit[0], align_bytes=64)
+            for unit in [(1, 1), (2, 0)]
         }
 
         def b_staged(c, half):
@@ -277,16 +277,16 @@ def tile_list_code_pair_match_kernel(
                 return h[0][:, S : S + BANK]
             if (c, half) in b_apart:
                 return b_apart[(c, half)][:]
-            return h[c - 2 + half][:, S + half * BANK : S + (half + 1) * BANK]
+            first = S + (1 - half) * BANK
+            return h[c - 2 + half][:, first : first + maxed(c, half)]
 
-        def multiply_w4(c, half, number, width):
-            cols = slice(half * BANK, half * BANK + width)
-            acc_b = bank(number, [width])
+        def multiply_w4(c, half, acc_b, width, skip=0):
+            cols = slice(half * BANK + skip, half * BANK + skip + width)
             nc.tensor.matmul_mx(
-                out=acc_b[:],
+                out=acc_b,
                 lhsT=w4_codes(c),
                 lhsT_scale=w4_s[:].bitcast(U8)[:, c * P : (c + 1) * P],
-                rhs=v_w[half][:, 0:width].bitcast(FP8X4),
+                rhs=v_w[half][:, skip : skip + width].bitcast(FP8X4),
                 rhs_scale=v_s[:, cols],
                 start=True,
                 stop=True,
@@ -295,17 +295,16 @@ def tile_list_code_pair_match_kernel(
 
         def project_w4(c, half, acc_b=None):
             if acc_b is None:
-                acc_b = multiply_w4(c, half, b_bank[(c, half)], maxed(c, half))
-            nc.scalar.copy(b_staged(c, half), acc_b[:])
+                acc_b = multiply_w4(c, half, bank(b_bank[(c, half)], [maxed(c, half)])[:], maxed(c, half))
+            nc.scalar.copy(b_staged(c, half), acc_b)
 
-        def multiply_w1(c, half, number, width):
-            cols = slice(half * BANK, half * BANK + width)
-            acc_a = bank(number, [width])
+        def multiply_w1(c, half, acc_a, width, skip=0):
+            cols = slice(half * BANK + skip, half * BANK + skip + width)
             nc.tensor.matmul_mx(
-                out=acc_a[:],
+                out=acc_a,
                 lhsT=w1_codes(c),
                 lhsT_scale=w1_s[:, c * P : (c + 1) * P],
-                rhs=v_w[half][:, 0:width].bitcast(FP8X4),
+                rhs=v_w[half][:, skip : skip + width].bitcast(FP8X4),
                 rhs_scale=v_s[:, cols],
                 start=True,
                 stop=True,
@@ -314,12 +313,8 @@ def tile_list_code_pair_match_kernel(
 
         def encode(c, half):
             width = maxed(c, half)
-            cols = slice(half * BANK, half * BANK + width)
-            acc_a = multiply_w1(c, half, a_bank[(c, half)], width)
-            if c in NEGATED:
-                nc.vector.scalar_tensor_tensor(h[c][:, cols], acc_a[:], -1.0, b_staged(c, half), MULT, MAX)
-            else:
-                nc.vector.tensor_tensor(h[c][:, cols], acc_a[:], b_staged(c, half), MAX)
+            acc_a = multiply_w1(c, half, bank(a_bank[(c, half)], [width])[:], width)
+            nc.vector.tensor_tensor(h[c][:, half * BANK : half * BANK + width], acc_a, b_staged(c, half), MAX)
 
         turned_parts = {}
         dealt = []
@@ -328,8 +323,19 @@ def tile_list_code_pair_match_kernel(
             dealt.append(TURNED_BANKS[len(dealt) % len(TURNED_BANKS)])
             return dealt[-1]
 
-        def project_turned(c, half):
-            skip = maxed(c, half) // P
+        def turn(acc, src, start, stop):
+            nc.tensor.matmul(acc, src, ident[:], start=start, stop=stop, is_transpose=True)
+
+        def project_short(c, half):
+            accs = bank(5, [2, P])
+            multiply_w1(c, half, accs[:, 0, :], P)
+            multiply_w4(c, half, accs[:, 1, :], P)
+            short = keep.tile([P, 2, P], F32, name="short", align_bytes=64)
+            nc.scalar.copy(short[:], accs[:])
+            return short
+
+        def project_turned(c, half, short=None):
+            skip = 0 if short is None else 1
             minus_a = bank(next_bank(), [PACK, P])
             b_less_a = bank(next_bank(), [PACK, P])
             w1_scales = w1_s[:, c * P : (c + 1) * P]
@@ -348,45 +354,77 @@ def tile_list_code_pair_match_kernel(
 
             for j in range(skip, PACK):
                 turned(minus_a, j, w1_codes(c), w1_scales, True, True)
+            if skip:
+                turn(minus_a[:, 0, :], short[:, 0, :], True, True)
+                turn(b_less_a[:, 0, :], short[:, 0, :], True, False)
+                turn(b_less_a[:, 0, :], short[:, 1, :], False, True)
             for j in range(skip, PACK):
                 turned(b_less_a, j, w1_codes(c), w1_scales, True, False)
                 turned(b_less_a, j, w4_codes(c), w4_scale, False, True)
             split_turned(c, half, minus_a, b_less_a, "parts%d" % ADDED.index((c, half)))
 
         def split_turned(c, half, minus_a, b_less_a, tag):
-            skip = maxed(c, half) // P
             parts = keep.tile([P, 2, PACK, P], F32, name="parts", tag=tag, align_bytes=64)
             a_t, r_t = parts[:, 0], parts[:, 1]
-            nc.scalar.activation(a_t[:, skip:], minus_a[:, skip:], COPY, scale=-1.0)
-            nc.scalar.activation(r_t[:, skip:], b_less_a[:, skip:], RELU)
+            nc.scalar.activation(a_t, minus_a[:], COPY, scale=-1.0)
+            nc.scalar.activation(r_t, b_less_a[:], RELU)
             turned_parts[(c, half)] = (a_t, r_t)
 
         def project_both(c, half):
             both = keep.tile([P, 2, PACK, P], F32, name="both", align_bytes=64)
-            acc_a = multiply_w1(c, half, next_bank(), BANK)
-            acc_b = multiply_w4(c, half, next_bank(), BANK)
-            nc.scalar.activation(both[:, 0].rearrange("p j s -> p (j s)"), acc_a[:], COPY, scale=-1.0)
-            nc.scalar.copy(both[:, 1].rearrange("p j s -> p (j s)"), acc_b[:])
+            acc_a = multiply_w1(c, half, bank(next_bank(), [BANK])[:], BANK)
+            acc_b = multiply_w4(c, half, bank(next_bank(), [BANK])[:], BANK)
+            nc.scalar.activation(both[:, 0].rearrange("p j s -> p (j s)"), acc_a, COPY, scale=-1.0)
+            nc.scalar.copy(both[:, 1].rearrange("p j s -> p (j s)"), acc_b)
             return both
 
         def turn_both(c, half, both):
             minus_a = bank(next_bank(), [PACK, P])
             b_less_a = bank(next_bank(), [PACK, P])
             for j in range(PACK):
-                nc.tensor.matmul(minus_a[:, j, :], both[:, 0, j, :], ident[:], start=True, stop=True, is_transpose=True)
+                turn(minus_a[:, j, :], both[:, 0, j, :], True, True)
             for j in range(PACK):
-                nc.tensor.matmul(b_less_a[:, j, :], both[:, 0, j, :], ident[:], start=True, stop=False, is_transpose=True)
-                nc.tensor.matmul(b_less_a[:, j, :], both[:, 1, j, :], ident[:], start=False, stop=True, is_transpose=True)
+                turn(b_less_a[:, j, :], both[:, 0, j, :], True, False)
+                turn(b_less_a[:, j, :], both[:, 1, j, :], False, True)
             split_turned(c, half, minus_a, b_less_a, "parts_last")
+
+        def project_narrow(c, half):
+            width = BANK - maxed(c, half)
+            accs = bank(5, [2, width])
+            multiply_w1(c, half, accs[:, 0, :], width, BANK - width)
+            multiply_w4(c, half, accs[:, 1, :], width, BANK - width)
+            pair = keep.tile([P, 2, width], F32, name="pair", align_bytes=64)
+            nc.scalar.activation(pair[:, 0, :], accs[:, 0, :], COPY, scale=-1.0)
+            nc.scalar.copy(pair[:, 1, :], accs[:, 1, :])
+            return pair
+
+        def turn_narrow(pair):
+            accs = bank(5, [2, 2, P])
+            for j in range(2):
+                turn(accs[:, 0, j, :], pair[:, 0, j * P : (j + 1) * P], True, True)
+            for j in range(2):
+                turn(accs[:, 1, j, :], pair[:, 0, j * P : (j + 1) * P], True, False)
+                turn(accs[:, 1, j, :], pair[:, 1, j * P : (j + 1) * P], False, True)
+            terms = keep.tile([P, 2, 2, P], F32, name="terms", align_bytes=64)
+            nc.scalar.activation(terms[:, 0], accs[:, 0], COPY, scale=-1.0)
+            nc.scalar.activation(terms[:, 1], accs[:, 1], RELU)
+            return terms
+
+        def add_narrow(c, half, terms):
+            total = bank(2, [2, P])
+            for j in range(2):
+                turn(total[:, j, :], terms[:, 0, j, :], True, False)
+                turn(total[:, j, :], terms[:, 1, j, :], False, True)
+            first = half * BANK + maxed(c, half)
+            nc.scalar.copy(h[c][:, first : (half + 1) * BANK], total[:].rearrange("p j s -> p (j s)"))
 
         def add_turned(c, half):
             a_t, r_t = turned_parts[(c, half)]
-            skip = maxed(c, half) // P
             total = bank(SUM_BANK[(c, half)], [PACK, P])
-            for j in range(skip, PACK):
-                nc.tensor.matmul(total[:, j, :], a_t[:, j, :], ident[:], start=True, stop=False, is_transpose=True)
-                nc.tensor.matmul(total[:, j, :], r_t[:, j, :], ident[:], start=False, stop=True, is_transpose=True)
-            nc.scalar.copy(h[c][:, half * BANK + skip * P : (half + 1) * BANK], total[:, skip:].rearrange("p j s -> p (j s)"))
+            for j in range(PACK):
+                turn(total[:, j, :], a_t[:, j, :], True, False)
+                turn(total[:, j, :], r_t[:, j, :], False, True)
+            nc.scalar.copy(h[c][:, half * BANK : (half + 1) * BANK], total[:].rearrange("p j s -> p (j s)"))
 
         z_f = {}
         z_f[(1, 0)] = keep.tile([P, PACK, CHUNKS[0][1]], F32, name="z_f1", tag="z_f1", align_bytes=64)
@@ -489,9 +527,9 @@ def tile_list_code_pair_match_kernel(
         round_halves(0, "w1_front")
         quantize_w1(0)
         quantize_w1(1)
-        round_halves(1, "w1_bf0")
-        h[0] = keep.tile([P, 2 * S + BANK], F32, name="h0", tag="w1_bf1", align_bytes=64)
-        early = {unit: multiply_w4(*unit, b_bank[unit], BANK) for unit in [(0, 0), (1, 0), (0, 1)]}
+        round_halves(1, "w1_bf1")
+        h[0] = keep.tile([P, 2 * S + BANK], F32, name="h0", tag="w1_bf0", align_bytes=64)
+        early = {unit: multiply_w4(*unit, bank(b_bank[unit], [BANK])[:], BANK) for unit in [(0, 0), (1, 0), (0, 1)]}
         for c, half in [(0, 0), (0, 1), (1, 0)]:
             project_w4(c, half, early[(c, half)])
             encode(c, half)
@@ -508,26 +546,33 @@ def tile_list_code_pair_match_kernel(
         round_w2_beside(0)
         encode(2, 0)
         encode(1, 1)
+        project_w4(2, 1)
+        cast_w1(2, 2)
+        cast_w1(2, 3)
+        quantize_w1(4)
+        cast_w1(2, 0)
         z_f[(0, 0)] = keep.tile([P, PACK, PAIRS], F32, name="z_f0", tag="b_apart2", align_bytes=64)
         pick_candidate(0, 0, PAIRS)
+        short = None
         for c in PAIRED:
-            project_w4(c + 1, 1)
-            if c < 3:
-                for t in [(2, 3), (0,)][c - 1]:
-                    cast_w1(2, t)
-                quantize_w1(5 - c)
             project_w4(c + 2, 0)
             pick_query(c, 0, PAIRS)
             round_w2_beside(c)
             encode(c + 2, 0)
             encode(c + 1, 1)
+            if c == 1:
+                project_w4(3, 1)
+                quantize_w1(3)
             pick_candidate(c, 0, PAIRS)
             if c > 1:
                 add_turned(*ADDED[c - 2])
-            if c == 2:
-                project_w4(6, 0)
-            project_turned(*ADDED[c - 1])
-        encode(6, 0)
+            if c == 3:
+                pair = project_narrow(*NARROW)
+            if c == 1:
+                short = project_short(*SHORT)
+                project_w4(4, 1)
+            project_turned(*ADDED[c - 1], short if ADDED[c - 1] == SHORT else None)
+        terms = turn_narrow(pair)
         both = project_both(*TWICE)
         add_turned(*ADDED[2])
         pick_query(4, 0, PAIRS)
@@ -535,9 +580,10 @@ def tile_list_code_pair_match_kernel(
         pick_candidate(4, *first_c)
         pick_candidate(6, *first_c)
         w2_w.append(keep.tile([P, GROUPS * N], U32, name="w2_w", tag="gain4", align_bytes=64))
-        for i in W2_BESIDE.values():
+        for i in range(4):
             quantize_w2(i)
         project_turned(*ADDED[3])
+        add_narrow(*NARROW, terms)
         turn_both(*TWICE, both)
         add_turned(*ADDED[3])
         add_turned(*TWICE)
@@ -545,18 +591,20 @@ def tile_list_code_pair_match_kernel(
         pick_query(5, 0, PAIRS)
         pick_candidate(7, *first_c)
         pick_candidate(5, *first_c)
-        round_w2_late(2, "parts3")
-        quantize_w2(2)
-        stage_z(0, 0, PAIRS, "gain7")
-        for first in range(0, PAIRS, 2 * P):
-            round_z(0, first, 2 * P, 0, 0)
-        quantize_z(0, 0, PAIRS)
-        z_f[(1, second_c[0])] = keep.tile([P, PACK, second_c[1]], F32, name="z_f1_next", tag="b_apart2", align_bytes=64)
+        round_w2_late("parts3")
+        quantize_w2(4)
+        quantize_w2(5)
+        stage_z(0, 0, third_c[0], "gain7")
+        round_z(0, 0, third_c[0], 0, 0)
+        quantize_z(0, 0, third_c[0])
+        z_f[(1, second_c[0])] = z_f[(0, 0)][:, :, 0 : second_c[1]]
         for c in LATE_ORDER:
             pick_candidate(c, *second_c)
         stage_z(1, *first_c, "z_first")
         round_z(1, *first_c, first_c[0], first_c[0])
         quantize_z(1, *first_c)
+        stage_z(0, *third_c, "gain5")
+        round_z(0, *third_c, 0, third_c[0])
         y_pair = bank(5, [2, first_c[1]])
         y_lone = bank(6, [first_c[1]])
         y_first = [y_pair[:, 0, :], y_lone[:], y_pair[:, 1, :]]
@@ -568,16 +616,17 @@ def tile_list_code_pair_match_kernel(
         score(*first_c, y_first, [2])
         for n in range(N_TILES):
             score_pass(0, n, *second_c, y_second[n])
-        for n in range(N_TILES):
-            score_pass(0, n, *third_c, y_third[n])
         stage_z(1, *second_c, "z_rest")
         round_z(1, *second_c, second_c[0], second_c[0])
         z_f[(1, third_c[0])] = keep.tile([P, PACK, third_c[1]], F32, name="z_f1_last", tag="z_f1", align_bytes=64)
         for c in LATE_ORDER:
             pick_candidate(c, *third_c)
         quantize_z(1, *second_c)
+        quantize_z(0, *third_c)
         score(*second_c, y_second, [])
-        z_last = keep.tile([P, third_c[1], PACK], BF16, name="z_last", align_bytes=64)
+        for n in range(N_TILES):
+            score_pass(0, n, *third_c, y_third[n])
+        z_last = keep.tile([P, third_c[1], PACK], BF16, name="z_last", tag="b_apart2", align_bytes=64)
         halves = [slice(0, third_c[1] // 2), slice(third_c[1] // 2, third_c[1])]
         for part in halves:
             interleave(nc.vector.tensor_copy, z_last[:, part, :], z_f[(1, third_c[0])][:, :, part])

@@ -44,10 +44,15 @@ SUM_BANK = {(6, 0): 5, (6, 1): 5, (7, 0): 0, (7, 1): 1, (5, 1): 3}
 TURNED_BANKS = (6, 7, 4)
 FIRST_BANK = {step: 2 * (step % 2) for step in PAIRED}
 PICKED_AT = {0: 0, 1: 2048, 2: 4096}
+LAST_TERMS_AT = 13312
+W2_SCALES_AT = {2: LAST_TERMS_AT + 2112, 3: LAST_TERMS_AT + 2240}
+W2_REST_AT = LAST_TERMS_AT + 2368
+Z_FIRST_AT = LAST_TERMS_AT - 3072 + 64
+PICKED_LAST_AT = LAST_TERMS_AT + 64
 GAIN_AT = {0: 6144, 1: 8192}
 CODES_AT = {6: 6144, 4: 8192}
 W2_AT = {0: 7168, 1: 0, 2: 2048, 3: 4096}
-W2_PIECES = [(0, 128), (128, 192), (384, 192), (576, 128), (320, 64), (704, 64)]
+W2_PIECES = [(0, 128), (128, 128), (256, 128), (384, 128), (512, 256)]
 NARROW = (5, 0)
 SCALAR_GAINS = 6
 CHUNKS = [(0, 256), (256, 128), (384, 128)]
@@ -224,7 +229,7 @@ def tile_list_code_pair_match_kernel(
                 quantize(w1_w, w1_s, src, c0 * P, (c1 - c0) * P)
 
         w2_w = []
-        w2_s = keep.tile([P, GROUPS * N], U8, name="w2_s", align_bytes=64)
+        w2_s = {}
 
         def interleave(copy, dst, src):
             copy(
@@ -244,18 +249,23 @@ def tile_list_code_pair_match_kernel(
             w2_bf[i] = laid.tile(shape, BF16, name="w2_bf%d" % i, offset=W2_AT[c], align_bytes=64)
             nc.gpsimd.tensor_copy(w2_bf[i][:], w2_source(i).rearrange("p t n -> p n t"))
 
-        def round_w2_late(tag):
-            rest = keep.tile([P, GROUPS, W2_PIECES[-1][1], PACK], BF16, name="w2_rest", tag=tag, align_bytes=64)
-            for g in range(GROUPS):
-                w2_bf[4 + g] = rest[:, g]
-                interleave(nc.scalar.copy, rest[:, g], w2_source(4 + g))
+        def round_w2_late():
+            w2_bf[4] = laid.tile([P, W2_PIECES[4][1], PACK], BF16, name="w2_rest", offset=W2_REST_AT, align_bytes=64)
+            interleave(nc.scalar.copy, w2_bf[4][:], w2_source(4))
 
         def quantize_w2(i):
             first, count = W2_PIECES[i]
+            if i in W2_SCALES_AT:
+                scales = laid.tile([P, count], U8, name="w2_s%d" % i, offset=W2_SCALES_AT[i], align_bytes=64)
+            else:
+                scales = keep.tile([P, count], U8, name="w2_s%d" % i, align_bytes=64)
             for at in range(0, count, P):
-                width = min(P, count - at)
-                src = w2_bf[i][:, at : at + width, :].rearrange("p n j -> p (n j)")
-                quantize(w2_w[0], w2_s, src, first + at, width)
+                w2_s[first + at] = scales[:, at : at + P]
+            nc.vector.quantize_mx(
+                out=w2_w[0][:, first : first + count].bitcast(FP8X4),
+                scales=scales[:],
+                in_=w2_bf[i][:].rearrange("p n j -> p (n j)"),
+            )
 
         def maxed(c, half):
             return BANK // 2 if (c, half) == NARROW else BANK
@@ -364,7 +374,10 @@ def tile_list_code_pair_match_kernel(
             split_turned(c, half, minus_a, b_less_a, "parts%d" % ADDED.index((c, half)))
 
         def split_turned(c, half, minus_a, b_less_a, tag):
-            parts = keep.tile([P, 2, PACK, P], F32, name="parts", tag=tag, align_bytes=64)
+            if tag is None:
+                parts = laid.tile([P, 2, PACK, P], F32, name="last_terms", offset=LAST_TERMS_AT, align_bytes=64)
+            else:
+                parts = keep.tile([P, 2, PACK, P], F32, name="parts", tag=tag, align_bytes=64)
             a_t, r_t = parts[:, 0], parts[:, 1]
             nc.scalar.activation(a_t, minus_a[:], COPY, scale=-1.0)
             nc.scalar.activation(r_t, b_less_a[:], RELU)
@@ -386,7 +399,7 @@ def tile_list_code_pair_match_kernel(
             for j in range(PACK):
                 turn(b_less_a[:, j, :], both[:, 0, j, :], True, False)
                 turn(b_less_a[:, j, :], both[:, 1, j, :], False, True)
-            split_turned(c, half, minus_a, b_less_a, "parts_last")
+            split_turned(c, half, minus_a, b_less_a, None)
 
         def project_narrow(c, half):
             width = BANK - maxed(c, half)
@@ -451,7 +464,7 @@ def tile_list_code_pair_match_kernel(
                     query["pair"] = keep.tile([P, 2, count], F32, name="picked_pair", tag="parts2", align_bytes=64)
                 picked = query["pair"][:, (c - 4) // 2, :]
             elif c == 7:
-                picked = keep.tile([P, count], F32, name="picked", tag="parts_last", align_bytes=64)[:]
+                picked = laid.tile([P, count], F32, name="picked7", offset=PICKED_LAST_AT, align_bytes=64)[:]
             else:
                 picked = picks.tile([P, count], F32, name="picked", align_bytes=64)[:]
             lst = pos1_sb[:, first // 16 : (first + count) // 16]
@@ -484,7 +497,7 @@ def tile_list_code_pair_match_kernel(
             nc.tensor.matmul_mx(
                 out=acc,
                 lhsT=w2_w[0][:, w_cols].bitcast(FP8X4),
-                lhsT_scale=w2_s[:, w_cols],
+                lhsT_scale=w2_s[w_cols.start],
                 rhs=z_w[g][:, cols].bitcast(FP8X4),
                 rhs_scale=z_s[g][:, cols],
                 start=(g == 0),
@@ -539,7 +552,6 @@ def tile_list_code_pair_match_kernel(
             staged[:, slot].rearrange("p (u e) j -> p u e j", e=RUN),
             w1_raw[2][:].rearrange("p j (u t e) -> p t u e j", t=PACK, e=RUN)[:, 1],
         )
-        permute_w4_words(nc.gpsimd.tensor_copy, 1, "w4_w1")
         project_w4(1, 1)
         project_w4(2, 0)
         pick_query(0, 0, PAIRS)
@@ -561,6 +573,7 @@ def tile_list_code_pair_match_kernel(
             encode(c + 2, 0)
             encode(c + 1, 1)
             if c == 1:
+                permute_w4_words(nc.scalar.copy, 1, "w4_w1")
                 project_w4(3, 1)
                 quantize_w1(3)
             pick_candidate(c, 0, PAIRS)
@@ -580,7 +593,7 @@ def tile_list_code_pair_match_kernel(
         pick_candidate(4, *first_c)
         pick_candidate(6, *first_c)
         w2_w.append(keep.tile([P, GROUPS * N], U32, name="w2_w", tag="gain4", align_bytes=64))
-        for i in range(4):
+        for i in range(2):
             quantize_w2(i)
         project_turned(*ADDED[3])
         add_narrow(*NARROW, terms)
@@ -588,13 +601,14 @@ def tile_list_code_pair_match_kernel(
         add_turned(*ADDED[3])
         add_turned(*TWICE)
         pick_query(7, 0, PAIRS)
+        for i in W2_SCALES_AT:
+            quantize_w2(i)
         pick_query(5, 0, PAIRS)
         pick_candidate(7, *first_c)
         pick_candidate(5, *first_c)
-        round_w2_late("parts3")
+        round_w2_late()
         quantize_w2(4)
-        quantize_w2(5)
-        stage_z(0, 0, third_c[0], "gain7")
+        z_bf[(0, 0)] = laid.tile([P, third_c[0], PACK], BF16, name="z_bf0", offset=Z_FIRST_AT, align_bytes=64)
         round_z(0, 0, third_c[0], 0, 0)
         quantize_z(0, 0, third_c[0])
         z_f[(1, second_c[0])] = z_f[(0, 0)][:, :, 0 : second_c[1]]

from contextlib import ExitStack

import concourse.mybir as mybir
from concourse.masks import make_identity

K, H, N, T, S, PAIRS = 512, 1024, 384, 2048, 1024, 512
FLOPS = 2 * (2 * K * H * S) + 2 * H * N * PAIRS

F32 = mybir.dt.float32
BF16 = mybir.dt.bfloat16
I32 = mybir.dt.int32
U32 = mybir.dt.uint32
U16 = mybir.dt.uint16
U8 = mybir.dt.uint8
FP8X4 = mybir.dt.float8_e4m3fn_x4
FP4X4 = mybir.dt.float4_e2m1fn_x4
MULT = mybir.AluOpType.mult
MAX = mybir.AluOpType.max
COPY = mybir.ActivationFunctionType.Copy
RELU = mybir.ActivationFunctionType.Relu
TANH = mybir.ActivationFunctionType.Tanh

P = 128
PACK = 4
PASS = P * PACK
BANK = 512
GROUPS = H // PASS
TILES = H // P
N_TILES = N // P
RUN = 2
SPAN = PACK * RUN
GZ_ROW = SPAN - RUN + 1
W1_CALLS = [(0, 1), (1, 2), (2, 4), (4, 6), (6, 8)]
W1_LOADS = [(0, 256), (256, 256), (512, 512)]
NEGATED = (6, 7)
ADDED = [(6, 0), (6, 1), (7, 0), (7, 1)]
TWICE = (5, 1)
SHORT = (7, 0)
PAIRED = (1, 2, 3)
LATE_ORDER = (4, 6, 7, 5)
B_BANK = {(0, 0): 0, (0, 1): 1, (1, 0): 5, (1, 1): 0, (2, 0): 1}
A_BANK = {(0, 0): 2, (0, 1): 3, (1, 0): 4, (1, 1): 1, (2, 0): 0}
SUM_BANK = {(6, 0): 5, (6, 1): 5, (7, 0): 0, (7, 1): 1, (5, 1): 3}
TURNED_BANKS = (6, 7, 4)
FIRST_BANK = {step: 2 * (step % 2) for step in PAIRED}
PICKED_AT = {0: 0, 1: 2048, 2: 4096}
LAST_TERMS_AT = 13312
W2_SCALES_AT = {2: LAST_TERMS_AT + 2112, 3: LAST_TERMS_AT + 2240}
W2_REST_AT = LAST_TERMS_AT + 2368
Z_FIRST_AT = LAST_TERMS_AT - 3072 + 64
PICKED_LAST_AT = LAST_TERMS_AT + 64
GAIN_AT = {0: 6144, 1: 8192}
CODES_AT = {6: 6144, 4: 8192}
W2_AT = {0: 7168, 1: 0, 2: 2048, 3: 4096}
W2_PIECES = [(0, 128), (128, 128), (256, 128), (384, 128), (512, 256)]
NARROW = (5, 0)
SCALAR_GAINS = 6
CHUNKS = [(0, 256), (256, 128), (384, 128)]


def tile_list_code_pair_match_kernel(
    tc, tab_words, tab_scales, offs, pos1, pos2, w1, w4_words, w4_scales, gz, w2, b2, out
):
    nc = tc.nc
    with ExitStack() as ctx:
        keep = ctx.enter_context(tc.tile_pool(name="keep", bufs=1))
        ring = ctx.enter_context(tc.tile_pool(name="ring", bufs=3))
        picks = ctx.enter_context(tc.tile_pool(name="picks", bufs=5))
        laid = ctx.enter_context(tc.tile_pool(name="laid", bufs=1))
        psum = ctx.enter_context(tc.psum_pool(name="psum", bufs=1))

        b_bank, a_bank = dict(B_BANK), dict(A_BANK)
        for step in PAIRED:
            b_bank[(step + 1, 1)] = a_bank[(step + 2, 0)] = FIRST_BANK[step]
            b_bank[(step + 2, 0)] = a_bank[(step + 1, 1)] = FIRST_BANK[step] + 1

        b_bank[(4, 1)] = 5

        def bank(number, shape):
            return psum.tile([P] + shape, F32, name="bank", tag="bank%d" % number)

        offs_sb = keep.tile([P, S // 16], U16, name="offs_sb")
        pos1_sb = keep.tile([P, PAIRS // 16], U16, name="pos1_sb")
        pos2_sb = keep.tile([P, PAIRS // 16], U16, name="pos2_sb")
        tab_w = keep.tile([P, T], I32, name="tab_w", align_bytes=64)
        tab_s = keep.tile([P, T // 4], I32, name="tab_s", align_bytes=64)
        w4_raw = [keep.tile([P, PASS // 2], I32, name="w4_raw%d" % g, align_bytes=64) for g in range(GROUPS)]
        w4s_raw = keep.tile([P, H // 4], I32, name="w4s_raw", tag="w4s_raw", align_bytes=64)
        w1_raw = [
            keep.tile([P, PACK, count], F32, name="w1_raw", tag="raw%d" % first, align_bytes=64)
            for first, count in W1_LOADS
        ]
        gz_sb = keep.tile([P, GROUPS, GZ_ROW], F32, name="gz_sb")
        b2_sb = keep.tile([P, N_TILES], F32, name="b2_sb")

        nc.vector.memset(tab_s[:], 0)
        nc.vector.memset(w4s_raw[:], 0)

        def load_scale_rows(plane, rows, queues):
            by_r = rows.rearrange("(q r) c -> r q c", r=4)
            for r in range(4):
                queues[r].dma_start(plane[r:P:32, :], by_r[r].bitcast(I32))

        w1_rows = w1.rearrange("(p j) c -> p j c", j=PACK)

        def load_w1(i):
            first, count = W1_LOADS[i]
            nc.sync.dma_start(w1_raw[i][:], w1_rows[:, :, first : first + count])

        def load_w4(g):
            nc.sync.dma_start(w4_raw[g][:], w4_words[0].bitcast(I32)[:, g * PASS // 2 : (g + 1) * PASS // 2])

        nc.sync.dma_start(offs_sb[:], offs)
        gz_runs = gz.rearrange("(g u s) -> u g s", g=GROUPS, s=SPAN)
        for e in range(RUN):
            nc.sync.dma_start(gz_sb[e:P:RUN, :, :], gz_runs[:, :, e : e + GZ_ROW])
        load_scale_rows(tab_s, tab_scales[0], [nc.sync] * 4)
        nc.sync.dma_start(tab_w[:], tab_words[0].rearrange("p t i -> p (t i)").bitcast(I32))
        load_w4(0)
        load_scale_rows(w4s_raw, w4_scales[0], [nc.sync] * 4)
        load_w1(0)
        load_w1(1)
        nc.sync.dma_start(pos1_sb[:], pos1)
        load_w1(2)
        load_w4(1)
        w2_rows = w2.rearrange("(g u t e) n -> g e u t n", g=GROUPS, t=PACK, e=RUN)
        w2_raw = [keep.tile([P, PACK, N], F32, name="w2_raw%d" % g, align_bytes=64) for g in range(GROUPS)]

        def load_w2(g):
            for e in range(RUN):
                nc.sync.dma_start(w2_raw[g][e:P:RUN, :, :], w2_rows[g, e])
                if (g, e) == (0, 0):
                    nc.sync.dma_start(pos2_sb[:], pos2)

        load_w2(0)
        load_w2(1)
        with nc.allow_non_contiguous_dma(reason="one bias value to a partition"):
            nc.sync.dma_start(b2_sb[:], b2.rearrange("(c p) -> p c", p=P))

        ident = keep.tile([P, P], F32, name="ident", align_bytes=64)
        zero = keep.tile([P, 1], F32, name="zero")
        nc.vector.memset(zero[:], 0.0)
        nc.scalar.activation(ident[:], zero[:].to_broadcast([P, P]), COPY)
        make_identity(nc, ident[:], nomemset=True)

        v_w = {}
        v_s = keep.tile([P, S], U8, name="v_s", align_bytes=64)

        def gather_scales():
            nc.vector.tensor_copy(v_s[:], tab_s[:].bitcast(U8).indirect(offs_sb[:]))

        def gather_words(half, tag):
            v_w[half] = keep.tile([P, BANK], U32, name="v_w", tag=tag, align_bytes=64)
            lst = offs_sb[:, half * BANK // 16 : (half + 1) * BANK // 16]
            nc.vector.tensor_copy(v_w[half][:], tab_w[:].bitcast(U32).indirect(lst))

        w4_w = {}
        w4_s = keep.tile([P, H // 4], I32, name="w4_s", align_bytes=64)

        def w4_codes(c):
            g, t = divmod(c, PACK)
            return w4_w[g][:].bitcast(U8)[:, 2 * t * P : 2 * (t + 1) * P].bitcast(FP4X4)

        def permute_w4_words(copy, g, tag):
            w4_w[g] = keep.tile([P, PASS // 2], I32, name="w4_w", tag=tag, align_bytes=64)
            copy(
                w4_w[g][:].bitcast(U32).rearrange("p (t b u) -> p b t u", t=PACK, u=4),
                w4_raw[g][:].bitcast(U32).rearrange("p (b u t) -> p b t u", t=PACK, u=4),
            )

        def permute_w4_scales(copy, g):
            cols = slice(g * PASS // 4, (g + 1) * PASS // 4)
            copy(
                w4_s[:, cols].bitcast(U16).rearrange("p (t b u) -> p b t u", t=PACK, u=8),
                w4s_raw[:, cols].bitcast(U16).rearrange("p (b u t) -> p b t u", t=PACK, u=8),
            )

        w1_bf = {}

        def stage_w1(i, tag):
            c0, c1 = W1_CALLS[i]
            staged = keep.tile([P, c1 - c0, P, PACK], BF16, name="w1_bf", tag=tag, align_bytes=64)
            for c in range(c0, c1):
                w1_bf[c] = (staged, c - c0)

        for i in (0, 1, 3, 4):
            stage_w1(i, "w1_bf%d" % W1_CALLS[i][0])
        w1_w = keep.tile([P, PASS], U32, name="w1_w", align_bytes=64)
        w1_late = {}

        def w1_codes(c):
            if c < PACK:
                return w1_w[:, c * P : (c + 1) * P].bitcast(FP8X4)
            return w1_late[c - c % 2][:, c % 2 * P : (c % 2 + 1) * P].bitcast(FP8X4)

        w1_s = keep.tile([P, H], U8, name="w1_s", align_bytes=64)

        def cast_w1(i, t):
            first, count = W1_LOADS[i]
            g, m0 = first // PASS, first % PASS // PACK
            staged, slot = w1_bf[g * PACK + t]
            nc.scalar.activation(
                staged[:, slot, m0 : m0 + count // PACK, :].rearrange("p (u e) j -> p u j e", e=RUN),
                w1_raw[i][:].rearrange("p j (u t e) -> p t u j e", t=PACK, e=RUN)[:, t],
                COPY,
                scale=-1.0 if g * PACK + t in NEGATED else 1.0,
            )

        def planes(i, t):
            return w1_raw[i][:].rearrange("p j (u t e) -> p t u j e", t=PACK, e=RUN)[:, t]

        def by_pairs(staged):
            return staged.rearrange("p (u e) j -> p u j e", e=RUN)

        def quantize(codes, scales, src, first, count):
            nc.vector.quantize_mx(
                out=codes[:, first : first + count].bitcast(FP8X4),
                scales=scales[:, first : first + count],
                in_=src,
            )

        def quantize_w1(i):
            c0, c1 = W1_CALLS[i]
            src = w1_bf[c0][0][:].rearrange("p t m j -> p (t m j)")
            if c0 in CODES_AT:
                w1_late[c0] = laid.tile([P, 2 * P], U32, name="w1_late%d" % c0, offset=CODES_AT[c0], align_bytes=64)
                nc.vector.quantize_mx(out=w1_late[c0][:].bitcast(FP8X4), scales=w1_s[:, c0 * P : c1 * P], in_=src)
            else:
                quantize(w1_w, w1_s, src, c0 * P, (c1 - c0) * P)

        w2_w = []
        w2_s = {}

        def interleave(copy, dst, src):
            copy(
                dst.rearrange("p (c i) t -> p c t i", i=4),
                src.rearrange("p t (c i) -> p c t i", i=4),
            )

        w2_bf = {}

        def w2_source(i):
            first, count = W2_PIECES[i]
            return w2_raw[first // N][:, :, first % N : first % N + count]

        def round_w2_beside(c):
            i = c
            shape = [P, W2_PIECES[i][1], PACK]
            w2_bf[i] = laid.tile(shape, BF16, name="w2_bf%d" % i, offset=W2_AT[c], align_bytes=64)
            nc.gpsimd.tensor_copy(w2_bf[i][:], w2_source(i).rearrange("p t n -> p n t"))

        def round_w2_late():
            w2_bf[4] = laid.tile([P, W2_PIECES[4][1], PACK], BF16, name="w2_rest", offset=W2_REST_AT, align_bytes=64)
            interleave(nc.scalar.copy, w2_bf[4][:], w2_source(4))

        def quantize_w2(i):
            first, count = W2_PIECES[i]
            if i in W2_SCALES_AT:
                scales = laid.tile([P, count], U8, name="w2_s%d" % i, offset=W2_SCALES_AT[i], align_bytes=64)
            else:
                scales = keep.tile([P, count], U8, name="w2_s%d" % i, align_bytes=64)
            for at in range(0, count, P):
                w2_s[first + at] = scales[:, at : at + P]
            nc.vector.quantize_mx(
                out=w2_w[0][:, first : first + count].bitcast(FP8X4),
                scales=scales[:],
                in_=w2_bf[i][:].rearrange("p n j -> p (n j)"),
            )

        def maxed(c, half):
            return BANK // 2 if (c, half) == NARROW else BANK

        h = {
            c: keep.tile([P, S + (BANK + maxed(c + 2, 0) if c in PAIRED else 0)], F32, name="h%d" % c, align_bytes=64)
            for c in range(1, TILES)
        }

        b_apart = {
            unit: keep.tile([P, BANK], F32, name="b_apart", tag="b_apart%d" % unit[0], align_bytes=64)
            for unit in [(1, 1), (2, 0)]
        }

        def b_staged(c, half):
            if c == 0:
                return h[0][:, S + (half + 1) * BANK : S + (half + 2) * BANK]
            if (c, half) == (1, 0):
                return h[0][:, S : S + BANK]
            if (c, half) in b_apart:
                return b_apart[(c, half)][:]
            first = S + (1 - half) * BANK
            return h[c - 2 + half][:, first : first + maxed(c, half)]

        def multiply_w4(c, half, acc_b, width, skip=0):
            cols = slice(half * BANK + skip, half * BANK + skip + width)
            nc.tensor.matmul_mx(
                out=acc_b,
                lhsT=w4_codes(c),
                lhsT_scale=w4_s[:].bitcast(U8)[:, c * P : (c + 1) * P],
                rhs=v_w[half][:, skip : skip + width].bitcast(FP8X4),
                rhs_scale=v_s[:, cols],
                start=True,
                stop=True,
            )
            return acc_b

        def project_w4(c, half, acc_b=None):
            if acc_b is None:
                acc_b = multiply_w4(c, half, bank(b_bank[(c, half)], [maxed(c, half)])[:], maxed(c, half))
            nc.scalar.copy(b_staged(c, half), acc_b)

        def multiply_w1(c, half, acc_a, width, skip=0):
            cols = slice(half * BANK + skip, half * BANK + skip + width)
            nc.tensor.matmul_mx(
                out=acc_a,
                lhsT=w1_codes(c),
                lhsT_scale=w1_s[:, c * P : (c + 1) * P],
                rhs=v_w[half][:, skip : skip + width].bitcast(FP8X4),
                rhs_scale=v_s[:, cols],
                start=True,
                stop=True,
            )
            return acc_a

        def encode(c, half):
            width = maxed(c, half)
            acc_a = multiply_w1(c, half, bank(a_bank[(c, half)], [width])[:], width)
            nc.vector.tensor_tensor(h[c][:, half * BANK : half * BANK + width], acc_a, b_staged(c, half), MAX)

        turned_parts = {}
        dealt = []

        def next_bank():
            dealt.append(TURNED_BANKS[len(dealt) % len(TURNED_BANKS)])
            return dealt[-1]

        def turn(acc, src, start, stop):
            nc.tensor.matmul(acc, src, ident[:], start=start, stop=stop, is_transpose=True)

        def project_short(c, half):
            accs = bank(5, [2, P])
            multiply_w1(c, half, accs[:, 0, :], P)
            multiply_w4(c, half, accs[:, 1, :], P)
            short = keep.tile([P, 2, P], F32, name="short", align_bytes=64)
            nc.scalar.copy(short[:], accs[:])
            return short

        def project_turned(c, half, short=None):
            skip = 0 if short is None else 1
            minus_a = bank(next_bank(), [PACK, P])
            b_less_a = bank(next_bank(), [PACK, P])
            w1_scales = w1_s[:, c * P : (c + 1) * P]
            w4_scale = w4_s[:].bitcast(U8)[:, c * P : (c + 1) * P]

            def turned(acc, j, codes, scales, start, stop):
                nc.tensor.matmul_mx(
                    out=acc[:, j, :],
                    lhsT=v_w[half][:, j * P : (j + 1) * P].bitcast(FP8X4),
                    lhsT_scale=v_s[:, half * BANK + j * P : half * BANK + (j + 1) * P],
                    rhs=codes,
                    rhs_scale=scales,
                    start=start,
                    stop=stop,
                )

            for j in range(skip, PACK):
                turned(minus_a, j, w1_codes(c), w1_scales, True, True)
            if skip:
                turn(minus_a[:, 0, :], short[:, 0, :], True, True)
                turn(b_less_a[:, 0, :], short[:, 0, :], True, False)
                turn(b_less_a[:, 0, :], short[:, 1, :], False, True)
            for j in range(skip, PACK):
                turned(b_less_a, j, w1_codes(c), w1_scales, True, False)
                turned(b_less_a, j, w4_codes(c), w4_scale, False, True)
            split_turned(c, half, minus_a, b_less_a, "parts%d" % ADDED.index((c, half)))

        def split_turned(c, half, minus_a, b_less_a, tag):
            if tag is None:
                parts = laid.tile([P, 2, PACK, P], F32, name="last_terms", offset=LAST_TERMS_AT, align_bytes=64)
            else:
                parts = keep.tile([P, 2, PACK, P], F32, name="parts", tag=tag, align_bytes=64)
            a_t, r_t = parts[:, 0], parts[:, 1]
            nc.scalar.activation(a_t, minus_a[:], COPY, scale=-1.0)
            nc.scalar.activation(r_t, b_less_a[:], RELU)
            turned_parts[(c, half)] = (a_t, r_t)

        def project_both(c, half):
            both = keep.tile([P, 2, PACK, P], F32, name="both", align_bytes=64)
            acc_a = multiply_w1(c, half, bank(next_bank(), [BANK])[:], BANK)
            acc_b = multiply_w4(c, half, bank(next_bank(), [BANK])[:], BANK)
            nc.scalar.activation(both[:, 0].rearrange("p j s -> p (j s)"), acc_a, COPY, scale=-1.0)
            nc.scalar.copy(both[:, 1].rearrange("p j s -> p (j s)"), acc_b)
            return both

        def turn_both(c, half, both):
            minus_a = bank(next_bank(), [PACK, P])
            b_less_a = bank(next_bank(), [PACK, P])
            for j in range(PACK):
                turn(minus_a[:, j, :], both[:, 0, j, :], True, True)
            for j in range(PACK):
                turn(b_less_a[:, j, :], both[:, 0, j, :], True, False)
                turn(b_less_a[:, j, :], both[:, 1, j, :], False, True)
            split_turned(c, half, minus_a, b_less_a, None)

        def project_narrow(c, half):
            width = BANK - maxed(c, half)
            accs = bank(5, [2, width])
            multiply_w1(c, half, accs[:, 0, :], width, BANK - width)
            multiply_w4(c, half, accs[:, 1, :], width, BANK - width)
            pair = keep.tile([P, 2, width], F32, name="pair", align_bytes=64)
            nc.scalar.activation(pair[:, 0, :], accs[:, 0, :], COPY, scale=-1.0)
            nc.scalar.copy(pair[:, 1, :], accs[:, 1, :])
            return pair

        def turn_narrow(pair):
            accs = bank(5, [2, 2, P])
            for j in range(2):
                turn(accs[:, 0, j, :], pair[:, 0, j * P : (j + 1) * P], True, True)
            for j in range(2):
                turn(accs[:, 1, j, :], pair[:, 0, j * P : (j + 1) * P], True, False)
                turn(accs[:, 1, j, :], pair[:, 1, j * P : (j + 1) * P], False, True)
            terms = keep.tile([P, 2, 2, P], F32, name="terms", align_bytes=64)
            nc.scalar.activation(terms[:, 0], accs[:, 0], COPY, scale=-1.0)
            nc.scalar.activation(terms[:, 1], accs[:, 1], RELU)
            return terms

        def add_narrow(c, half, terms):
            total = bank(2, [2, P])
            for j in range(2):
                turn(total[:, j, :], terms[:, 0, j, :], True, False)
                turn(total[:, j, :], terms[:, 1, j, :], False, True)
            first = half * BANK + maxed(c, half)
            nc.scalar.copy(h[c][:, first : (half + 1) * BANK], total[:].rearrange("p j s -> p (j s)"))

        def add_turned(c, half):
            a_t, r_t = turned_parts[(c, half)]
            total = bank(SUM_BANK[(c, half)], [PACK, P])
            for j in range(PACK):
                turn(total[:, j, :], a_t[:, j, :], True, False)
                turn(total[:, j, :], r_t[:, j, :], False, True)
            nc.scalar.copy(h[c][:, half * BANK : (half + 1) * BANK], total[:].rearrange("p j s -> p (j s)"))

        z_f = {}
        z_f[(1, 0)] = keep.tile([P, PACK, CHUNKS[0][1]], F32, name="z_f1", tag="z_f1", align_bytes=64)
        z_bf = {}
        z_w = [keep.tile([P, PAIRS], U32, name="z_w%d" % g, align_bytes=64) for g in range(GROUPS)]
        z_s = [keep.tile([P, PAIRS], U8, name="z_s%d" % g, align_bytes=64) for g in range(GROUPS)]
        gain = {}
        query = {}

        def spread_gain(c, count):
            g, t = divmod(c, PACK)
            if c in GAIN_AT:
                gain[c] = laid.tile([P, PAIRS], F32, name="gain%d" % c, offset=GAIN_AT[c], align_bytes=64)
            else:
                gain[c] = keep.tile([P, PAIRS], F32, name="gain", tag="gain%d" % c, align_bytes=64)
            copy = nc.scalar.copy if c < SCALAR_GAINS else nc.vector.tensor_copy
            copy(gain[c][:], gz_sb[:, g, RUN * t : RUN * t + 1].to_broadcast([P, count]))

        def pick_query(c, first, count):
            if c in PICKED_AT:
                picked = laid.tile([P, count], F32, name="picked%d" % c, offset=PICKED_AT[c], align_bytes=64)[:]
            elif c in (4, 6):
                if c == 4:
                    query["pair"] = keep.tile([P, 2, count], F32, name="picked_pair", tag="parts2", align_bytes=64)
                picked = query["pair"][:, (c - 4) // 2, :]
            elif c == 7:
                picked = laid.tile([P, count], F32, name="picked7", offset=PICKED_LAST_AT, align_bytes=64)[:]
            else:
                picked = picks.tile([P, count], F32, name="picked", align_bytes=64)[:]
            lst = pos1_sb[:, first // 16 : (first + count) // 16]
            nc.vector.tensor_tensor(picked, h[c][:].indirect(lst), gain[c][:], MULT)
            for at in range(0, count, P):
                query[(c, first + at)] = (picked, at)

        def pick_candidate(c, first, count):
            g, t = divmod(c, PACK)
            lst = pos2_sb[:, first // 16 : (first + count) // 16]
            picked, at = query[(c, first)]
            nc.vector.tensor_tensor(z_f[(g, first)][:, t, :], h[c][:].indirect(lst), picked[:, at : at + count], MULT)

        def stage_z(g, first, count, tag):
            z_bf[(g, first)] = keep.tile([P, count, PACK], BF16, name="z_bf", tag=tag, align_bytes=64)

        def round_z(g, first, count, products, staged):
            src = z_f[(g, products)][:, :, first - products : first - products + count]
            interleave(nc.scalar.copy, z_bf[(g, staged)][:, first - staged : first - staged + count, :], src)

        def quantize_z(g, first, count):
            src = z_bf[(g, first)][:].rearrange("p n j -> p (n j)")
            quantize(z_w[g], z_s[g], src, first, count)

        out_rows = out.rearrange("(c p) j -> p c j", p=P)

        def score_pass(g, n, first, count, acc):
            cols = slice(first, first + count)
            w_cols = slice(g * N + n * P, g * N + (n + 1) * P)
            nc.tensor.matmul_mx(
                out=acc,
                lhsT=w2_w[0][:, w_cols].bitcast(FP8X4),
                lhsT_scale=w2_s[w_cols.start],
                rhs=z_w[g][:, cols].bitcast(FP8X4),
                rhs_scale=z_s[g][:, cols],
                start=(g == 0),
                stop=(g == GROUPS - 1),
            )

        def score(first, count, accs, unopened):
            cols = slice(first, first + count)
            result = ring.tile([P, N_TILES, count], F32, name="result", align_bytes=64)
            order = [1, 0, 2]
            for n in order:
                if n in unopened:
                    score_pass(0, n, first, count, accs[n])
                score_pass(1, n, first, count, accs[n])
            for n in order:
                nc.scalar.activation(result[:, n, :], accs[n], TANH, bias=b2_sb[:, n : n + 1])
                queue = nc.scalar if first == CHUNKS[-1][0] and n == order[-1] else nc.sync
                queue.dma_start(out_rows[:, n, cols], result[:, n, :])

        for c in range(TILES):
            spread_gain(c, PAIRS)
        gather_scales()
        gather_words(0, "v_w0")
        gather_words(1, "v_w1")
        permute_w4_words(nc.scalar.copy, 0, "w4_w0")
        permute_w4_scales(nc.scalar.copy, 0)
        permute_w4_scales(nc.vector.tensor_copy, 1)
        for i in range(2):
            for t in range(2):
                cast_w1(i, t)

        def round_halves(i, tag):
            staged = keep.tile([P, 2, P // 2, PACK], BF16, name="halves", tag=tag, align_bytes=64)
            for t in (2, 3):
                nc.vector.tensor_copy(by_pairs(staged[:, t - 2]), planes(i, t))
            for t in (2, 3):
                src = staged[:, t - 2].rearrange("p m j -> p (m j)")
                quantize(w1_w, w1_s, src, t * P + i * P // 2, P // 2)

        round_halves(0, "w1_front")
        quantize_w1(0)
        quantize_w1(1)
        round_halves(1, "w1_bf1")
        h[0] = keep.tile([P, 2 * S + BANK], F32, name="h0", tag="w1_bf0", align_bytes=64)
        early = {unit: multiply_w4(*unit, bank(b_bank[unit], [BANK])[:], BANK) for unit in [(0, 0), (1, 0), (0, 1)]}
        for c, half in [(0, 0), (0, 1), (1, 0)]:
            project_w4(c, half, early[(c, half)])
            encode(c, half)
        first_c, second_c, third_c = CHUNKS
        staged, slot = w1_bf[5]
        nc.gpsimd.tensor_copy(
            staged[:, slot].rearrange("p (u e) j -> p u e j", e=RUN),
            w1_raw[2][:].rearrange("p j (u t e) -> p t u e j", t=PACK, e=RUN)[:, 1],
        )
        project_w4(1, 1)
        project_w4(2, 0)
        pick_query(0, 0, PAIRS)
        round_w2_beside(0)
        encode(2, 0)
        encode(1, 1)
        project_w4(2, 1)
        cast_w1(2, 2)
        cast_w1(2, 3)
        quantize_w1(4)
        cast_w1(2, 0)
        z_f[(0, 0)] = keep.tile([P, PACK, PAIRS], F32, name="z_f0", tag="b_apart2", align_bytes=64)
        pick_candidate(0, 0, PAIRS)
        short = None
        for c in PAIRED:
            project_w4(c + 2, 0)
            pick_query(c, 0, PAIRS)
            round_w2_beside(c)
            encode(c + 2, 0)
            encode(c + 1, 1)
            if c == 1:
                permute_w4_words(nc.scalar.copy, 1, "w4_w1")
                project_w4(3, 1)
                quantize_w1(3)
            pick_candidate(c, 0, PAIRS)
            if c > 1:
                add_turned(*ADDED[c - 2])
            if c == 3:
                pair = project_narrow(*NARROW)
            if c == 1:
                short = project_short(*SHORT)
                project_w4(4, 1)
            project_turned(*ADDED[c - 1], short if ADDED[c - 1] == SHORT else None)
        terms = turn_narrow(pair)
        both = project_both(*TWICE)
        add_turned(*ADDED[2])
        pick_query(4, 0, PAIRS)
        pick_query(6, 0, PAIRS)
        pick_candidate(4, *first_c)
        pick_candidate(6, *first_c)
        w2_w.append(keep.tile([P, GROUPS * N], U32, name="w2_w", tag="gain4", align_bytes=64))
        for i in range(2):
            quantize_w2(i)
        project_turned(*ADDED[3])
        add_narrow(*NARROW, terms)
        turn_both(*TWICE, both)
        add_turned(*ADDED[3])
        add_turned(*TWICE)
        pick_query(7, 0, PAIRS)
        for i in W2_SCALES_AT:
            quantize_w2(i)
        pick_query(5, 0, PAIRS)
        pick_candidate(7, *first_c)
        pick_candidate(5, *first_c)
        round_w2_late()
        quantize_w2(4)
        z_bf[(0, 0)] = laid.tile([P, third_c[0], PACK], BF16, name="z_bf0", offset=Z_FIRST_AT, align_bytes=64)
        round_z(0, 0, third_c[0], 0, 0)
        quantize_z(0, 0, third_c[0])
        z_f[(1, second_c[0])] = z_f[(0, 0)][:, :, 0 : second_c[1]]
        for c in LATE_ORDER:
            pick_candidate(c, *second_c)
        stage_z(1, *first_c, "z_first")
        round_z(1, *first_c, first_c[0], first_c[0])
        quantize_z(1, *first_c)
        stage_z(0, *third_c, "gain5")
        round_z(0, *third_c, 0, third_c[0])
        y_pair = bank(5, [2, first_c[1]])
        y_lone = bank(6, [first_c[1]])
        y_first = [y_pair[:, 0, :], y_lone[:], y_pair[:, 1, :]]
        y_rest = [bank(number, [P]) for number in (2, 0, 1, 7, 4, 3)]
        y_second = [acc[:] for acc in y_rest[:N_TILES]]
        y_third = [acc[:] for acc in y_rest[N_TILES:]]
        for n in range(2):
            score_pass(0, n, *first_c, y_first[n])
        score(*first_c, y_first, [2])
        for n in range(N_TILES):
            score_pass(0, n, *second_c, y_second[n])
        stage_z(1, *second_c, "z_rest")
        round_z(1, *second_c, second_c[0], second_c[0])
        z_f[(1, third_c[0])] = keep.tile([P, PACK, third_c[1]], F32, name="z_f1_last", tag="z_f1", align_bytes=64)
        for c in LATE_ORDER:
            pick_candidate(c, *third_c)
        quantize_z(1, *second_c)
        quantize_z(0, *third_c)
        score(*second_c, y_second, [])
        for n in range(N_TILES):
            score_pass(0, n, *third_c, y_third[n])
        z_last = keep.tile([P, third_c[1], PACK], BF16, name="z_last", tag="b_apart2", align_bytes=64)
        halves = [slice(0, third_c[1] // 2), slice(third_c[1] // 2, third_c[1])]
        for part in halves:
            interleave(nc.vector.tensor_copy, z_last[:, part, :], z_f[(1, third_c[0])][:, :, part])
        for part in halves:
            src = z_last[:, part, :].rearrange("p n j -> p (n j)")
            quantize(z_w[1], z_s[1], src, third_c[0] + part.start, part.stop - part.start)
        score(*third_c, y_third, [])
